import numpy as np, ml_dtypes
CORES = [48,51,52,55]
N = 4
BF = ml_dtypes.bfloat16
V, HP, Y, L, A, R, LM, C, RO, H = 4096, 16384, 1024, 32, 4, 4, 24, 1536, 3, 9
Q, TOP = L * A * R, 2 ** 20
def chain(rng, brk, gone, uneven):
    s = (N, 8, 16, V); i = np.arange(V)
    last = np.maximum.accumulate(np.where(rng.random(s) < brk, i, 0), axis=-1)
    off = np.exp2(19.8 * rng.random(s)).astype(np.int64) if uneven else rng.integers(1, TOP - V, s)
    away = rng.random(s) < gone
    p = np.where(away, 0, np.take_along_axis(off, last, -1) + i)
    one = rng.random(s) < 0.3; one[..., 0] = False; one[..., 1:] &= away[..., :-1] & ~away[..., 1:]
    return np.where(one, 1, p)
def place(p, order):
    inv = np.argsort(order, axis=-1)
    return np.stack([p[:, g][:, :, inv[g]] for g in range(8)], axis=1)
def names_of(rng, order, jump, power):
    i = np.arange(HP); last = np.maximum.accumulate(np.where(rng.random((N, 8, HP)) < jump, i, 0), axis=-1)
    first = (V * rng.random((N, 8, HP)) ** power).astype(np.int64)
    c = (np.take_along_axis(first, last, -1) + i - last) % V
    return np.take_along_axis(np.broadcast_to(order, (N, 8, V)), c, -1)
def parts(rng, uneven=False):
    order = np.argsort(rng.random((8, V)), axis=-1)
    brk = rng.choice(np.array([0.02, 0.1, 0.3]), (N, 8, 16, 1)); gone = rng.choice(np.array([0.05, 0.2, 0.35]), (N, 8, 16, 1))
    top = rng.integers(LM // 2, LM + 1, (N, 8, 1)); top[0] = LM
    d = {"wpos": place(chain(rng, brk, gone, uneven), order), "heap": names_of(rng, order, 0.25, 3 if uneven else 1),
         "gst": rng.integers(0, HP - LM + 1, (N, 8, Y)), "gln": ((top + 1) * rng.random((N, 8, Y))).astype(np.int64),
         "sens": rng.integers(0, Y, (N, 8, A * Y)), "rel": rng.integers(0, N * Y, (N, 8, R * Y)), "nxt": rng.integers(0, Y, (N, 8, Y)), "cur": rng.integers(0, Y, (N, 8, L))}
    return d, order
def pack(d):
    r = {"wpos": np.ascontiguousarray(d["wpos"].reshape(N, 128, V)).astype(np.int32)}
    for k in ("heap", "gst", "gln", "sens", "rel", "nxt", "cur"): r[k] = np.ascontiguousarray(d[k]).astype(np.int32)
    return r
def some(rng, ln, n, k):
    return rng.choice(np.flatnonzero(ln == n), k)
def plant(rng, d, g, w):
    m, n = w.shape
    p = rng.integers(1, TOP - n + 1, (N, 16, m, 1)) + np.arange(n)
    d["wpos"][:, g][:, :, w.reshape(-1)] = p.reshape(N, 16, m * n)
    s = rng.integers(0, HP - LM - m * n + 1, (N, 1)) + n * np.arange(m)
    d["heap"][np.arange(N)[:, None], g, s[:, :1] + np.arange(m * n)] = w.reshape(-1)
    return s
def ask_few(rng, d, g, w, heads):
    m, n = len(w), len(heads); s = plant(rng, d, g, w)
    t = rng.permutation(Y)[:2 * m + 1]; u = rng.permutation(Y)[:n + 1]
    for k, ln in ((t[:m], 3), (t[m:2 * m], 2)):
        d["gst"][:, g][:, k] = s; d["gln"][:, g][:, k] = ln
    d["gln"][:, g, t[2 * m]] = 0
    for a in range(N):
        o = ((a + 1) % N) * Y; se = d["sens"][a, g].reshape(Y, A); re_ = d["rel"][a, g].reshape(Y, R)
        se[heads] = u[n]; se[heads, rng.integers(0, A, n)] = u[:n]; re_[u[n]] = o + t[2 * m]
        for i in range(n): re_[u[i]] = o + t[(np.arange(R) + i) % m + m * (a & 1)]
        d["nxt"][a, g, u[:n]] = np.roll(heads, -1); d["cur"][a, g] = heads[(np.arange(L) + a) % n]
    return u[:n], t
def setup_inputs(rng):
    return pack(parts(rng)[0])
def setup_inputs_spread(rng):
    d, order = parts(rng, True)
    e = rng.choice(np.array([0.3, 1.0, 4.0]), (N, 8, 1))
    d["gln"] = ((LM + 1) * rng.random((N, 8, Y)) ** e).astype(np.int64)
    d["gst"] = ((HP - LM + 1) * rng.random((N, 8, Y)) ** 2).astype(np.int64)
    q = ((N * rng.random((N, 8, R * Y)) ** 2).astype(np.int64) + np.arange(N)[:, None, None]) % N
    d["rel"] = q * Y + (Y * rng.random((N, 8, R * Y)) ** 1.5).astype(np.int64)
    d["sens"] = (Y * rng.random((N, 8, A * Y)) ** 2).astype(np.int64); d["cur"] = (Y * rng.random((N, 8, L)) ** 2).astype(np.int64)
    d["nxt"] = (Y * rng.random((N, 8, Y)) ** 0.5).astype(np.int64)
    for k in ("sens", "cur", "nxt"): d[k] = np.minimum(d[k], Y - 1)
    d["gln"] = np.minimum(d["gln"], LM); d["gst"] = np.minimum(d["gst"], HP - LM)
    return pack(d)
def setup_inputs_ends(rng):
    d, order = parts(rng)
    for k, hi in (("heap", V - 1), ("gst", HP - LM), ("sens", Y - 1), ("rel", N * Y - 1), ("nxt", Y - 1), ("cur", Y - 1), ("wpos", TOP - 1)):
        m = rng.random(d[k].shape); d[k] = np.where(m < 0.38, 0, np.where(m < 0.76, hi, d[k]))
    d["gln"] = LM * rng.integers(0, 2, (N, 8, Y))
    for g in range(8):
        o = rng.permutation(np.arange(1, V - 1)); c0 = np.concatenate([np.array([0]), o[:LM - 1]]); c1 = np.concatenate([o[LM:2 * LM - 1], np.array([V - 1])])
        if g == 3: c0 = np.roll(c0, -1)
        d["heap"][:, g, :LM] = c0; d["heap"][:, g, HP - LM:] = c1
        w = d["wpos"][:, g]; w[:, :, c0] = 1 + np.arange(LM); w[:, :, c1] = TOP - LM + np.arange(LM)
        if g < 3: w[:, g::3, c1[LM // 2]] = 0
        if g == 4 or g == 5:
            n = H if g == 4 else H - 1
            w[:, n:, c0] = TOP - 1; w[:, n:, c1] = TOP - 1
        if g == 6: w[:, 3, 0] = 0
    d["gst"][:, :, 0] = 0; d["gst"][:, :, Y - 1] = HP - LM; d["gln"][:, :, Y - 1] = LM; d["gln"][:, ::2, 0] = LM; d["gln"][:, 1::2, 0] = 0
    n = C // (A * R * LM)
    d["cur"][:, 7] = 0; d["cur"][:, 7, L - n:] = Y - 1; d["sens"][:, 7, :A] = 0; d["sens"][:, 7, (Y - 1) * A:] = Y - 1
    d["rel"][:, 7, :R] = 0; d["rel"][:, 7, (Y - 1) * R:] = N * Y - 1; d["nxt"][:, 7, 0] = Y - 1; d["nxt"][:, 7, Y - 1] = rng.choice(np.array([0, Y - 1]), N)
    d["cur"][:, 6, 0] = Y - 1; d["sens"][:, 6, (Y - 1) * A:] = Y - 1; d["sens"][:, 6, (Y - 1) * A] = Y - 2
    d["rel"][:, 6, (Y - 2) * R:] = N * Y - 1; d["rel"][:, 6, (Y - 2) * R] = 0; d["nxt"][:, 6, Y - 1] = 0; d["nxt"][:, 6, Y - 2] = Y - 1
    return pack(d)
def setup_inputs_corners(rng):
    d, order = parts(rng)
    d["gln"] = np.array([0, 1, LM - 1, LM, LM, LM, LM, 2])[np.argsort(rng.random((N, 8, Y)), axis=-1) & 7]
    d["gst"][:, 3] = rng.choice(np.array([0, 1, HP - LM - 1, HP - LM]), (N, Y))
    m = C // LM
    for a in range(N):
        for g in range(8):
            got = []
            for o in range(N):
                ln = d["gln"][o, g]; case = (o + 3 * a + g) % 6
                want = ([(LM, m)], [(LM, m - 1), (LM - 1, 1)], [(LM, m), (1, 1)], [(LM, m + m // 2)], [(0, 2)], [(1, m)])[case]
                for n, k in want: got.append(o * Y + some(rng, ln, n, k))
            have = np.concatenate(got)[:Q]
            have = rng.permutation(np.concatenate([have, a * Y + some(rng, d["gln"][a, g], 0, Q - len(have))]))
            w = rng.permutation(Y)[:L]; s = rng.permutation(Y)[:L * A]
            d["cur"][a, g] = w; d["sens"][a, g].reshape(Y, A)[w] = s.reshape(L, A); d["rel"][a, g].reshape(Y, R)[s] = have.reshape(L * A, R)
            if g % 4 == 1: d["nxt"][a, g, s] = np.repeat(w, A)
            if g % 4 == 2: d["nxt"][a, g] = rng.choice(np.array([0, Y - 1]), Y)
    return pack(d)
def setup_inputs_crowd(rng):
    d, order = parts(rng)
    n = np.array([16, 15, H, H - 1, 16, H + 1, H, H - 1])[(np.arange(8)[None, :] + np.arange(N)[:, None]) & 7]
    turn = (np.arange(16)[None, None, :] + rng.integers(0, 16, (N, 8, 1))) & 15
    off = rng.integers(1, TOP - V, (N, 8, 16, 1)); i = np.arange(V)
    d["wpos"] = place(np.where((turn < n[:, :, None])[..., None], off + i, (off + 257 * i) & (TOP - 1)), order)
    d["cur"][:, ::2] = rng.integers(0, Y, (N, 4, 1)); d["cur"][:, 1::4, :L - 1] = rng.integers(0, Y, (N, 2, 1))
    few = rng.integers(0, Y, (N, 2, 3)); d["cur"][:, 3::4] = np.take_along_axis(few, rng.integers(0, 3, (N, 2, L)), -1)
    d["gln"][:, 4:] = np.minimum(d["gln"][:, 4:], 4)
    d["rel"][:, 2] = np.arange(N)[:, None] * Y + rng.integers(0, Y, (N, R * Y)); d["rel"][:, 6] = (N - 1) * Y + rng.integers(0, Y, (N, R * Y))
    return pack(d)
def setup_inputs_calm(rng):
    d, order = parts(rng); gs = [int(x) for x in rng.permutation(8)[:4]]; c = rng.permutation(np.arange(4, V - 4))
    g = gs[0]; h = rng.permutation(Y)[:2]
    u, t = ask_few(rng, d, g, c[None, :3], h)
    d["nxt"][:, g][:, u] = h; d["rel"][:, g, u[1] * R + R - 1] = ((np.arange(N) + 1) % N) * Y + t[2]
    d["cur"][:, g] = h[0]; d["cur"][1::2, g, L - 1] = h[1]
    ask_few(rng, d, gs[1], np.stack([c[3:7], np.arange(4), c[7:11]], axis=1), rng.permutation(4))
    ask_few(rng, d, gs[2], np.stack([c[11:15], V - 1 - np.arange(4), c[15:19]], axis=1), Y - 1 - rng.permutation(4))
    g = gs[3]; m = L * R; t = rng.permutation(Y)
    s = plant(rng, d, g, rng.permutation(V)[:2 * m].reshape(m, 2))
    d["gst"][:, g][:, t[:m]] = s; d["gln"][:, g] = 1; d["gln"][:, g][:, t[:m]] = 2
    for a in range(N):
        o = ((a + N - 1) % N) * Y; w = rng.permutation(Y)[:L]; u = rng.permutation(Y)[:L * A].reshape(L, A); v = rng.integers(0, A, L); v[L - 1] = A - 1
        d["sens"][a, g].reshape(Y, A)[w] = u; d["cur"][a, g] = w; d["nxt"][a, g, u] = w[:, None]
        rows = d["rel"][a, g].reshape(Y, R); rows[u] = o + t[rng.integers(m, Y, (L, A, R))]
        rows[u[np.arange(L), v]] = o + rng.permutation(t[:m]).reshape(L, R)
    return pack(d)
def check_inputs(d):
    bad = []
    for k, hi in (("wpos", 2 ** 20 - 1), ("heap", V - 1), ("gst", HP - LM), ("gln", LM), ("sens", Y - 1), ("rel", N * Y - 1), ("nxt", Y - 1), ("cur", Y - 1)):
        if np.min(d[k]) < 0 or np.max(d[k]) > hi: bad.append("range of " + k)
    return bad
def reference(wpos, heap, gst, gln, sens, rel, nxt, cur):
    P = np.array(wpos, dtype=np.int32).reshape(N, 8, 16, V); w = cur.astype(np.int64)
    yt = np.zeros((N, 8, RO, L, A), np.int64); yb = np.zeros((N, 8, RO, L, R), np.int64); yw = np.zeros((N, 8, RO, L), np.int64)
    gi = np.arange(8)[:, None]; e = np.arange(LM)[:, None]
    for rnd in range(RO):
        for a in range(N):
            s = np.take_along_axis(sens[a], (w[a][:, :, None] * A + np.arange(A)).reshape(8, L * A), 1).astype(np.int64)
            rq = np.take_along_axis(rel[a], (s[:, :, None] * R + np.arange(R)).reshape(8, Q), 1).astype(np.int64)
            q = rq // Y; t = rq - q * Y; ln = gln[q, gi, t].astype(np.int64); st = gst[q, gi, t].astype(np.int64)
            kept = np.zeros((8, Q), np.int64)
            for o in range(N):
                m = np.where(q == o, ln, 0); before = np.add.accumulate(m, axis=1) - m
                kept = kept + np.minimum(np.maximum(C - before, 0), m)
            word = heap[q[:, None, :], gi[:, :, None], st[:, None, :] + e]
            x = np.take_along_axis(P[a], word.reshape(8, 1, LM * Q), 2).reshape(8, 16, LM, Q)
            x = np.where((e < kept[:, None, :])[:, None], x, 0)
            more = np.zeros(x.shape, bool); more[:, :, 1:] = (x[:, :, 1:] == x[:, :, :-1] + 1) & (x[:, :, :-1] > 0)
            run = np.zeros((8, 16, Q), np.int64); score = np.zeros((8, 16, Q), np.int64)
            for i in range(LM):
                run = np.where(x[:, :, i] > 0, np.where(more[:, :, i], run, 0) + 1, 0)
                score = score + np.where(run > 0, 2 * run - 1, 0)
            tot = np.add.reduce(np.add.reduce(score, axis=1).reshape(8, L, A, R), axis=3)
            win = np.argmax(tot, axis=2)
            hot = np.add.reduce(more, axis=1, dtype=np.int64) >= H
            at = np.maximum.reduce(np.where(hot, e, -1), axis=1)
            b = np.where(at >= 0, np.take_along_axis(word, np.maximum(at, 0)[:, None, :], 1)[:, 0], -1).reshape(8, L, A, R)
            b = np.take_along_axis(b, win[:, :, None, None], 2)[:, :, 0]
            if rnd < RO - 1:
                for g in range(8):
                    c = b[g].reshape(-1); P[a, g][:, c[c >= 0]] = 0
            sw = np.take_along_axis(s.reshape(8, L, A), win[:, :, None], 2)[:, :, 0]
            w[a] = np.take_along_axis(nxt[a], sw, 1)
            yt[a, :, rnd] = tot; yb[a, :, rnd] = b; yw[a, :, rnd] = w[a]
    return {"yt": yt.reshape(N, 8, RO * L * A).astype(np.float32), "yb": yb.reshape(N, 8, RO * L * R).astype(np.float32), "yw": yw.reshape(N, 8, RO * L).astype(np.float32)}

@@ -1,0 +1,723 @@
+import numpy as np
+from concourse.bass import DstId, RemoteDMATransfer
+from concourse.mybir import AluOpType, AxisListType, ActivationFunctionType
+
+N, RO, C = 4, 3, 1536
+F32, BF, F16, I32, U16 = "float32", "bfloat16", "float16", "int32", "uint16"
+XS, CS, WS = 1544, 1568, 2560
+
+BUFS = {
+    "wraw": (I32, [2, 1024]), "A": (F32, [4240]), "hraw": (I32, [1024]), "HW": (BF, [16384]), "ZB": (BF, [1536]), "T3": (BF, [4096]),
+    "TB": (F32, [1024]), "srn": (I32, [2, 256]), "srd": (F32, [8, 64]), "nxn": (I32, [64]), "nxf": (F32, [2, 64]), "curi": (I32, [32]),
+    "mg": (I32, [64]), "mo": (I32, [64]), "mq": (I32, [2, 64]), "mf": (F32, [3, 64]), "mlf": (F32, [66]), "mlh": (F32, [66]), "msnd": (U16, [88]),
+    "mrcv": (U16, [3, 88]), "mi": (I32, [4, 88]), "ml": (I32, [4, 66]), "mrole": (BF, [3, 4, 64]),
+    "pi": (I32, [8]), "pc": (F32, [96]), "X": (F32, [144]), "Xi": (I32, [128]), "WA": (F16, [4, 144]), "WL": (F16, [144]), "WD": (F16, [144]),
+    "WLb": (BF, [144]), "WH": (BF, [4, 144]), "WZ": (BF, [144]), "W4": (F32, [2, 144]), "Wn": (F32, [144]), "ONE": (F32, [128]),
+    "ON8": (F32, [128]), "WK": (F32, [4, 128]), "WE": (F16, [4, 128]), "ID": (F16, [2, 128]), "slf": (F32, [96]), "slc": (F16, [96]),
+    "r1": (F32, [128]), "Cc": (F32, [128]), "c3": (F32, [128]), "pat4": (F32, [128]), "pat7": (F32, [252]), "pat3": (F32, [72]), "pat5": (F32, [66]),
+    "pat16": (F32, [128]), "sc7": (F32, [288]), "repf": (F32, [288]), "reph": (F16, [288]), "repl": (U16, [18]), "drow": (BF, [768]),
+    "cap": (BF, [512]), "neg8": (F32, [128]), "on1": (F32, [152]), "qrt": (F32, [128]), "i16": (F32, [128]), "tri": (BF, [8, 16]),
+    "M16": (F32, [128]), "Dc": (F32, [8]),
+    "nx": (F32, [32]), "hc": (U16, [8]), "sl": (U16, [32]), "RG": (F32, [512]), "RC": (F32, [3, 128]), "oh": (F32, [128]),
+    "pr": (F32, [3, 128]), "ps": (F32, [3, 128]), "rq": (U16, [32]), "rqi": (I32, [32]), "qi": (I32, [32]), "qh": (F16, [32]),
+    "G3": (BF, [512]), "Gb": (BF, [512]), "G2": (BF, [512]), "F": (F16, [520]), "vv": (F16, [512]), "d0": (BF, [512]), "ff": (BF, [520]),
+    "off": (U16, [32]), "W": (BF, [4 * WS]), "Ds": (F16, [2, C]), "ai": (I32, [4, 96]), "aa": (I32, [384]),
+    "pk": (I32, [288]), "pk2": (I32, [288]), "pk3": (I32, [3, 96]), "asnd": (U16, [3, 3, 88]), "arcv": (U16, [3, 3, 88]),
+    "ui": (I32, [3, 84]), "ua": (I32, [3, 84]), "uh": (BF, [252]), "us": (F32, [252]), "hl": (U16, [4, 96]),
+    "G": (BF, [2 * C]), "rsnd": (U16, [3, 3, 72]), "rrcv": (U16, [3, 3, 72]), "ri": (I32, [72]), "rh": (BF, [72]), "rs": (F32, [72]),
+    "Ww": (I32, [512]), "w2": (I32, [96]), "l1": (U16, [4, 96]), "l2": (U16, [4, 96]),
+    "xs": (F32, [2 * XS]), "ct": (BF, [2 * CS]), "d1": (BF, [C]), "z": (BF, [C]), "Pz": (F32, [136]), "T1": (F32, [2, 128]), "T2": (F32, [2, 128]),
+    "nh": (BF, [152]), "DS": (F32, [1056]), "Es": (F16, [128]), "Et": (F32, [128]), "EB": (F32, [512]), "WDf": (F32, [144]), "n32": (F16, [96]), "ch": (BF, [512]), "lt": (BF, [512]), "eq": (BF, [512]),
+    "bi": (I32, [32]), "bj": (I32, [32]), "bl": (U16, [32]), "S": (F32, [136]), "key": (F32, [128]), "m1": (F32, [64]), "m": (F32, [32]),
+    "s0": (F32, [32]), "s1": (F32, [32]), "s2": (F32, [32]), "s3": (F32, [32]), "s4": (F32, [32]), "Xq": (F32, [32]), "mi3": (I32, [2, 32]),
+    "ohs": (F32, [32]), "Xs": (F32, [32]),
+    "b0": (F32, [128]), "b1": (F32, [128]), "c0": (I32, [4, 8]), "cl": (U16, [2, 8]), "xi": (I32, [4, 128]), "be": (F32, [128]), "bg": (F32, [128]),
+    "va": (F32, [128]), "ys": (I32, [2, 128]), "mv": (F32, [128]), "B1": (F32, [144]), "E8": (BF, [8, 144]), "jk": (BF, [144]), "cn": (F32, [4, 8]),
+    "yto": (F32, [384]), "ybo": (F32, [384]), "ywo": (F32, [96]), "kd": (F32, [128]),
+}
+BANKS = ["pA", "pB", "pR0", "pR1", "pZ", "pC", "pT", "pS"]
+PLACE, SCRATCH = {}, {}
+for _k, (_d, _s) in BUFS.items():
+    if len(_s) == 1 and _s[0] <= 520:
+        _at = SCRATCH.get("pool_" + _d, (0, [128, 0]))[1][1]
+        PLACE[_k] = ("pool_" + _d, _at)
+        SCRATCH["pool_" + _d] = ("sbuf", [128, _at + (_s[0] + 15) // 16 * 16], _d)
+    else:
+        SCRATCH[_k] = ("sbuf", [128] + _s, _d)
+SCRATCH.update({k: ("psum", [128, 512], F32) for k in BANKS})
+SEMAPHORES = (["V", "S", "P", "Q", "sent", "rm", "lm", "ls", "lc", "lh", "tb", "t3a", "hw0", "hw1", "oy0", "oy1", "oy2"]
+              + ["%s%d" % (k, i) for k in ("ra", "wz", "rr0", "rr1", "rr2") for i in range(RO)] + ["lw%d" % i for i in range(4)])
+ALL = slice(None)
+CY, GATHER, SCATTER, PECY, WAKE, DMAT, FART = 1.04, 1.56, 3.8, 0.55, 90.0, 2000.0, 2800.0
+
+
+def rank_program(g, core, T, topo):
+    me = T.rank_of(core)
+    if me is None:
+        return
+    Op, Act = AluOpType, ActivationFunctionType
+    eng = {"V": g.vector, "S": g.scalar, "P": g.tensor, "Q": g, "Y": g.sync}
+    nodes, hist, bysem, up, gate = [], {}, {}, [0.0], []
+
+    def v(name, *idx, p=ALL):
+        if name in PLACE:
+            a, b, st = (idx[0] if idx else ALL).indices(BUFS[name][1][0])
+            name, at = PLACE[name]
+            idx = (slice(at + a, at + b, st) if st > 1 else slice(at + a, at + b),)
+        shape = SCRATCH[name][1]
+        cols = np.arange(int(np.prod(shape[1:]))).reshape(shape[1:])[idx if idx else ALL]
+        lo, hi = int(np.min(cols)), int(np.max(cols)) + 1
+        pm = sum(1 << int(x) for x in np.arange(128)[p])
+        if name in BANKS:
+            lo, hi, pm = 0, 512, (1 << 128) - 1
+        return (T[name][(p,) + (tuple(idx) if idx else (ALL,))], [(name, lo, hi, pm)], [], int(np.size(cols)), SCRATCH[name][2] in (BF, F16, U16), name in BANKS)
+
+    def ind(win, off):
+        return (win[0].indirect(off[0]), win[1], off[1], 16 * off[3], win[4], False)
+
+    def ap(x):
+        return x[0] if isinstance(x, tuple) else x
+
+    def node(q, kind, outs, ins, call, busy, late=0.0, sem=None, n=1, after=()):
+        outs = [x for x in outs if isinstance(x, tuple)]
+        ins = [x for x in ins if isinstance(x, tuple)]
+        rd = [r for x in ins for r in x[1]] + [r for x in outs + ins for r in x[2]]
+        wr = [r for x in outs for r in x[1]] + [r for r in rd if r[0] in BANKS]
+        i = len(nodes)
+        dep = {j: False for j in after}
+        for k, rs in (("w", wr), ("r", rd)):
+            for (nm, lo, hi, pm) in rs:
+                for (l2, h2, p2, k2, j) in hist.get(nm, []):
+                    if l2 < hi and lo < h2 and (pm & p2) and (k == "w" or k2 == "w"):
+                        soft = kind == "c" and nodes[j]["kind"] == "c" and nodes[j]["q"] == q == "P"
+                        dep[j] = dep.get(j, False) or not soft
+        for j in gate:
+            dep.setdefault(j, False)
+        del gate[:]
+        for j in list(dep):
+            if nodes[j]["kind"] == "d" and dep[j]:
+                for j2 in bysem[nodes[j]["sem"]]:
+                    dep[j2] = True
+        for (nm, lo, hi, pm) in wr:
+            hist[nm] = [e for e in hist.get(nm, []) if not (lo <= e[0] and e[1] <= hi and (e[2] & ~pm) == 0)] + [(lo, hi, pm, "w", i)]
+        for (nm, lo, hi, pm) in rd:
+            hist.setdefault(nm, []).append((lo, hi, pm, "r", i))
+        nodes.append({"q": q, "kind": kind, "call": call, "busy": busy, "late": late, "sem": sem, "n": n, "dep": dep, "up": up[0]})
+        if kind == "d":
+            bysem.setdefault(sem, []).append(i)
+        return i
+
+    def run(q, o, ins, call, k=1.0, fast=True, more=()):
+        xs = [x for x in [o] + ins if isinstance(x, tuple) and x[3] > 1] or [o]
+        if o[2]:
+            t = 50 + o[3] * SCATTER * CY
+        elif any(x[2] for x in xs):
+            t = 50 + o[3] * GATHER * CY
+        else:
+            t = max(64, max(x[3] for x in xs) * (0.5 if fast and all(x[4] for x in xs) else k)) * CY
+        node(q, "c", [o] + list(more), ins, call, t)
+
+    def cp(o, i): run("V", o, [i], lambda: g.vector.tensor_copy(ap(o), ap(i)))
+    def ms(o, c): run("V", o, [], lambda: g.vector.memset(ap(o), c))
+    def tt(o, a, b, op): run("V", o, [a, b], lambda: g.vector.tensor_tensor(ap(o), ap(a), ap(b), op), 1.0 if a[5] or b[5] else 2.0, False)
+
+    def ts(o, a, s1, op0, s2=None, op1=None):
+        if op1 is None:
+            run("V", o, [a, s1], lambda: g.vector.tensor_scalar(ap(o), ap(a), ap(s1), None, op0))
+        else:
+            run("V", o, [a, s1, s2], lambda: g.vector.tensor_scalar(ap(o), ap(a), ap(s1), ap(s2), op0, op1))
+
+    def scan(o, a, b, init, op0, op1):
+        run("V", o, [a, b, init], lambda: g.vector.tensor_tensor_scan(ap(o), ap(a), ap(b), ap(init), op0, op1))
+
+    def act(o, i, f, bias=0.0, scale=1.0, acc=None):
+        run("S", o, [i, bias, scale], lambda: g.scalar.activation(ap(o), ap(i), f, bias=ap(bias), scale=ap(scale), accum_out=ap(acc)), 1.0, False, [acc])
+
+    def iota(o, pat, base, cm):
+        node("Q", "c", [o], [], lambda: g.iota(ap(o), pat, base, cm, allow_small_or_imprecise_dtypes=True), 130 + 2 * CY * o[3])
+
+    def mm(items, first=True, last=True):
+        def call():
+            for n, (o, l, r) in enumerate(items):
+                inst = g.tensor.matmul(ap(o), ap(l), ap(r), first and n == 0, last and n == len(items) - 1)
+            return inst
+        node("P", "c", [items[0][0]], [y for x in items for y in x[1:]], call, sum(max(64, x[2][3]) * (1 if x[2][4] else 4) * PECY for x in items))
+
+    def dma(q, sem, o, i, nbytes=0):
+        node(q, "d", [o], [i], lambda: eng[q].dma_start(ap(o), ap(i)), 100.0, DMAT + nbytes / 200.0, sem, 16)
+
+    peer = [T.cores[(me + 1 + s) % N] for s in range(3)]
+    whole = len(topo.engines(core, peer[0]))
+    quarter = whole // 4
+    sends = []
+
+    def send3(sem, srcs, dsts):
+        def call():
+            trs = []
+            for s in range(3):
+                rid, pid, _ = topo.addr(peer[s])
+                es = topo.engines(core, peer[s])[s * quarter:(s + 1) * quarter]
+                trs.append(RemoteDMATransfer(dst_ids=[DstId(rid=rid, pnc=pid)], dma_engine_mask=sum(1 << e for e in es),
+                                             remote_sem=T.sem[sem], src=ap(srcs[s]), dst=ap(dsts[s])))
+            g.remote_dma_fused(trs, local_sem=T.sem["sent"])
+        sends.append(node("Q", "r", [], srcs, call, 300.0 if sends else 2300.0, n=3 * quarter, after=sends[-1:]))
+        return sends[-1]
+
+    def send1(s, sem, src, dst):
+        def call():
+            rid, pid, _ = topo.addr(peer[s])
+            g.remote_dma(ap(dst), ap(src), T.sem[sem], T.sem["sent"], pid, rid, topo.mask(core, peer[s]))
+        sends.append(node("Q", "r", [], [src], call, 300.0, n=whole, after=sends[-1:]))
+        return sends[-1]
+
+    def arrive(sem, n, land, twin):
+        node("A", "a", [land], [], None, 0.0, FART, sem, n, [twin])
+
+    ncol = [0]
+
+    def newcol():
+        ncol[0] += 1
+        return v("pc", slice(ncol[0] - 1, ncol[0]))
+
+    def colts(a, s1, op0, s2=None, op1=None):
+        c = newcol()
+        ts(c, a, s1, op0, s2, op1)
+        return c
+
+    def const(x):
+        c = newcol()
+        ms(c, x)
+        return c
+
+    def wide(name, u, *i): return v(name, *i, slice(15 - u, 143 - u))
+    def wide4(i, b): return v("W4", i, slice(12 - 4 * b, 140 - 4 * b))
+    def rows(r): return slice(r, 128, 16)
+    def sl(a, n, st=1): return slice(a, a + n, st)
+    secs = [(me + 1 + s) % N for s in range(3)] + [me]
+
+    dma("Y", "lm", v("mg"), T.gst[:])
+    dma("S", "lm", v("mo"), T.gln[:])
+    dma("Y", "ls", v("srn", 0), T.sens[:])
+    dma("S", "ls", v("srn", 1), T.rel[:])
+    dma("Y", "ls", v("nxn"), T.nxt[:])
+    ms(v("curi"), 0)
+    dma("S", "lc", v("curi", p=rows(0)), T.cur[:])
+    dma("Y", "lh", v("hraw"), T.heap[:], 1 << 19)
+    ms(v("ZB"), 0.0)
+    P16, P4, PA, G16, PG = [newcol() for _ in range(5)]
+    BM1 = const(-1.0)
+    act(v("TB"), v("ZB", sl(0, 1024)), Act.Copy)
+    for h in range(4):
+        act(v("T3", sl(1024 * h, 1024)), v("ZB", sl(0, 1024)), Act.Identity, bias=BM1)
+    iota(v("pi", sl(0, 1)), [[0, 1]], 0, 1)
+    iota(v("X"), [[1, 144]], 0, 0)
+    iota(v("nxf", 1), [[1, 64]], 0, 64)
+    iota(v("slf"), [[16, 96]], 0, 1)
+    iota(v("r1"), [[4, 128]], -508, 0)
+    iota(v("c3"), [[0, 32], [-1, 4]], 3, 0)
+    iota(v("i16"), [[0, 8], [1, 16]], 0, 0)
+    iota(v("repf"), [[0, 288]], 0, 0)
+    for s in range(3):
+        iota(v("repf", sl(96 * s, 84)), [[1, 12], [0, 7]], 96 * s + 84, 0)
+    iota(v("Xi"), [[1, 128]], 0, 0)
+
+    ms(v("mlf"), 0.0)
+    ms(v("pat5"), 32.0); ms(v("pat5", sl(0, 66, 3)), 0.0)
+    ms(v("msnd", sl(86, 2)), 0)
+    cp(v("mlf", sl(0, 64)), v("mo"))
+    scan(v("mlh"), v("pat5"), v("mlf"), 0.0, Op.mult, Op.add)
+    cp(v("msnd", sl(64, 22)), v("mlh", slice(2, 66, 3)))
+    ts(v("mq", 0), v("mg"), 7, Op.logical_shift_right)
+    ts(v("mf", 0), v("mg"), 257.0, Op.add)
+    ts(v("mf", 1), v("mq", 0), 128.0, Op.mult)
+    ts(v("mf", 2), v("mo"), 65535.0, Op.mult)
+    tt(v("mf", 0), v("mf", 0), v("mf", 1), Op.add)
+    tt(v("mf", 1), v("mf", 0), v("mf", 2), Op.min)
+    cp(v("msnd", sl(0, 64)), v("mf", 1))
+    tw = send3("rm", [v("msnd")] * 3, [v("mrcv", 2 - s) for s in range(3)])
+    arrive("rm", 3 * quarter, v("mrcv"), tw)
+
+    for k, (sh, an) in enumerate(((0, 15), (0, 3), (2, 3), (0, 112), (4, 7))):
+        ts(v("pi", sl(k + 1, 1)), v("pi", sl(0, 1)), sh, Op.logical_shift_right, an, Op.bitwise_and)
+    cp(v("pc", sl(0, 5)), v("pi", sl(1, 5)))
+    G15 = colts(G16, 15.0, Op.add)
+    for t in range(2):
+        for a in range(4):
+            cp(v("srd", 4 * t + a), v("srn", t, slice(a, 256, 4)))
+    cp(v("nxf", 0), v("nxn"))
+    ts(v("nxf", 1), v("nxf", 1), colts(G16, 64.0, Op.mult), Op.subtract)
+    for r in range(10):
+        dma("Y", "tb", v("TB", p=rows(r)), v("srd", r) if r < 8 else v("nxf", r - 8))
+
+    def rowcol(vals, by):
+        c = None
+        for i, x in enumerate(vals):
+            if x:
+                d = colts(by, float(i), Op.is_equal, float(x), Op.mult)
+                c = d if c is None else colts(d, c, Op.add)
+        return c
+
+    def weights(o, at, w): ts(o, v("X"), at, Op.is_equal, w, Op.mult)
+    for i in range(2):
+        weights(v("W4", i), colts(P16, 12.0 - 4 * i, Op.add, G16, Op.add), colts(PA, float(i), Op.is_equal))
+    weights(v("Wn"), G15, colts(P16, 8.0, Op.is_equal))
+    cp(v("nx"), v("curi"))
+    ms(v("oh"), 0.0); ms(v("oh", sl(0, 128, 4)), 1.0)
+    ms(v("pat4"), 1.0); ms(v("pat4", sl(0, 128, 4)), 0.0)
+
+    def chain(more):
+        mm([(v("pB", sl(0, 8)), wide4(0, b), v("nx", slice(b, 32, 4))) for b in range(4)])
+        cp(v("hc"), v("pB", sl(0, 8)))
+        act(v("RC", 2), ind(v("TB"), v("hc")), Act.Copy)
+        if more:
+            mm([(v("pB", sl(0, 32)), wide4(0, b), v("RC", 2, slice(b, 128, 4))) for b in range(4)])
+            cp(v("sl"), v("pB", sl(0, 32)))
+            act(v("RG"), ind(v("TB"), v("sl")), Act.Copy)
+            mm([(v("pB", sl(0, 128)), wide4(1, b), v("RG", slice(b, 512, 4))) for b in range(4)])
+            act(v("RC", 0), v("pB", sl(0, 128)), Act.Copy)
+            mm([(v("pB", sl(128, 128)), wide("Wn", b), v("RG", slice(b, 512, 4))) for b in range(4)])
+            act(v("RC", 1), v("pB", sl(128, 128)), Act.Copy)
+
+    chain(True)
+    wa = rowcol([-128, -1, -1, 49152], P4)
+    ms(v("n32"), -32768.0)
+    for o in range(4):
+        weights(v("WA", o), G15, colts(PA, float(o), Op.is_equal, wa, Op.mult))
+    isl = colts(P4, 2.0, Op.is_equal)
+    weights(v("WL"), G15, isl)
+    ts(v("WLb"), v("WL"), 1.0 / 4096, Op.mult)
+    FF0, KAP, BIA = colts(isl, -1.0, Op.mult), colts(P4, 2.0, Op.is_lt, -1.0, Op.mult), colts(P4, 2.0, Op.is_ge)
+    BG4, BXS, BSG, BR2, B160, BNH = const(4096.0), const(1.0), const(-1250.0), const(160.0 - 7.5 / 16), const(-160.0), const(8500.0)
+    cp(v("ff", sl(0, 1)), FF0)
+    ms(v("F", sl(0, 1)), 512.0)
+    iota(v("cap"), [[0, 512]], 2048, 0)
+    pp = colts(P16, G16, Op.add)
+    ts(v("ID", 0), v("X", sl(0, 128)), pp, Op.is_equal)
+    ts(v("ID", 1), v("X", sl(0, 128)), pp, Op.is_equal, float(WS), Op.mult)
+    ts(v("slc"), v("slf"), G16, Op.subtract)
+    weights(v("WD"), G15, colts(P16, 0.0, Op.is_equal))
+
+    cp(v("mi", 3), v("msnd"))
+    cp(v("mi", sl(0, 3)), v("mrcv"))
+    for k in range(3):
+        ts(v("ml", ALL, slice(k, 66, 3)), v("mi", ALL, sl(64, 22)), 10 - 5 * k, Op.logical_shift_right, 31, Op.bitwise_and)
+    for r in (2, 0, 1):
+        if r == 2:
+            src = v("ml", ALL, sl(0, 64))
+        else:
+            src = v("pk" if r else "pk2", sl(0, 256))
+            ts(src, v("mi", ALL, sl(0, 64)), 0 if r else 8, Op.logical_shift_right, 255, Op.bitwise_and)
+        ts(v("mrole", r), src, -1.0, Op.add)
+        for s in range(4):
+            dma("YS"[s & 1], "t3a", v("T3", sl(1024 * secs[s], 1024), p=rows(4 * secs[s] + r)), v("mrole", r, s))
+    act(v("drow"), v("ZB", sl(0, 768)), Act.Identity, bias=colts(P4, 3.0, Op.is_lt))
+    cp(v("reph"), v("repf"))
+    mm([(v("pS", sl(0, 18)), wide("WD", u), v("reph", slice(u, 288, 16))) for u in range(16)])
+    cp(v("repl"), v("pS", sl(0, 18)))
+    ms(v("sc7", sl(0, 96)), 0.0)
+    for k in range(7):
+        ms(v("sc7", slice(k, 84, 7)), float(4 ** (k + 1)))
+    cp(v("sc7", sl(96, 96)), v("sc7", sl(0, 96)))
+    cp(v("sc7", sl(192, 96)), v("sc7", sl(0, 96)))
+
+    def zero_w(rd, gate=None):
+        for o in range(4):
+            node("Y", "d", [v("W", sl(o * WS + 512, C))], [v("ZB"), gate],
+                 lambda o=o: g.sync.dma_start(ap(v("W", sl(o * WS + 512, C))), ap(v("ZB"))), 100.0, DMAT + 1700.0, "wz%d" % rd, 16)
+    zero_w(0, v("hc"))
+    for k in range(HS):
+        act(v("HW", sl(1024 * k, 1024)), v("ZB", sl(0, 1024)), Act.Copy)
+    for k in range(2 * HS, 32):
+        iota(v("HW", sl(512 * k, 512)), [[0, 512]], 0, 0)
+    ts(v("G", sl(0, 1024)), v("hraw"), 1.0 / 256, Op.mult, 160.0 - 127.5 / 256, Op.add)
+    ts(v("hraw"), v("hraw"), 255, Op.bitwise_and)
+    cp(v("G", sl(1024, 1024)), v("hraw"))
+    act(v("G", sl(2048, 1024)), v("G", sl(1024, 1024)), Act.Identity, bias=BR2, scale=1.0 / 16)
+    for r in (0, 2):
+        act(v("G", sl(1024 * r, 1024)), v("G", sl(1024 * r, 1024)), Act.Identity, bias=B160)
+    for r in range(3):
+        dma("Y", "hw0", v("HW", p=rows(r)), v("G", sl(1024 * r, 1024)), 1 << 18)
+    r0, r1, r2 = [colts(P16, float(i), Op.is_equal) for i in range(3)]
+    weights(v("WH", 0), G15, colts(r0, 256.0, Op.mult, r1, Op.add))
+    weights(v("WH", 1), G15, colts(r0, 4096.0, Op.mult))
+    weights(v("WH", 2), G15, colts(r2, 4096.0, Op.mult))
+    weights(v("WH", 3), G15, colts(colts(r2, -16.0, Op.mult, r1, Op.add), 4096.0, Op.mult))
+    weights(v("WZ"), G15, 1.0)
+    ms(v("pat7"), 4.0); ms(v("pat7", sl(0, 252, 7)), 0.0)
+    ms(v("pat3"), 16.0); ms(v("pat3", sl(0, 72, 3)), 0.0)
+    ts(v("Xi"), v("Xi"), 4, Op.logical_shift_right)
+    ts(v("ONE"), v("Xi"), PG, Op.is_equal)
+    act(v("ON8"), v("ONE"), Act.Copy, scale=8.0)
+    for k in range(4):
+        ts(v("WE", k), v("ONE"), colts(P16, float(4 * k + 2), Op.is_equal), Op.mult)
+        act(v("WK", k), v("ONE"), Act.Identity, scale=colts(P4, float(k), Op.is_equal))
+    for k in range(2):
+        ms(v("xs", sl(k * XS, 8)), 0.0)
+        ms(v("ct", sl(k * CS, 32)), 0.0)
+    A3, PCH = colts(PA, -1.0, Op.mult, 3.0, Op.add), colts(P16, 160.0, Op.add)
+    BCH, BLT = const(160.0 - 63.5 / 128), colts(P16, -1000.0, Op.mult, -160500.0, Op.add)
+    cp(v("WDf"), v("WD"))
+    iota(v("on1"), [[0, 152]], 1, 0); iota(v("neg8"), [[0, 128]], -8, 0); ms(v("qrt"), 0.25)
+    scan(v("Cc"), v("on1", sl(0, 128)), v("c3"), 0.0, Op.mult, Op.add)
+    ms(v("pat16"), 1.0); ms(v("pat16", sl(0, 128, 16)), 0.0)
+    ts(v("M16"), v("i16"), P16, Op.is_equal)
+    ts(v("tri"), v("i16"), P16, Op.is_gt)
+    ts(v("Dc"), v("slc", sl(0, 8)), 4104.0, Op.add)
+    ms(v("Pz", sl(0, 1)), 0.0); ms(v("Pz", sl(128, 8)), 0.0); ms(v("S", sl(0, 1)), 0.0)
+    for h in range(2):
+        iota(v("DS", sl(528 * h, 528)), [[0, 528]], 0, 0)
+    iota(v("Ww"), [[0, 512]], 0, 0); iota(v("B1", sl(128, 16)), [[0, 16]], 0, 0)
+    iota(v("A", sl(4096, 144)), [[0, 144]], -9, 0)
+    for h in range(4):
+        node("Y", "d", [v("wraw", h & 1)], [], lambda h=h: g.sync.dma_start(ap(v("wraw", h & 1)), T.wpos[:, sl(1024 * h, 1024)]),
+             100.0, DMAT + 2300.0, "lw%d" % h, 16, bysem["t3a"])
+        ts(v("A", sl(1024 * h, 1024)), v("wraw", h & 1), 0.25, Op.max)
+
+    def select(i, out):
+        tt(v("pr", i), v("RC", i), v("oh"), Op.mult)
+        scan(v("ps", i), v("pat4"), v("pr", i), 0.0, Op.mult, Op.add)
+        for o in out:
+            cp(o, v("ps", i, slice(3, 128, 4)))
+
+    def diag(src):
+        tt(v("b0"), src, v("M16"), Op.mult)
+        scan(v("b1"), v("pat16"), v("b0"), 0.0, Op.mult, Op.add)
+        return v("b1", slice(15, 128, 16))
+
+    xb = v("pS", sl(384, 128))
+
+    def barrier(rd):
+        cp(v("mi3", 0), v("m"))
+        ts(v("mi3", 1), v("mi3", 0), 3, Op.bitwise_and)
+        ts(v("ohs"), v("mi3", 1), A3, Op.is_equal)
+        tt(v("Xs"), v("Xq"), v("ohs"), Op.mult)
+        for k in range(4):
+            mm([(v("pS", slice(384 + k, 512, 4)), v("WK", k), v("Xs"))])
+        cp(v("c0", 0), diag(xb))
+        cp(v("xi", 0), xb)
+        ts(v("c0", 1), v("c0", 0), 5, Op.logical_shift_right, 127, Op.bitwise_and)
+        ts(v("c0", 2), v("c0", 0), 8, Op.logical_shift_right, 768, Op.bitwise_and)
+        ts(v("xi", 3), v("xi", 0), 12, Op.logical_shift_right, 15, Op.bitwise_and)
+        tt(v("c0", 3), v("c0", 1), v("c0", 2), Op.add)
+        ts(v("be"), v("xi", 3), P16, Op.is_equal)
+        cp(v("cl", 0), v("c0", 3))
+        tt(v("bg"), ind(v("DS", slice(24, 1056)), v("cl", 0)), v("be"), Op.mult)
+        mm([(xb, v("ONE"), v("bg"))])
+        ts(v("xi", 1), v("xi", 0), 31, Op.bitwise_and)
+        ts(v("xi", 2), v("xi", 0), 5, Op.logical_shift_right)
+        tt(v("be"), v("xi", 2), xb, Op.subtract)
+        tt(v("va"), xb, v("xi", 1), Op.is_lt)
+        ts(v("ys", 0), v("be"), 0.0, Op.max)
+        cp(v("c0", 0), diag(v("ys", 0)))
+        ts(v("ys", 1), v("ys", 0), 15, Op.bitwise_and)
+        ts(v("c0", 1), v("c0", 0), 4, Op.logical_shift_right)
+        ts(v("be"), v("ys", 1), P16, Op.is_equal)
+        cp(v("cl", 0), v("c0", 1))
+        tt(v("mv"), v("be"), v("va"), Op.mult)
+        tt(v("bg"), ind(v("Ww"), v("cl", 0)), v("mv"), Op.mult)
+        mm([(xb, v("ONE"), v("mv")), (xb, v("ONE"), v("bg"))])
+        if rd < RO - 1:
+            sm = diag(xb)
+            act(v("B1", sl(0, 128)), xb, Act.Copy)
+            for c in range(8):
+                ts(v("E8", c, sl(0, 129 - 16 * c)), v("B1", slice(16 * c, 129)), v("b1", sl(16 * c + 15, 1)), Op.is_equal)
+            tt(v("E8", ALL, sl(0, 16)), v("E8", ALL, sl(0, 16)), v("tri"), Op.mult)
+            for c in range(8):
+                o1, i1 = v("cn", 0, sl(c, 1)), v("E8", c, sl(0, 129 - 16 * c))
+                run("V", o1, [i1], lambda o1=o1, i1=i1: g.vector.tensor_reduce(ap(o1), ap(i1), AxisListType.X, Op.max), 1.0, False)
+            ts(v("cn", 1), v("cn", 0), 8192.0, Op.mult, -1.0, Op.add)
+            tt(v("cn", 2), v("cn", 1), sm, Op.add)
+            tt(v("cn", 3), v("cn", 2), v("Dc"), Op.min)
+            cp(v("cl", 1), v("cn", 3))
+            cp(ind(v("A"), v("cl", 1)), v("qrt"))
+        act(v("ybo", sl(128 * rd, 128)), xb, Act.Identity, bias=BM1)
+
+    def outputs(rd):
+        select(2, [v("ywo", sl(32 * rd, 32))])
+        tt(v("kd"), v("key"), v("c3"), Op.subtract)
+        act(v("yto", sl(128 * rd, 128)), v("kd"), Act.Copy, scale=0.25)
+
+    def expand(rd):
+        select(0, [v("rq"), v("rqi")])
+        act(v("G3"), ind(v("T3"), v("rq")), Act.Copy)
+        act(v("Gb"), v("G3"), Act.Identity, bias=BG4, scale=4096.0)
+        ts(v("qi"), v("rqi"), 10, Op.logical_shift_right)
+        scan(v("F", sl(1, 512)), v("G3"), v("cap"), 512.0, Op.add, Op.min)
+        cp(v("qh"), v("qi"))
+        act(v("d0"), v("G3"), Act.Relu, scale=-1.0)
+        act(v("G2"), v("G3"), Act.Identity, bias=BIA, scale=KAP)
+        o32 = v("pS", sl(0, 32))
+        mm([(o32, v("ID", 0), v("slc", sl(0, 32))), (o32, v("ID", 1), v("qh"))], last=False)
+        for h in range(2):
+            tt(v("vv", sl(256 * h, 256)), v("F", sl(256 * h, 256)), v("Gb", sl(256 * h, 256)), Op.min)
+        mm([(o32, wide("WL", u), v("vv", slice(u, 512, 16))) for u in range(16)], first=False)
+        scan(v("ff", sl(1, 512)), v("d0"), v("G3"), FF0, Op.mult, Op.max)
+        cp(v("off"), o32)
+        tt(ind(v("W"), v("off")), v("ff", sl(0, 512)), v("G2"), Op.add)
+        ts(v("s0"), v("qi"), -512.0, Op.mult, -512.0, Op.add)
+        tt(v("s1"), o32, v("s0"), Op.add)
+        for n, s in enumerate(ORD):
+            o = secs[s]
+            out = v("pA", sl(96 * s, 96)) if s < 3 else v("pR1", sl(256, 96))
+            for h in range(2):
+                scan(v("Ds", n & 1, sl(768 * h, 768)), v("drow", sl(0, 768)), v("W", sl(o * WS + 512 + 768 * h, 768)),
+                     v("Ds", n & 1, sl(767, 1)) if h else 0.0, Op.mult, Op.add)
+            mm([(out, v("ID", 0), v("slc")), (out, v("ID", 0), v("n32"))] + [(out, wide("WA", u, o), v("Ds", n & 1, slice(u, C, 16))) for u in range(16)])
+        cp(v("ai", sl(0, 3)), v("pA", sl(0, 288)))
+        ts(v("aa", sl(0, 288)), v("ai", sl(0, 3)), 16383, Op.bitwise_and)
+        tt(v("pk"), ind(v("aa", sl(0, 288)), v("repl")), v("sc7"), Op.mult)
+        ts(v("pk2"), v("pk"), 49152, Op.bitwise_and)
+        tt(v("pk3"), v("aa", sl(0, 288)), v("pk2"), Op.add)
+        cp(v("asnd", rd, ALL, sl(0, 84)), v("pk3", ALL, sl(0, 84)))
+        tw = send3("ra%d" % rd, [v("asnd", rd, s, sl(0, 84)) for s in range(3)], [v("arcv", rd, 2 - s, sl(0, 84)) for s in range(3)])
+        arrive("ra%d" % rd, 3 * quarter, v("arcv", rd), tw)
+        cp(v("ai", 3), v("pR1", sl(256, 96)))
+        ts(v("aa", sl(288, 96)), v("ai", 3), 16383, Op.bitwise_and)
+        cp(v("hl", 3), v("aa", sl(288, 96)))
+
+    def ends():
+        mm([(v("pC", sl(0, 32)), wide("WLb", u), v("Gb", slice(u, 512, 16))) for u in range(16)])
+        ts(v("s0"), v("qi"), 2048.0, Op.mult, 1536.0, Op.add)
+        tt(v("s2"), v("pC", sl(0, 32)), v("s1"), Op.add)
+        tt(v("s3"), v("s2"), v("s0"), Op.min)
+        tt(v("s2"), v("s3"), v("s1"), Op.subtract)
+        ts(v("s0"), v("s3"), 32.0, Op.mult)
+        ts(v("s4"), v("s2"), 0.0, Op.max, -32.0, Op.add)
+        tt(v("s2"), v("s0"), v("s4"), Op.add)
+        ts(v("Xq"), v("s2"), 0.0, Op.max)
+
+    def bounds():
+        tt(v("Et"), v("F", slice(4, 513, 4)), v("r1"), Op.add)
+        ts(v("Es"), v("Et"), 1536.0, Op.min)
+        for o in range(4):
+            mm([(v("pZ", sl(128 * o, 128)), v("WE", o), v("Es"))])
+        act(v("EB"), v("pZ"), Act.Copy)
+        mm([(v("pZ", sl(0, 32)), wide("WDf", u), v("EB", slice(u, 512, 16))) for u in range(16)])
+        act(v("ch"), v("EB"), Act.Identity, bias=BCH, scale=1.0 / 128)
+        act(v("lt"), v("ch"), Act.Sigmoid, bias=BLT, scale=1000.0)
+        ts(v("eq"), v("ch"), PCH, Op.is_equal)
+        cp(v("bi"), v("pZ", sl(0, 32)))
+        ts(v("bj"), v("bi"), 127, Op.bitwise_and)
+        cp(v("bl"), v("bj"))
+
+    def unpack_addr(rd):
+        cp(v("ui"), v("arcv", rd, ALL, sl(0, 84)))
+        ts(v("uh"), v("arcv", rd, ALL, sl(0, 84)), 1.0 / 16384, Op.mult, 160.0 - 8191.5 / 16384, Op.add)
+        scan(v("us"), v("pat7"), v("uh"), 0.0, Op.mult, Op.add)
+        ts(v("hl", sl(0, 3), sl(84, 12)), v("us", slice(6, 252, 7)), -160.0 * 5461, Op.add)
+        ts(v("ua"), v("ui"), 16383, Op.bitwise_and)
+        cp(v("hl", sl(0, 3), sl(0, 84)), v("ua"))
+
+    def look(s):
+        bank, g0 = "pR%d" % (s & 1), C * (s & 1)
+
+        def part(a, n, q="S"):
+            if q == "S":
+                act(v("G", sl(g0 + 16 * a, 16 * n)), ind(v("HW"), v("hl", s, sl(a, n))), Act.Copy)
+            else:
+                cp(v("G", sl(g0 + 16 * a, 16 * n)), ind(v("HW"), v("hl", s, sl(a, n))))
+        if s == 3:
+            part(0, 48); part(48, 48)
+            mm([(v(bank, sl(0, 96)), wide("WH", u, 0), v("G", sl(g0 + u, C - u, 16))) for u in range(16)])
+        else:
+            part(72, 24, LQ[s]); part(0, 36); part(36, 36)
+            mm([(v(bank, sl(0, 72)), wide("WH", 0, 0), v("ZB", sl(0, 72)))]
+               + [(v(bank, slice(k, 72, 3)), wide("WH", u, k + 1), v("G", sl(g0 + 1152 + u, 384 - u, 16))) for u in range(16) for k in range(3)], last=False)
+            mm([(v(bank, sl(0, 72)), wide("WH", u, 0), v("G", sl(g0 + u, 1152 - u, 16))) for u in range(16)], first=False)
+
+    twin = {}
+
+    def reply(rd, s):
+        cp(v("rsnd", rd, s), v("pR%d" % (s & 1), sl(0, 72)))
+        twin[2 - s] = send1(s, "rr%d%d" % (2 - s, rd), v("rsnd", rd, s), v("rrcv", rd, 2 - s))
+
+    def lists(rd, s):
+        o = secs[s]
+        if s == 3:
+            cp(v("Ww", sl(128 * o, 96)), v("pR1", sl(0, 96)))
+        else:
+            arrive("rr%d%d" % (s, rd), whole, v("rrcv", rd, s), twin[s])
+            cp(v("ri"), v("rrcv", rd, s))
+            ts(v("rh"), v("rrcv", rd, s), 1.0 / 4096, Op.mult, 160.0 - 2047.5 / 4096, Op.add)
+            ts(v("Ww", sl(128 * o, 72)), v("ri"), 4095, Op.bitwise_and)
+            scan(v("rs"), v("pat3"), v("rh"), 0.0, Op.mult, Op.add)
+            ts(v("Ww", sl(128 * o + 72, 24)), v("rs", slice(2, 72, 3)), -160.0 * 273, Op.add)
+        cp(v("l1", s), v("Ww", sl(128 * o, 96)))
+        tt(v("w2"), v("Ww", sl(128 * o, 96)), v("ai", s), Op.max)
+        ts(v("l2", s), v("w2"), 4096.0, Op.min)
+
+    Aw = v("A", sl(0, 4104))
+
+    def phrases(s, n):
+        o, x0, c0 = secs[s], (n & 1) * XS + 8, (n & 1) * CS + 32
+        for h in range(NP):
+            w = C // NP
+            x, d, z, ct = v("xs", sl(x0 + w * h, w)), v("d1", sl(w * h, w)), v("z", sl(w * h, w)), v("ct", sl(c0 + w * h, w))
+            act(x, ind(Aw, v("l1", s, sl(w * h // 16, w // 16))), Act.Identity, bias=BXS)
+            act(d, x, Act.Sigmoid, bias=BSG, scale=1000.0)
+            tt(ct, ind(Aw, v("l2", s, sl(w * h // 16, w // 16))), v("xs", sl(x0 - 1 + w * h, w)), Op.is_equal)
+            scan(z, ct, d, v("z", sl(w * h - 1, 1)) if h else 0.0, Op.mult, Op.add)
+            k = 12 // NP
+            mm([(v("pZ", sl(0, 128)), wide("WZ", i), v("z", sl(128 * i, 128))) for i in range(k * h, k * h + k)], h == 0, h == NP - 1)
+            mm([(v("pC", sl(0, 152)), wide("WZ", i), v("ct", sl(c0 - 24 + 128 * i, 152))) for i in range(k * h, k * h + k)], h == 0, h == NP - 1)
+        scan(v("Pz", sl(1, 128)), v("pZ", sl(0, 128)), v("neg8"), 0.0, Op.add, Op.add)
+        tt(v("T1", n & 1), ind(v("Pz"), v("bl", sl(8 * o, 8))), v("eq", sl(128 * o, 128)), Op.mult)
+        act(v("T2", n & 1), v("lt", sl(128 * o, 128)), Act.Identity, scale=v("Pz", sl(128, 1)))
+        t = v("pT", sl(0, 128))
+        mm([(t, v("ON8"), v("T1", n & 1)), (t, v("ON8"), v("T2", n & 1))], n == 0, n == 3)
+        act(v("nh"), v("pC", sl(0, 152)), Act.Sigmoid, bias=BNH, scale=-1000.0)
+        scan(v("DS", sl(256 * o, 152)), v("on1"), v("nh"), 100.0, Op.add, Op.mult)
+
+    def winners():
+        tt(v("S", sl(1, 128)), v("pT", sl(0, 128)), v("Cc"), Op.add)
+        tt(v("key"), v("S", sl(1, 128)), v("S", sl(0, 128)), Op.subtract)
+        tt(v("m1"), v("key", slice(0, 128, 2)), v("key", slice(1, 128, 2)), Op.max)
+        tt(v("m"), v("m1", slice(0, 64, 2)), v("m1", slice(1, 64, 2)), Op.max)
+        for a in range(4):
+            tt(v("oh", slice(a, 128, 4)), v("key", slice(a, 128, 4)), v("m"), Op.is_equal)
+
+    NP = 2
+    for rd in range(RO):
+        expand(rd)
+        if rd > 0:
+            barrier(rd - 1)
+            outputs(rd - 1)
+        up[0] = UP
+        gate.extend(sends[-1:] if GATE else [])
+        select(1, [v("nx")])
+        chain(rd < RO - 1)
+        up[0] = 0.0
+        ends()
+        bounds()
+        look(3)
+        lists(rd, 3)
+        unpack_addr(rd)
+        for s in (2, 1, 0):
+            look(s)
+            reply(rd, s)
+        if rd < RO - 1:
+            zero_w(rd + 1, v("rsnd", rd, 0))
+        for n, s in enumerate((3, 0, 1, 2)):
+            if s < 3:
+                lists(rd, s)
+            phrases(s, n)
+        winners()
+    outputs(RO - 1)
+    dma("Y", "oy0", T.yt[:], v("yto", p=rows(0)))
+    dma("S", "oy1", T.yw[:], v("ywo", p=rows(9)))
+    barrier(RO - 1)
+    dma("Y", "oy2", T.yb[:], v("ybo", p=rows(0)))
+
+    succ = [[] for _ in nodes]
+    for i, x in enumerate(nodes):
+        for j in x["dep"]:
+            succ[j].append(i)
+    level = [0.0] * len(nodes)
+    for i in range(len(nodes) - 1, -1, -1):
+        level[i] = nodes[i]["busy"] + nodes[i]["late"] + max([level[k] + WAKE for k in succ[i]] + [0.0])
+    level = [level[i] + nodes[i]["up"] for i in range(len(nodes))]
+    Q_, K_, B_, L_ = [[x[k] for x in nodes] for k in ("q", "kind", "busy", "late")]
+    gap = [[(k, 30.0 if Q_[k] == Q_[i] and K_[i] == "c" else WAKE) for k in succ[i]] for i in range(len(nodes))]
+
+    def lay_out(rank):
+        left = [len(x["dep"]) for x in nodes]
+        start, free, turn, end = [0.0] * len(nodes), {q: 0.0 for q in "VSPQYAD"}, [], 0.0
+        ready = {q: [i for i in range(len(nodes)) if not left[i] and Q_[i] == q] for q in "VSPQYA"}
+        for _ in nodes:
+            t0, q = min((max(free[q], min(start[i] for i in ready[q])), q) for q in ready if ready[q])
+            pick = max((i for i in ready[q] if start[i] <= t0 + 1.0), key=lambda i: rank[i])
+            soon = [i for i in ready[q] if start[i] < t0 + AHEAD * B_[pick] and rank[i] > rank[pick] + MARGIN]
+            if soon:
+                pick = max(soon, key=lambda i: rank[i])
+            ready[q].remove(pick)
+            turn.append(pick)
+            done = max(t0, start[pick]) + B_[pick]
+            if q != "A":
+                free[q] = done
+            if K_[pick] == "d":
+                free["D"] = max(free["D"], done) + L_[pick] - DMAT
+                done = free["D"] + DMAT
+            else:
+                done += L_[pick]
+            end = max(end, done)
+            for k, w in gap[pick]:
+                start[k] = max(start[k], done + w)
+                left[k] -= 1
+                if not left[k]:
+                    ready[Q_[k]].append(k)
+        return end, turn
+
+    if not FOUND:
+        rs = np.random.RandomState(SEED)
+        best, rank = lay_out(level)[0], np.array(level)
+        pred = [[] for _ in nodes]
+        for i in range(len(nodes)):
+            for k, w in gap[i]:
+                pred[k].append((i, w + L_[i]))
+
+        def backwards(turn):
+            place = {i: n for n, i in enumerate(turn)}
+            left, start, free, out = [len(x) for x in succ], list(L_), {q: 0.0 for q in "VSPQYA"}, [0.0] * len(nodes)
+            ready = {q: [i for i in range(len(nodes)) if not left[i] and Q_[i] == q] for q in free}
+            for _ in nodes:
+                t0, q = min((max(free[q], min(start[i] for i in ready[q])), q) for q in ready if ready[q])
+                pick = max((i for i in ready[q] if start[i] <= t0 + BACK), key=lambda i: place[i])
+                ready[q].remove(pick)
+                out[pick] = max(t0, start[pick]) + B_[pick]
+                if q != "A":
+                    free[q] = out[pick]
+                for k, w in pred[pick]:
+                    start[k] = max(start[k], out[pick] + w)
+                    left[k] -= 1
+                    if not left[k]:
+                        ready[Q_[k]].append(k)
+            return out
+        for n in range(TRIES):
+            if n % 100 == 0:
+                new = backwards(lay_out(rank.tolist())[1])
+                for _ in range(4):
+                    t, tn = lay_out(new)
+                    if t < best:
+                        best, rank = t, np.array(new)
+                    new = backwards(tn)
+            a = rs.randint(0, len(nodes))
+            new = rank.copy()
+            new[a:a + rs.randint(1, 40)] += rs.choice([-1.0, 1.0]) * rs.choice([300.0, 1000.0, 3000.0, 8000.0])
+            t = lay_out(new.tolist())[0]
+            if t <= best:
+                best, rank = t, new
+        FOUND.extend([rank.tolist(), best])
+    turn = lay_out(FOUND[0])[1]
+    count = {s: 0 for s in SEMAPHORES}
+    seen = {q: {} for q in eng}
+    mark = {}
+
+    def wait(q, sem, val):
+        if seen[q].get(sem, 0) < val:
+            eng[q].wait_ge(T.sem[sem], val)
+            seen[q][sem] = val
+
+    for i in turn:
+        x = nodes[i]
+        q = x["q"]
+        if x["kind"] != "a":
+            need = {}
+            for j, hard in x["dep"].items():
+                if hard and nodes[j]["kind"] != "r":
+                    need[mark[j][0]] = max(need.get(mark[j][0], 0), mark[j][1])
+            for sem in need:
+                wait(q, sem, need[sem])
+            inst = x["call"]()
+            if x["kind"] != "r":
+                inst.then_inc(T.sem[x["sem"] or q], x["n"])
+        sem = "sent" if x["kind"] == "r" else x["sem"] or q
+        count[sem] += x["n"]
+        mark[i] = (sem, count[sem])
+    for s in SEMAPHORES:
+        if count[s]:
+            wait("Q", s, count[s])
+
+
+FOUND, SEED, TRIES, GATE = [], 1, 1500, False
+BACK = 800.0
+AHEAD, MARGIN, UP, ORD, HS, LQ = 0.4, 300.0, 0.0, (0, 1, 2, 3), 11, "VVV"

@@ -1,41 +1,42 @@
 import numpy as np
 from concourse.bass import DstId, RemoteDMATransfer
-from concourse.mybir import AluOpType, AxisListType, ActivationFunctionType
+from concourse.mybir import AluOpType, ActivationFunctionType
 
 N, RO, C = 4, 3, 1536
 F32, BF, F16, I32, U16 = "float32", "bfloat16", "float16", "int32", "uint16"
 XS, CS, WS = 1544, 1568, 2560
+ROUND, HALF = 12582912.0, 1536.0
 
 BUFS = {
-    "wraw": (I32, [2, 1024]), "A": (F32, [4240]), "hraw": (I32, [1024]), "HW": (BF, [16384]), "ZB": (BF, [1536]), "T3": (BF, [4096]),
+    "wraw": (I32, [4096]), "A": (F32, [4240]), "hraw": (I32, [1024]), "HW": (BF, [16384]), "ZB": (BF, [1536]), "T3": (BF, [4096]),
     "TB": (F32, [1024]), "srn": (I32, [2, 256]), "srd": (F32, [8, 64]), "nxn": (I32, [64]), "nxf": (F32, [2, 64]), "curi": (I32, [32]),
-    "mg": (I32, [64]), "mo": (I32, [64]), "mq": (I32, [2, 64]), "mf": (F32, [3, 64]), "mlf": (F32, [66]), "mlh": (F32, [66]), "msnd": (U16, [88]),
-    "mrcv": (U16, [3, 88]), "mi": (I32, [4, 88]), "ml": (I32, [4, 66]), "mrole": (BF, [3, 4, 64]),
-    "pi": (I32, [8]), "pc": (F32, [96]), "X": (F32, [144]), "Xi": (I32, [128]), "WA": (F16, [4, 144]), "WL": (F16, [144]), "WD": (F16, [144]),
-    "WLb": (BF, [144]), "WH": (BF, [4, 144]), "WZ": (BF, [144]), "W4": (F32, [2, 144]), "Wn": (F32, [144]), "ONE": (F32, [128]),
-    "ON8": (F32, [128]), "WK": (F32, [4, 128]), "WE": (F16, [4, 128]), "ID": (F16, [2, 128]), "slf": (F32, [96]), "slc": (F16, [96]),
-    "r1": (F32, [128]), "Cc": (F32, [128]), "c3": (F32, [128]), "pat4": (F32, [128]), "pat7": (F32, [252]), "pat3": (F32, [72]), "pat5": (F32, [66]),
-    "pat16": (F32, [128]), "sc7": (F32, [288]), "repf": (F32, [288]), "reph": (F16, [288]), "repl": (U16, [18]), "drow": (BF, [768]),
-    "cap": (BF, [512]), "neg8": (F32, [128]), "on1": (F32, [152]), "qrt": (F32, [128]), "i16": (F32, [128]), "tri": (BF, [8, 16]),
-    "M16": (F32, [128]), "Dc": (F32, [8]),
-    "nx": (F32, [32]), "hc": (U16, [8]), "sl": (U16, [32]), "RG": (F32, [512]), "RC": (F32, [3, 128]), "oh": (F32, [128]),
-    "pr": (F32, [3, 128]), "ps": (F32, [3, 128]), "rq": (U16, [32]), "rqi": (I32, [32]), "qi": (I32, [32]), "qh": (F16, [32]),
-    "G3": (BF, [512]), "Gb": (BF, [512]), "G2": (BF, [512]), "F": (F16, [520]), "vv": (F16, [512]), "d0": (BF, [512]), "ff": (BF, [520]),
-    "off": (U16, [32]), "W": (BF, [4 * WS]), "Ds": (F16, [2, C]), "ai": (I32, [4, 96]), "aa": (I32, [384]),
-    "pk": (I32, [288]), "pk2": (I32, [288]), "pk3": (I32, [3, 96]), "asnd": (U16, [3, 3, 88]), "arcv": (U16, [3, 3, 88]),
-    "ui": (I32, [3, 84]), "ua": (I32, [3, 84]), "uh": (BF, [252]), "us": (F32, [252]), "hl": (U16, [4, 96]),
+    "mg": (I32, [64]), "mo": (I32, [64]), "mq": (I32, [2, 64]), "mf": (F32, [3, 64]), "mlf": (F32, [66]), "mlh": (F32, [66]),
+    "mx": (U16, [4, 88]), "mi": (I32, [4, 86]), "ml": (I32, [4, 66]), "mlo": (I32, [4, 64]), "mrole": (BF, [3, 4, 64]),
+    "pi": (I32, [8]), "pc": (F32, [128]), "X": (F32, [144]), "i16": (F32, [2, 128]), "NI": (F32, [400]),
+    "Mw": (F32, [144]), "M4": (F32, [144]), "ONE": (F32, [128]), "M16": (F32, [128]), "TR": (F32, [3, 128]), "ON8": (F32, [128]),
+    "WA": (BF, [4, 144]), "WL": (BF, [1, 144]), "TS": (BF, [2, 128]), "sg": (BF, [2, 104]), "WH": (BF, [4, 144]), "WZ": (BF, [2, 144]), "Wn": (F32, [2, 144]), "W4f": (F32, [2, 144]),
+    "W4": (BF, [4, 144]), "WB": (BF, [2, 144]), "ME": (BF, [144]), "WK": (BF, [12, 128]), "WE": (BF, [4, 128]), "ONn": (BF, [128]), "ID": (BF, [2, 128]),
+    "slc": (F16, [32]), "k24": (F16, [32]), "r1": (F16, [128]), "ck": (F16, [72]), "ck0": (F16, [96]), "Cc": (F32, [128]),
+    "pat4": (BF, [128]), "pat7": (BF, [84]), "pat3": (BF, [72]), "pat5": (F32, [66]), "pat16": (BF, [128]), "pat9": (BF, [72]),
+    "sc7": (F32, [96]), "repf": (F32, [6]), "repl": (U16, [6]), "l43": (U16, [8]), "cap": (BF, [512]), "top": (F32, [96]),
+    "neg8": (BF, [128]), "on1": (BF, [480]), "qrt": (F32, [128]), "Dc": (F32, [8]),
+    "hc": (U16, [8]), "sl": (U16, [32]), "RG": (F32, [512]), "RS": (F32, [128]), "oh": (F32, [128]),
+    "pr": (F32, [2, 128]), "ps": (F32, [2, 128]), "rq": (U16, [32]), "fld": (F16, [4, 32]),
+    "G3": (BF, [512]), "Gb": (BF, [512]), "G2": (BF, [512]), "F": (F16, [520]), "vv": (F16, [512]), "nf": (BF, [520]),
+    "off": (U16, [32]), "W": (BF, [4 * WS]), "dl": (F32, [4, 104]), "aa": (F32, [4, 96]),
+    "pk": (I32, [96]), "pk2": (I32, [84]), "pk3": (F32, [84]), "asnd": (U16, [3, 3, 88]), "arcv": (U16, [3, 3, 88]),
+    "ui": (I32, [84]), "ua": (I32, [84]), "uh": (BF, [84]), "us": (F32, [84]), "hl": (U16, [4, 96]),
     "G": (BF, [2 * C]), "rsnd": (U16, [3, 3, 72]), "rrcv": (U16, [3, 3, 72]), "ri": (I32, [72]), "rh": (BF, [72]), "rs": (F32, [72]),
-    "Ww": (I32, [512]), "w2": (I32, [96]), "l1": (U16, [4, 96]), "l2": (U16, [4, 96]),
-    "xs": (F32, [2 * XS]), "ct": (BF, [2 * CS]), "d1": (BF, [C]), "z": (BF, [C]), "Pz": (F32, [136]), "T1": (F32, [2, 128]), "T2": (F32, [2, 128]),
-    "nh": (BF, [152]), "DS": (F32, [1056]), "Es": (F16, [128]), "Et": (F32, [128]), "EB": (F32, [512]), "WDf": (F32, [144]), "n32": (F16, [96]), "ch": (BF, [512]), "lt": (BF, [512]), "eq": (BF, [512]),
-    "bi": (I32, [32]), "bj": (I32, [32]), "bl": (U16, [32]), "S": (F32, [136]), "key": (F32, [128]), "m1": (F32, [64]), "m": (F32, [32]),
-    "s0": (F32, [32]), "s1": (F32, [32]), "s2": (F32, [32]), "s3": (F32, [32]), "s4": (F32, [32]), "Xq": (F32, [32]), "mi3": (I32, [2, 32]),
-    "ohs": (F32, [32]), "Xs": (F32, [32]),
-    "b0": (F32, [128]), "b1": (F32, [128]), "c0": (I32, [4, 8]), "cl": (U16, [2, 8]), "xi": (I32, [4, 128]), "be": (F32, [128]), "bg": (F32, [128]),
-    "va": (F32, [128]), "ys": (I32, [2, 128]), "mv": (F32, [128]), "B1": (F32, [144]), "E8": (BF, [8, 144]), "jk": (BF, [144]), "cn": (F32, [4, 8]),
+    "Ww": (I32, [96]), "W2": (I32, [400]), "l1": (U16, [4, 96]), "l2": (U16, [4, 96]),
+    "xs": (F32, [2 * XS]), "ct": (BF, [2 * CS]), "d1": (BF, [2, C]), "z": (BF, [2, C]), "Pz": (F32, [2, 136]), "T1": (F32, [2, 128]), "T2": (F32, [2, 128]),
+    "nh": (BF, [480]), "DS": (BF, [480]), "ch": (BF, [512]), "lt": (BF, [512]), "eq": (BF, [512]),
+    "bi": (I32, [32]), "bj": (I32, [32]), "bh": (BF, [32]), "bl": (U16, [32]), "S": (F32, [136]), "key": (F32, [128]), "mk": (F32, [128]),
+    "s0": (F32, [32]), "s1": (F32, [32]), "s2": (F32, [32]), "s3": (F32, [32]), "s4": (F32, [32]),
+    "p2": (F16, [128]), "se": (F16, [128]), "cl": (U16, [3, 8]), "m1": (BF, [128]), "m2": (BF, [128]), "bg": (BF, [128]), "ys": (F32, [128]),
+    "m3": (F32, [128]), "bw": (F32, [128]), "b0": (F32, [128]), "b1": (F32, [136]), "E3": (BF, [8, 16, 9]), "cn": (F32, [72]), "co": (F32, [8]),
     "yto": (F32, [384]), "ybo": (F32, [384]), "ywo": (F32, [96]), "kd": (F32, [128]),
 }
-BANKS = ["pA", "pB", "pR0", "pR1", "pZ", "pC", "pT", "pS"]
+BANKS = ["pA", "pB", "pK", "pM", "pZ", "pC", "pT", "pS"]
 PLACE, SCRATCH = {}, {}
 for _k, (_d, _s) in BUFS.items():
     if len(_s) == 1 and _s[0] <= 520:
@@ -45,10 +46,10 @@ for _k, (_d, _s) in BUFS.items():
     else:
         SCRATCH[_k] = ("sbuf", [128] + _s, _d)
 SCRATCH.update({k: ("psum", [128, 512], F32) for k in BANKS})
-SEMAPHORES = (["V", "S", "P", "Q", "sent", "rm", "lm", "ls", "lc", "lh", "tb", "t3a", "hw0", "hw1", "oy0", "oy1", "oy2"]
-              + ["%s%d" % (k, i) for k in ("ra", "wz", "rr0", "rr1", "rr2") for i in range(RO)] + ["lw%d" % i for i in range(4)])
+SEMAPHORES = (["V", "S", "P", "Q", "sent", "rm", "lm", "ls", "lc", "lh", "tb", "t3a", "hw0", "hz", "oy0", "oy1", "oy2"]
+              + ["%s%d" % (k, i) for k in ("wz", "ra0", "ra1", "ra2", "rr0", "rr1", "rr2") for i in range(RO)] + ["lw%d" % i for i in range(8)])
 ALL = slice(None)
-CY, GATHER, SCATTER, PECY, WAKE, DMAT, FART = 1.04, 1.56, 3.8, 0.55, 90.0, 2000.0, 2800.0
+MODELS = [dict(c=1.04, g=1.62, s=3.95, p=0.52, byte=0.005, rows=250.0, same=30.0, wake=90.0, dma=2000.0, far=2800.0, call=300.0)]
 
 
 def rank_program(g, core, T, topo):
@@ -57,7 +58,7 @@ def rank_program(g, core, T, topo):
         return
     Op, Act = AluOpType, ActivationFunctionType
     eng = {"V": g.vector, "S": g.scalar, "P": g.tensor, "Q": g, "Y": g.sync}
-    nodes, hist, bysem, up, gate = [], {}, {}, [0.0], []
+    nodes, hist, bysem, tag = [], {}, {}, ["", 0]
 
     def v(name, *idx, p=ALL):
         if name in PLACE:
@@ -78,22 +79,19 @@ def rank_program(g, core, T, topo):
     def ap(x):
         return x[0] if isinstance(x, tuple) else x
 
-    def node(q, kind, outs, ins, call, busy, late=0.0, sem=None, n=1, after=()):
+    def node(q, kind, outs, ins, call, busy, late=(0, "c"), sem=None, n=1, after=()):
         outs = [x for x in outs if isinstance(x, tuple)]
         ins = [x for x in ins if isinstance(x, tuple)]
         rd = [r for x in ins for r in x[1]] + [r for x in outs + ins for r in x[2]]
-        wr = [r for x in outs for r in x[1]] + [r for r in rd if r[0] in BANKS]
+        wr = [r for x in outs for r in x[1]]
         i = len(nodes)
         dep = {j: False for j in after}
         for k, rs in (("w", wr), ("r", rd)):
             for (nm, lo, hi, pm) in rs:
                 for (l2, h2, p2, k2, j) in hist.get(nm, []):
-                    if l2 < hi and lo < h2 and (pm & p2) and (k == "w" or k2 == "w"):
+                    if l2 < hi and lo < h2 and (pm & p2) and (k == "w" or k2 == "w" or (nm in BANKS and nodes[j]["q"] != q)):
                         soft = kind == "c" and nodes[j]["kind"] == "c" and nodes[j]["q"] == q == "P"
                         dep[j] = dep.get(j, False) or not soft
-        for j in gate:
-            dep.setdefault(j, False)
-        del gate[:]
         for j in list(dep):
             if nodes[j]["kind"] == "d" and dep[j]:
                 for j2 in bysem[nodes[j]["sem"]]:
@@ -102,20 +100,21 @@ def rank_program(g, core, T, topo):
             hist[nm] = [e for e in hist.get(nm, []) if not (lo <= e[0] and e[1] <= hi and (e[2] & ~pm) == 0)] + [(lo, hi, pm, "w", i)]
         for (nm, lo, hi, pm) in rd:
             hist.setdefault(nm, []).append((lo, hi, pm, "r", i))
-        nodes.append({"q": q, "kind": kind, "call": call, "busy": busy, "late": late, "sem": sem, "n": n, "dep": dep, "up": up[0]})
+        nodes.append({"q": q, "kind": kind, "call": call, "busy": busy, "late": late, "sem": sem, "n": n, "dep": dep, "tag": tuple(tag)})
+        tag[1] += 1
         if kind == "d":
             bysem.setdefault(sem, []).append(i)
         return i
 
-    def run(q, o, ins, call, k=1.0, fast=True, more=()):
+    def run(q, o, ins, call, k=1.0, fast=True):
         xs = [x for x in [o] + ins if isinstance(x, tuple) and x[3] > 1] or [o]
         if o[2]:
-            t = 50 + o[3] * SCATTER * CY
+            t = (50.0, o[3], "s")
         elif any(x[2] for x in xs):
-            t = 50 + o[3] * GATHER * CY
+            t = (50.0 if q == "V" else 65.0, o[3], "g")
         else:
-            t = max(64, max(x[3] for x in xs) * (0.5 if fast and all(x[4] for x in xs) else k)) * CY
-        node(q, "c", [o] + list(more), ins, call, t)
+            t = (0.0, max(64, max(x[3] for x in xs) * (0.5 if fast and all(x[4] for x in xs) else k)), "c")
+        node(q, "c", [o], ins, call, t)
 
     def cp(o, i): run("V", o, [i], lambda: g.vector.tensor_copy(ap(o), ap(i)))
     def ms(o, c): run("V", o, [], lambda: g.vector.memset(ap(o), c))
@@ -130,567 +129,618 @@ def rank_program(g, core, T, topo):
     def scan(o, a, b, init, op0, op1):
         run("V", o, [a, b, init], lambda: g.vector.tensor_tensor_scan(ap(o), ap(a), ap(b), ap(init), op0, op1))
 
-    def act(o, i, f, bias=0.0, scale=1.0, acc=None):
-        run("S", o, [i, bias, scale], lambda: g.scalar.activation(ap(o), ap(i), f, bias=ap(bias), scale=ap(scale), accum_out=ap(acc)), 1.0, False, [acc])
+    def act(o, i, f, bias=0.0, scale=1.0):
+        run("S", o, [i, bias, scale], lambda: g.scalar.activation(ap(o), ap(i), f, bias=ap(bias), scale=ap(scale)), 1.0, False)
 
     def iota(o, pat, base, cm):
-        node("Q", "c", [o], [], lambda: g.iota(ap(o), pat, base, cm, allow_small_or_imprecise_dtypes=True), 130 + 2 * CY * o[3])
+        node("Q", "c", [o], [], lambda: g.iota(ap(o), pat, base, cm, allow_small_or_imprecise_dtypes=True), (130.0, 2 * o[3], "c"))
+
+    def pick(o, i, step, op):
+        node("Q", "c", [o], [i], lambda: g.affine_select(ap(o), ap(i), [[step, 128]], op, 0.0, 0, -step), (170.0, 2 * o[3], "c"))
+
+    def fill(q, o, c):
+        if q == "V":
+            ms(o, c)
+        elif q == "S":
+            act(o, v("ZB", sl(16, o[3])), Act.Identity, bias=c)
+        else:
+            iota(o, [[0, o[3]]], int(c), 0)
 
     def mm(items, first=True, last=True):
+        cost = [max(64, x[2][3]) * (1 if x[2][4] else 4) for x in items]
+        if sum(cost) > CHUNK and len(items) > 1:
+            h = len(items) // 2
+            mm(items[:h], first, False)
+            mm(items[h:], False, last)
+            return
+
         def call():
             for n, (o, l, r) in enumerate(items):
                 inst = g.tensor.matmul(ap(o), ap(l), ap(r), first and n == 0, last and n == len(items) - 1)
             return inst
-        node("P", "c", [items[0][0]], [y for x in items for y in x[1:]], call, sum(max(64, x[2][3]) * (1 if x[2][4] else 4) * PECY for x in items))
+        node("P", "c", [items[0][0]], [y for x in items for y in x[1:]], call, (0.0, sum(cost), "p"))
 
-    def dma(q, sem, o, i, nbytes=0):
-        node(q, "d", [o], [i], lambda: eng[q].dma_start(ap(o), ap(i)), 100.0, DMAT + nbytes / 200.0, sem, 16)
+    def dma(q, sem, o, i, nbytes=0, gate=None, after=()):
+        node(q, "d", [o], [i, gate], lambda: eng[q].dma_start(ap(o), ap(i)), (100.0, 0, "c"), (nbytes, "byte"), sem, 16, after)
 
     peer = [T.cores[(me + 1 + s) % N] for s in range(3)]
     whole = len(topo.engines(core, peer[0]))
-    quarter = whole // 4
     sends = []
 
-    def send3(sem, srcs, dsts):
+    def send_all(sem, src, dsts):
         def call():
-            trs = []
-            for s in range(3):
-                rid, pid, _ = topo.addr(peer[s])
-                es = topo.engines(core, peer[s])[s * quarter:(s + 1) * quarter]
-                trs.append(RemoteDMATransfer(dst_ids=[DstId(rid=rid, pnc=pid)], dma_engine_mask=sum(1 << e for e in es),
-                                             remote_sem=T.sem[sem], src=ap(srcs[s]), dst=ap(dsts[s])))
-            g.remote_dma_fused(trs, local_sem=T.sem["sent"])
-        sends.append(node("Q", "r", [], srcs, call, 300.0 if sends else 2300.0, n=3 * quarter, after=sends[-1:]))
+            ids = [DstId(rid=topo.addr(c)[0], pnc=topo.addr(c)[1]) for c in peer]
+            g.remote_dma_fused([RemoteDMATransfer(dst_ids=ids, dma_engine_mask=topo.mask(core, peer[0]), remote_sem=T.sem[sem],
+                                                  srcs=[ap(src)], dsts=[ap(d) for d in dsts])], local_sem=T.sem["sent"])
+        sends.append(node("Q", "r", [], [src], call, (2000.0, 1, "call"), n=whole))
         return sends[-1]
 
     def send1(s, sem, src, dst):
         def call():
             rid, pid, _ = topo.addr(peer[s])
             g.remote_dma(ap(dst), ap(src), T.sem[sem], T.sem["sent"], pid, rid, topo.mask(core, peer[s]))
-        sends.append(node("Q", "r", [], [src], call, 300.0, n=whole, after=sends[-1:]))
+        sends.append(node("Q", "r", [], [src], call, (0.0, 1, "call"), n=whole, after=sends[-1:]))
         return sends[-1]
 
     def arrive(sem, n, land, twin):
-        node("A", "a", [land], [], None, 0.0, FART, sem, n, [twin])
+        node("A", "a", [land], [], None, (0.0, 0, "c"), (1, "far"), sem, n, [twin])
 
     ncol = [0]
 
-    def newcol():
-        ncol[0] += 1
-        return v("pc", slice(ncol[0] - 1, ncol[0]))
+    def newcol(n=1):
+        ncol[0] += n
+        return v("pc", slice(ncol[0] - n, ncol[0]))
 
-    def colts(a, s1, op0, s2=None, op1=None):
-        c = newcol()
-        ts(c, a, s1, op0, s2, op1)
-        return c
+    def cols(a, s1, op0, s2=None, op1=None):
+        at = ncol[0]
+        ts(newcol(a[3]), a, s1, op0, s2, op1)
+        return [v("pc", sl(at + i, 1)) for i in range(a[3])]
 
-    def const(x):
-        c = newcol()
-        ms(c, x)
-        return c
-
-    def wide(name, u, *i): return v(name, *i, slice(15 - u, 143 - u))
-    def wide4(i, b): return v("W4", i, slice(12 - 4 * b, 140 - 4 * b))
-    def rows(r): return slice(r, 128, 16)
+    def colts(*a): return cols(*a)[0]
     def sl(a, n, st=1): return slice(a, a + n, st)
+    def wide(name, u, *i): return v(name, *i, slice(15 - u, 143 - u))
+    def wide4(name, i, b): return v(name, i, slice(12 - 4 * b, 140 - 4 * b))
+    def rows(r): return slice(r, 128, 16)
     secs = [(me + 1 + s) % N for s in range(3)] + [me]
 
     dma("Y", "lm", v("mg"), T.gst[:])
     dma("S", "lm", v("mo"), T.gln[:])
-    dma("Y", "ls", v("srn", 0), T.sens[:])
-    dma("S", "ls", v("srn", 1), T.rel[:])
+    dma("Y", "ls", v("srn", 0), T.sens[:], 1 << 17)
+    dma("S", "ls", v("srn", 1), T.rel[:], 1 << 17)
     dma("Y", "ls", v("nxn"), T.nxt[:])
     ms(v("curi"), 0)
     dma("S", "lc", v("curi", p=rows(0)), T.cur[:])
-    dma("Y", "lh", v("hraw"), T.heap[:], 1 << 19)
     ms(v("ZB"), 0.0)
-    P16, P4, PA, G16, PG = [newcol() for _ in range(5)]
-    BM1 = const(-1.0)
-    act(v("TB"), v("ZB", sl(0, 1024)), Act.Copy)
-    for h in range(4):
-        act(v("T3", sl(1024 * h, 1024)), v("ZB", sl(0, 1024)), Act.Identity, bias=BM1)
     iota(v("pi", sl(0, 1)), [[0, 1]], 0, 1)
     iota(v("X"), [[1, 144]], 0, 0)
     iota(v("nxf", 1), [[1, 64]], 0, 64)
-    iota(v("slf"), [[16, 96]], 0, 1)
-    iota(v("r1"), [[4, 128]], -508, 0)
-    iota(v("c3"), [[0, 32], [-1, 4]], 3, 0)
-    iota(v("i16"), [[0, 8], [1, 16]], 0, 0)
-    iota(v("repf"), [[0, 288]], 0, 0)
-    for s in range(3):
-        iota(v("repf", sl(96 * s, 84)), [[1, 12], [0, 7]], 96 * s + 84, 0)
-    iota(v("Xi"), [[1, 128]], 0, 0)
+    iota(v("i16", 0), [[0, 8], [1, 16]], 0, 0)
+    iota(v("i16", 1), [[1, 8], [0, 16]], 0, 0)
 
     ms(v("mlf"), 0.0)
     ms(v("pat5"), 32.0); ms(v("pat5", sl(0, 66, 3)), 0.0)
-    ms(v("msnd", sl(86, 2)), 0)
     cp(v("mlf", sl(0, 64)), v("mo"))
     scan(v("mlh"), v("pat5"), v("mlf"), 0.0, Op.mult, Op.add)
-    cp(v("msnd", sl(64, 22)), v("mlh", slice(2, 66, 3)))
-    ts(v("mq", 0), v("mg"), 7, Op.logical_shift_right)
-    ts(v("mf", 0), v("mg"), 257.0, Op.add)
-    ts(v("mf", 1), v("mq", 0), 128.0, Op.mult)
+    cp(v("mx", 3, sl(64, 22)), v("mlh", slice(2, 66, 3)))
+    tt(v("mq", 0), v("mg"), v("mo"), Op.add)
+    ts(v("mq", 1), v("mq", 0), 1.0 / 128, Op.mult, -64.5 / 128, Op.add)
+    ts(v("mf", 0), v("mq", 1), 128.0, Op.mult, 256.0, Op.add)
     ts(v("mf", 2), v("mo"), 65535.0, Op.mult)
-    tt(v("mf", 0), v("mf", 0), v("mf", 1), Op.add)
-    tt(v("mf", 1), v("mf", 0), v("mf", 2), Op.min)
-    cp(v("msnd", sl(0, 64)), v("mf", 1))
-    tw = send3("rm", [v("msnd")] * 3, [v("mrcv", 2 - s) for s in range(3)])
-    arrive("rm", 3 * quarter, v("mrcv"), tw)
+    tt(v("mf", 1), v("mf", 0), v("mq", 0), Op.add)
+    tt(v("mf", 0), v("mf", 1), v("mf", 2), Op.min)
+    cp(v("mx", 3, sl(0, 64)), v("mf", 0))
+    tw = send_all("rm", v("mx", 3, sl(0, 86)), [v("mx", 2 - s, sl(0, 86)) for s in range(3)])
+    arrive("rm", 3 * whole, v("mx", sl(0, 3)), tw)
 
-    for k, (sh, an) in enumerate(((0, 15), (0, 3), (2, 3), (0, 112), (4, 7))):
+    for k, (sh, an) in enumerate(((0, 15), (0, 3), (2, 3), (0, 112), (4, 7), (0, 127))):
         ts(v("pi", sl(k + 1, 1)), v("pi", sl(0, 1)), sh, Op.logical_shift_right, an, Op.bitwise_and)
-    cp(v("pc", sl(0, 5)), v("pi", sl(1, 5)))
-    G15 = colts(G16, 15.0, Op.add)
+    P16, P4, PA, G16, PG, PP = cols(v("pi", sl(1, 6)), 0.0, Op.add)
+    QA = cols(v("X", sl(0, 4)), PA, Op.is_equal)
+    Q4 = newcol(4)
+    ts(Q4, v("X", sl(0, 4)), P4, Op.is_equal)
+    ts(v("M16"), v("i16", 0), P16, Op.is_equal)
+    ts(v("ONE"), v("i16", 1), PG, Op.is_equal)
+    Q16 = [v("M16", sl(i, 1)) for i in range(16)]
+    ts(v("Mw"), v("X"), colts(G16, 15.0, Op.add), Op.is_equal)
+    ts(v("M4"), v("X"), colts(G16, P4, Op.add, 12.0, Op.add), Op.is_equal)
+
+    def weights(o, master, scale): act(o, v(master), Act.Identity, scale=scale)
+
+    fill(FILL["TB"], v("TB"), 0.0)
     for t in range(2):
         for a in range(4):
             cp(v("srd", 4 * t + a), v("srn", t, slice(a, 256, 4)))
     cp(v("nxf", 0), v("nxn"))
     ts(v("nxf", 1), v("nxf", 1), colts(G16, 64.0, Op.mult), Op.subtract)
     for r in range(10):
-        dma("Y", "tb", v("TB", p=rows(r)), v("srd", r) if r < 8 else v("nxf", r - 8))
-
-    def rowcol(vals, by):
-        c = None
-        for i, x in enumerate(vals):
-            if x:
-                d = colts(by, float(i), Op.is_equal, float(x), Op.mult)
-                c = d if c is None else colts(d, c, Op.add)
-        return c
-
-    def weights(o, at, w): ts(o, v("X"), at, Op.is_equal, w, Op.mult)
+        dma("YS"[r & 1], "tb", v("TB", p=rows(r)), v("srd", r) if r < 8 else v("nxf", r - 8))
+    dma("Y", "lh", v("hraw"), T.heap[:], 1 << 19, None, bysem["tb"][::2])
     for i in range(2):
-        weights(v("W4", i), colts(P16, 12.0 - 4 * i, Op.add, G16, Op.add), colts(PA, float(i), Op.is_equal))
-    weights(v("Wn"), G15, colts(P16, 8.0, Op.is_equal))
-    cp(v("nx"), v("curi"))
+        weights(v("W4f", i), "M4", QA[i])
+        weights(v("Wn", i), "Mw", Q16[8 + i])
+    cp(v("ps", 1, slice(3, 128, 4)), v("curi"))
     ms(v("oh"), 0.0); ms(v("oh", sl(0, 128, 4)), 1.0)
     ms(v("pat4"), 1.0); ms(v("pat4", sl(0, 128, 4)), 0.0)
+    RC0, RC1, XF = [v("pK", sl(128 * i, 128)) for i in range(3)]
 
     def chain(more):
-        mm([(v("pB", sl(0, 8)), wide4(0, b), v("nx", slice(b, 32, 4))) for b in range(4)])
-        cp(v("hc"), v("pB", sl(0, 8)))
-        act(v("RC", 2), ind(v("TB"), v("hc")), Act.Copy)
+        mm([(v("pK", sl(384, 8)), wide4("W4f", 0, b), v("ps", 1, slice(3 + 4 * b, 128, 16))) for b in range(4)])
+        cp(v("hc"), v("pK", sl(384, 8)))
+        act(v("RS"), ind(v("TB"), v("hc")), Act.Copy)
         if more:
-            mm([(v("pB", sl(0, 32)), wide4(0, b), v("RC", 2, slice(b, 128, 4))) for b in range(4)])
-            cp(v("sl"), v("pB", sl(0, 32)))
+            mm([(v("pK", sl(384, 32)), wide4("W4f", 0, b), v("RS", slice(b, 128, 4))) for b in range(4)])
+            cp(v("sl"), v("pK", sl(384, 32)))
             act(v("RG"), ind(v("TB"), v("sl")), Act.Copy)
-            mm([(v("pB", sl(0, 128)), wide4(1, b), v("RG", slice(b, 512, 4))) for b in range(4)])
-            act(v("RC", 0), v("pB", sl(0, 128)), Act.Copy)
-            mm([(v("pB", sl(128, 128)), wide("Wn", b), v("RG", slice(b, 512, 4))) for b in range(4)])
-            act(v("RC", 1), v("pB", sl(128, 128)), Act.Copy)
+            mm([(RC0, wide4("W4f", 1, b), v("RG", slice(b, 512, 4))) for b in range(4)])
+        mm([(RC1, wide("Wn", 9, 1), v("RS"))] + [(RC1, wide("Wn", b, 0), v("RG", slice(b, 512, 4))) for b in range(4 * more)])
 
     chain(True)
-    wa = rowcol([-128, -1, -1, 49152], P4)
-    ms(v("n32"), -32768.0)
-    for o in range(4):
-        weights(v("WA", o), G15, colts(PA, float(o), Op.is_equal, wa, Op.mult))
-    isl = colts(P4, 2.0, Op.is_equal)
-    weights(v("WL"), G15, isl)
-    ts(v("WLb"), v("WL"), 1.0 / 4096, Op.mult)
-    FF0, KAP, BIA = colts(isl, -1.0, Op.mult), colts(P4, 2.0, Op.is_lt, -1.0, Op.mult), colts(P4, 2.0, Op.is_ge)
-    BG4, BXS, BSG, BR2, B160, BNH = const(4096.0), const(1.0), const(-1250.0), const(160.0 - 7.5 / 16), const(-160.0), const(8500.0)
-    cp(v("ff", sl(0, 1)), FF0)
-    ms(v("F", sl(0, 1)), 512.0)
-    iota(v("cap"), [[0, 512]], 2048, 0)
-    pp = colts(P16, G16, Op.add)
-    ts(v("ID", 0), v("X", sl(0, 128)), pp, Op.is_equal)
-    ts(v("ID", 1), v("X", sl(0, 128)), pp, Op.is_equal, float(WS), Op.mult)
-    ts(v("slc"), v("slf"), G16, Op.subtract)
-    weights(v("WD"), G15, colts(P16, 0.0, Op.is_equal))
 
-    cp(v("mi", 3), v("msnd"))
-    cp(v("mi", sl(0, 3)), v("mrcv"))
-    for k in range(3):
-        ts(v("ml", ALL, slice(k, 66, 3)), v("mi", ALL, sl(64, 22)), 10 - 5 * k, Op.logical_shift_right, 31, Op.bitwise_and)
-    for r in (2, 0, 1):
-        if r == 2:
-            src = v("ml", ALL, sl(0, 64))
-        else:
-            src = v("pk" if r else "pk2", sl(0, 256))
-            ts(src, v("mi", ALL, sl(0, 64)), 0 if r else 8, Op.logical_shift_right, 255, Op.bitwise_and)
-        ts(v("mrole", r), src, -1.0, Op.add)
-        for s in range(4):
-            dma("YS"[s & 1], "t3a", v("T3", sl(1024 * secs[s], 1024), p=rows(4 * secs[s] + r)), v("mrole", r, s))
-    act(v("drow"), v("ZB", sl(0, 768)), Act.Identity, bias=colts(P4, 3.0, Op.is_lt))
-    cp(v("reph"), v("repf"))
-    mm([(v("pS", sl(0, 18)), wide("WD", u), v("reph", slice(u, 288, 16))) for u in range(16)])
-    cp(v("repl"), v("pS", sl(0, 18)))
-    ms(v("sc7", sl(0, 96)), 0.0)
+    LEN = colts(PA, 2.0, Op.is_ge)
+    EMP = colts(LEN, -129.0, Op.mult, 128.0, Op.add)
+    for h in range(4):
+        act(v("T3", sl(1024 * h, 1024)), v("ZB", sl(16, 1024)), Act.Identity, bias=EMP)
+    for ss in (sl(3, 1), sl(0, 3)):
+        cp(v("mi", ss), v("mx", ss, sl(0, 86)))
+        for r in (0, 1, 2):
+            if r == 2 and ss.start:
+                ts(v("mrole", r, 3), v("mo"), -1.0, Op.add)
+            elif r == 2:
+                for k in range(3):
+                    ts(v("ml", ss, slice(k, 66, 3)), v("mi", ss, sl(64, 22)), 10 - 5 * k, Op.logical_shift_right, 31, Op.bitwise_and)
+                ts(v("mrole", r, ss), v("ml", ss, sl(0, 64)), -1.0, Op.add)
+            elif r == 0:
+                ts(v("mrole", r, ss), v("mx", ss, sl(0, 64)), 1.0 / 256, Op.mult, 127.76, Op.add)
+            else:
+                ts(v("mlo", ss), v("mi", ss, sl(0, 64)), 255, Op.bitwise_and)
+                ts(v("mrole", r, ss), v("mlo", ss), 128.0, Op.add)
+            for s in range(4)[ss]:
+                dma("Y", "t3a", v("T3", sl(1024 * secs[s], 1024), p=rows(4 * r + secs[s])), v("mrole", r, s))
+    BGB, KAP = colts(EMP, -4096.0, Op.mult), colts(LEN, -1.0, Op.add)
+    BG2 = colts(LEN, QA[3], Op.add)
+    NF0 = colts(LEN, 129.0, Op.mult, colts(BG2, -129.0, Op.add), Op.add)
+    cp(v("nf", sl(0, 1)), NF0)
+    ms(v("F", sl(0, 1)), 512.0)
+    fill("V", v("cap"), 2048.0)
+    pick(v("TR", 0), v("ONE"), 1, Op.is_ge)
+    pick(v("TR", 1), v("ONE"), -1, Op.is_gt)
+    pick(v("TR", 2), v("ONE"), 1, Op.is_equal)
+    act(v("ID", 0), v("TR", 2), Act.Copy)
+    act(v("ID", 1), v("TR", 2), Act.Copy, scale=float(WS))
+    iota(v("NI"), [[16, 400]], 0, 1)
+    act(v("NI"), v("NI"), Act.Identity, bias=colts(G16, -1.0, Op.mult))
+    cp(v("slc"), v("NI", sl(0, 32)))
+    ms(v("k24"), -HALF)
+    weights(v("WL", 0), "Mw", LEN)
+    wa = colts(colts(PA, -127.0, Op.mult, 128.0, Op.add), -1.0, Op.max, colts(QA[3], -32767.0, Op.mult), Op.add)
+    for o, c in enumerate(cols(Q4, wa, Op.mult)):
+        weights(v("WA", o), "Mw", c)
+    ms(v("dl", ALL, sl(0, 1)), 0.0)
+    ms(v("top"), 16383.0)
+    ms(v("sc7"), 0.0)
     for k in range(7):
         ms(v("sc7", slice(k, 84, 7)), float(4 ** (k + 1)))
-    cp(v("sc7", sl(96, 96)), v("sc7", sl(0, 96)))
-    cp(v("sc7", sl(192, 96)), v("sc7", sl(0, 96)))
+    ts(v("repf"), v("NI", sl(0, 6)), 1.0 / 7, Op.mult, 84.0 - 3.0 / 7, Op.add)
+    ts(v("repl"), v("repf"), 95.0, Op.min)
+    ms(v("sg", ALL, sl(0, 1)), 0.0)
+    for i in range(2):
+        act(v("TS", i), v("TR", i), Act.Copy, scale=-16384.0)
+    cp(v("ZB", sl(0, 1)), QA[3])
 
     def zero_w(rd, gate=None):
         for o in range(4):
-            node("Y", "d", [v("W", sl(o * WS + 512, C))], [v("ZB"), gate],
-                 lambda o=o: g.sync.dma_start(ap(v("W", sl(o * WS + 512, C))), ap(v("ZB"))), 100.0, DMAT + 1700.0, "wz%d" % rd, 16)
-    zero_w(0, v("hc"))
-    for k in range(HS):
-        act(v("HW", sl(1024 * k, 1024)), v("ZB", sl(0, 1024)), Act.Copy)
-    for k in range(2 * HS, 32):
-        iota(v("HW", sl(512 * k, 512)), [[0, 512]], 0, 0)
+            pp = slice(o, 128, 4)
+            dma("Y", "wz%d" % rd, v("W", sl(o * WS + 512, C), p=pp), v("ZB", p=pp), 3 << 15, gate)
+    for o, q in enumerate(FILL["W"]):
+        for h in range(2):
+            fill(q, v("W", sl(o * WS + 512 + 768 * h, 768)), 0.0)
+    ts(v("W", slice(512, 4 * WS, WS)), v("X", sl(0, 4)), 0.0, Op.mult, QA[3], Op.add)
+    for k, q in enumerate(FILL["HW"]):
+        if q == "D":
+            dma("Y", "hz", v("HW", sl(1024 * k, 1024)), v("ZB", sl(16, 1024)), 1 << 18, v("hraw"))
+        else:
+            for h in range(2 if q == "Q" else 1):
+                fill(q, v("HW", sl(1024 * k + 512 * h, 512 if q == "Q" else 1024)), 0.0)
     ts(v("G", sl(0, 1024)), v("hraw"), 1.0 / 256, Op.mult, 160.0 - 127.5 / 256, Op.add)
     ts(v("hraw"), v("hraw"), 255, Op.bitwise_and)
     cp(v("G", sl(1024, 1024)), v("hraw"))
-    act(v("G", sl(2048, 1024)), v("G", sl(1024, 1024)), Act.Identity, bias=BR2, scale=1.0 / 16)
-    for r in (0, 2):
-        act(v("G", sl(1024 * r, 1024)), v("G", sl(1024 * r, 1024)), Act.Identity, bias=B160)
+    act(v("G", sl(2048, 1024)), v("G", sl(1024, 1024)), Act.Identity, bias=160.0 - 7.5 / 16, scale=1.0 / 16)
     for r in range(3):
         dma("Y", "hw0", v("HW", p=rows(r)), v("G", sl(1024 * r, 1024)), 1 << 18)
-    r0, r1, r2 = [colts(P16, float(i), Op.is_equal) for i in range(3)]
-    weights(v("WH", 0), G15, colts(r0, 256.0, Op.mult, r1, Op.add))
-    weights(v("WH", 1), G15, colts(r0, 4096.0, Op.mult))
-    weights(v("WH", 2), G15, colts(r2, 4096.0, Op.mult))
-    weights(v("WH", 3), G15, colts(colts(r2, -16.0, Op.mult, r1, Op.add), 4096.0, Op.mult))
-    weights(v("WZ"), G15, 1.0)
-    ms(v("pat7"), 4.0); ms(v("pat7", sl(0, 252, 7)), 0.0)
+    h0, h1, h2 = cols(v("M16", sl(0, 3)), 4096.0, Op.mult)
+    for i, c in enumerate((colts(Q16[0], 256.0, Op.mult, Q16[1], Op.add), h0, h2, colts(Q16[2], -65536.0, Op.mult, h1, Op.add))):
+        weights(v("WH", i), "Mw", c)
+    ms(v("ck"), -272.0); ms(v("ck", slice(2, 72, 3)), 4080.0); ms(v("ck0"), -16.0)
+    act(v("WZ", 0), v("Mw"), Act.Copy)
+    act(v("WZ", 1), v("Mw"), Act.Copy, scale=-1.0 / 16)
+    ms(v("pat7"), 4.0); ms(v("pat7", sl(0, 84, 7)), 0.0)
     ms(v("pat3"), 16.0); ms(v("pat3", sl(0, 72, 3)), 0.0)
-    ts(v("Xi"), v("Xi"), 4, Op.logical_shift_right)
-    ts(v("ONE"), v("Xi"), PG, Op.is_equal)
     act(v("ON8"), v("ONE"), Act.Copy, scale=8.0)
-    for k in range(4):
-        ts(v("WE", k), v("ONE"), colts(P16, float(4 * k + 2), Op.is_equal), Op.mult)
-        act(v("WK", k), v("ONE"), Act.Identity, scale=colts(P4, float(k), Op.is_equal))
+    act(v("ONn"), v("ONE"), Act.Copy, scale=-1.0)
+    for a in range(4):
+        weights(v("W4", a), "M4", QA[a])
+        weights(v("WE", a), "ONE", Q16[8 + a])
+    ts(v("ME"), v("X"), colts(colts(P4, 4.0, Op.mult, G16, Op.add), 3.0, Op.add), Op.is_equal, QA[2], Op.mult)
+    ts(v("r1"), v("X", sl(0, 128)), 4.0, Op.mult, -508.0, Op.add)
+    weights(v("WB", 0), "M4", colts(QA[1], -96.0, Op.mult, colts(QA[0], 120.0, Op.mult, QA[2], Op.add), Op.add))
+    weights(v("WB", 1), "M4", colts(QA[0], 96.0, Op.mult, colts(QA[2], 1.0 / 16, Op.mult), Op.add))
+    for k, c in enumerate(cols(v("M16", sl(0, 4)), float(C), Op.mult)):
+        weights(v("WK", k), "ONE", colts(c, Q16[8 + k], Op.add))
+        weights(v("WK", 4 + k), "ONE", Q16[4 + k])
+        weights(v("WK", 8 + k), "ONE", Q16[12 + k])
     for k in range(2):
         ms(v("xs", sl(k * XS, 8)), 0.0)
         ms(v("ct", sl(k * CS, 32)), 0.0)
-    A3, PCH = colts(PA, -1.0, Op.mult, 3.0, Op.add), colts(P16, 160.0, Op.add)
-    BCH, BLT = const(160.0 - 63.5 / 128), colts(P16, -1000.0, Op.mult, -160500.0, Op.add)
-    cp(v("WDf"), v("WD"))
-    iota(v("on1"), [[0, 152]], 1, 0); iota(v("neg8"), [[0, 128]], -8, 0); ms(v("qrt"), 0.25)
-    scan(v("Cc"), v("on1", sl(0, 128)), v("c3"), 0.0, Op.mult, Op.add)
+    PCH, PPC = colts(P16, 160.0, Op.add), colts(P16, HALF, Op.add)
+    BLT = colts(P16, -1000.0, Op.mult, -160500.0, Op.add)
+    act(v("neg8"), v("ZB", sl(16, 128)), Act.Identity, bias=colts(P16, 12.0, Op.is_lt, -8.0, Op.mult))
+    fill("S", v("on1"), 1.0); fill("S", v("qrt"), 0.25)
+    ms(v("Cc"), 1.5 / 128); ms(v("Cc", slice(1, 128, 4)), 2.0 / 128); ms(v("Cc", slice(3, 128, 4)), 0.0)
     ms(v("pat16"), 1.0); ms(v("pat16", sl(0, 128, 16)), 0.0)
-    ts(v("M16"), v("i16"), P16, Op.is_equal)
-    ts(v("tri"), v("i16"), P16, Op.is_gt)
-    ts(v("Dc"), v("slc", sl(0, 8)), 4104.0, Op.add)
-    ms(v("Pz", sl(0, 1)), 0.0); ms(v("Pz", sl(128, 8)), 0.0); ms(v("S", sl(0, 1)), 0.0)
-    for h in range(2):
-        iota(v("DS", sl(528 * h, 528)), [[0, 528]], 0, 0)
-    iota(v("Ww"), [[0, 512]], 0, 0); iota(v("B1", sl(128, 16)), [[0, 16]], 0, 0)
-    iota(v("A", sl(4096, 144)), [[0, 144]], -9, 0)
-    for h in range(4):
-        node("Y", "d", [v("wraw", h & 1)], [], lambda h=h: g.sync.dma_start(ap(v("wraw", h & 1)), T.wpos[:, sl(1024 * h, 1024)]),
-             100.0, DMAT + 2300.0, "lw%d" % h, 16, bysem["t3a"])
-        ts(v("A", sl(1024 * h, 1024)), v("wraw", h & 1), 0.25, Op.max)
+    ms(v("pat9"), 1.0); ms(v("pat9", sl(0, 72, 9)), 0.0); ms(v("pat9", slice(8, 72, 9)), 8192.0)
+    act(v("Dc"), v("NI", sl(0, 8)), Act.Identity, bias=4104.0)
+    ts(v("l43"), v("NI", sl(0, 8)), P4, Op.subtract, 3.0, Op.add)
+    ms(v("Pz", ALL, sl(0, 1)), 0.0); ms(v("S", sl(0, 1)), 0.0); ms(v("b1", sl(0, 1)), 0.0)
+    ms(v("E3"), 0.0); ms(v("W2", sl(384, 16)), -1)
+    ms(v("A", sl(0, 1)), -9.0); fill("S", v("A", sl(4097, 143)), -9.0)
+    for h in range(8):
+        dma("Y", "lw%d" % h, v("wraw", sl(512 * h, 512)), T.wpos[:, sl(512 * h, 512)], 1 << 18, None, bysem["t3a" if h < EARLY else "hw0"])
+        ts(v("A", sl(1 + 512 * h, 512)), v("wraw", sl(512 * h, 512)), 0.25, Op.max)
 
-    def select(i, out):
-        tt(v("pr", i), v("RC", i), v("oh"), Op.mult)
+    def select(i, src):
+        tt(v("pr", i), src, v("oh"), Op.mult)
         scan(v("ps", i), v("pat4"), v("pr", i), 0.0, Op.mult, Op.add)
-        for o in out:
-            cp(o, v("ps", i, slice(3, 128, 4)))
-
-    def diag(src):
-        tt(v("b0"), src, v("M16"), Op.mult)
-        scan(v("b1"), v("pat16"), v("b0"), 0.0, Op.mult, Op.add)
-        return v("b1", slice(15, 128, 16))
-
-    xb = v("pS", sl(384, 128))
+        return v("ps", i, slice(3, 128, 4))
 
     def barrier(rd):
-        cp(v("mi3", 0), v("m"))
-        ts(v("mi3", 1), v("mi3", 0), 3, Op.bitwise_and)
-        ts(v("ohs"), v("mi3", 1), A3, Op.is_equal)
-        tt(v("Xs"), v("Xq"), v("ohs"), Op.mult)
-        for k in range(4):
-            mm([(v("pS", slice(384 + k, 512, 4)), v("WK", k), v("Xs"))])
-        cp(v("c0", 0), diag(xb))
-        cp(v("xi", 0), xb)
-        ts(v("c0", 1), v("c0", 0), 5, Op.logical_shift_right, 127, Op.bitwise_and)
-        ts(v("c0", 2), v("c0", 0), 8, Op.logical_shift_right, 768, Op.bitwise_and)
-        ts(v("xi", 3), v("xi", 0), 12, Op.logical_shift_right, 15, Op.bitwise_and)
-        tt(v("c0", 3), v("c0", 1), v("c0", 2), Op.add)
-        ts(v("be"), v("xi", 3), P16, Op.is_equal)
-        cp(v("cl", 0), v("c0", 3))
-        tt(v("bg"), ind(v("DS", slice(24, 1056)), v("cl", 0)), v("be"), Op.mult)
-        mm([(xb, v("ONE"), v("bg"))])
-        ts(v("xi", 1), v("xi", 0), 31, Op.bitwise_and)
-        ts(v("xi", 2), v("xi", 0), 5, Op.logical_shift_right)
-        tt(v("be"), v("xi", 2), xb, Op.subtract)
-        tt(v("va"), xb, v("xi", 1), Op.is_lt)
-        ts(v("ys", 0), v("be"), 0.0, Op.max)
-        cp(v("c0", 0), diag(v("ys", 0)))
-        ts(v("ys", 1), v("ys", 0), 15, Op.bitwise_and)
-        ts(v("c0", 1), v("c0", 0), 4, Op.logical_shift_right)
-        ts(v("be"), v("ys", 1), P16, Op.is_equal)
-        cp(v("cl", 0), v("c0", 1))
-        tt(v("mv"), v("be"), v("va"), Op.mult)
-        tt(v("bg"), ind(v("Ww"), v("cl", 0)), v("mv"), Op.mult)
-        mm([(xb, v("ONE"), v("mv")), (xb, v("ONE"), v("bg"))])
+        act(v("nh"), v("pC", sl(0, 480)), Act.Sigmoid, bias=8500.0, scale=-1000.0)
+        scan(v("DS"), v("on1"), v("nh"), 100.0, Op.add, Op.mult)
+        tt(v("p2"), XF, v("oh"), Op.mult)
+        scan(v("se"), v("pat4"), v("p2"), 0.0, Op.mult, Op.add)
+        lanes, by4 = v("se", slice(3, 128, 4)), [v("se", slice(3 + 4 * b, 128, 16)) for b in range(4)]
+        mm([(v("pZ", sl(0, 8)), wide4("WB", 0, b), by4[b]) for b in range(4)]
+           + [(v("pZ", slice(128 * i + k, 128 * i + 128, 4)), v("WK", 4 * i + k), lanes) for i in (1, 2) for k in range(4)])
+        y, y16, xb = v("pZ", sl(384, 128)), v("pC", sl(480, 8)), v("pZ", sl(128, 128))
+        mm([(y16, wide4("WB", 1, b), by4[b]) for b in range(4)], last=False)
+        ts(v("cl", 0), v("pZ", sl(0, 8)), 24.0 - 24.0 * HALF, Op.add)
+        ts(v("m1"), v("pZ", sl(128, 128)), PPC, Op.is_equal)
+        tt(v("m2"), v("pZ", sl(256, 128)), v("m1"), Op.mult)
+        tt(v("bg"), ind(v("DS"), v("cl", 0)), v("m2"), Op.min)
+        mm([(y16, wide("WZ", u, 1), v("bg", slice(u, 128, 16))) for u in range(16)], first=False)
+        mm([(y, v("ONn"), v("bg"))] + [(v("pZ", slice(384 + k, 512, 4)), v("WK", k), lanes) for k in range(4)])
+        ts(v("cl", 1), y16, -96.0 * HALF - 7.5 / 16, Op.add)
+        act(v("ys"), y, Act.Identity, bias=-HALF * C)
+        tt(v("m3"), ind(v("NI"), v("cl", 1)), v("ys"), Op.is_equal)
+        tt(v("bw"), ind(v("W2"), v("cl", 1)), v("m3"), Op.mult)
+        mm([(xb, v("ON8"), v("bw"))])
+        act(xb, xb, Act.Relu, bias=1.0, scale=0.125)
         if rd < RO - 1:
-            sm = diag(xb)
-            act(v("B1", sl(0, 128)), xb, Act.Copy)
-            for c in range(8):
-                ts(v("E8", c, sl(0, 129 - 16 * c)), v("B1", slice(16 * c, 129)), v("b1", sl(16 * c + 15, 1)), Op.is_equal)
-            tt(v("E8", ALL, sl(0, 16)), v("E8", ALL, sl(0, 16)), v("tri"), Op.mult)
-            for c in range(8):
-                o1, i1 = v("cn", 0, sl(c, 1)), v("E8", c, sl(0, 129 - 16 * c))
-                run("V", o1, [i1], lambda o1=o1, i1=i1: g.vector.tensor_reduce(ap(o1), ap(i1), AxisListType.X, Op.max), 1.0, False)
-            ts(v("cn", 1), v("cn", 0), 8192.0, Op.mult, -1.0, Op.add)
-            tt(v("cn", 2), v("cn", 1), sm, Op.add)
-            tt(v("cn", 3), v("cn", 2), v("Dc"), Op.min)
-            cp(v("cl", 1), v("cn", 3))
-            cp(ind(v("A"), v("cl", 1)), v("qrt"))
-        act(v("ybo", sl(128 * rd, 128)), xb, Act.Identity, bias=BM1)
+            tt(v("b0"), xb, v("M16"), Op.mult)
+            scan(v("b1", sl(1, 128)), v("pat16"), v("b0"), 0.0, Op.mult, Op.add)
+            tt(v("E3", ALL, ALL, 7), xb, v("b1", sl(0, 128)), Op.is_equal)
+            for c in range(7):
+                ts(v("E3", slice(c + 1, 8), ALL, c), v("pZ", slice(144 + 16 * c, 256)), v("b1", sl(16 * c + 16, 1)), Op.is_equal)
+            mm([(v("pC", sl(0, 72)), wide("WZ", u, 0), v("E3", ALL, u, ALL)) for u in range(16)]
+               + [(v("pC", slice(8, 72, 9)), v("TR", 2), v("b1", slice(16, 129, 16)))])
+            scan(v("cn"), v("pat9"), v("pC", sl(0, 72)), 0.0, Op.mult, Op.add)
+            tt(v("co"), v("cn", slice(8, 72, 9)), v("Dc"), Op.min)
+            cp(v("cl", 2), v("co"))
+            cp(ind(v("A"), v("cl", 2)), v("qrt"))
+        act(v("ybo", sl(128 * rd, 128)), xb, Act.Identity, bias=-1.0)
 
-    def outputs(rd):
-        select(2, [v("ywo", sl(32 * rd, 32))])
-        tt(v("kd"), v("key"), v("c3"), Op.subtract)
-        act(v("yto", sl(128 * rd, 128)), v("kd"), Act.Copy, scale=0.25)
+    o32 = v("pS", sl(0, 32))
+    twa, twin = {}, {}
 
     def expand(rd):
-        select(0, [v("rq"), v("rqi")])
+        rq = select(0, RC0)
+        cp(v("rq"), rq)
         act(v("G3"), ind(v("T3"), v("rq")), Act.Copy)
-        act(v("Gb"), v("G3"), Act.Identity, bias=BG4, scale=4096.0)
-        ts(v("qi"), v("rqi"), 10, Op.logical_shift_right)
+        ts(v("fld", 0), rq, 1.0 / 1024, Op.mult, HALF - 511.5 / 1024, Op.add)
+        act(v("Gb"), v("G3"), Act.Identity, bias=BGB, scale=4096.0)
         scan(v("F", sl(1, 512)), v("G3"), v("cap"), 512.0, Op.add, Op.min)
-        cp(v("qh"), v("qi"))
-        act(v("d0"), v("G3"), Act.Relu, scale=-1.0)
-        act(v("G2"), v("G3"), Act.Identity, bias=BIA, scale=KAP)
-        o32 = v("pS", sl(0, 32))
-        mm([(o32, v("ID", 0), v("slc", sl(0, 32))), (o32, v("ID", 1), v("qh"))], last=False)
-        for h in range(2):
-            tt(v("vv", sl(256 * h, 256)), v("F", sl(256 * h, 256)), v("Gb", sl(256 * h, 256)), Op.min)
-        mm([(o32, wide("WL", u), v("vv", slice(u, 512, 16))) for u in range(16)], first=False)
-        scan(v("ff", sl(1, 512)), v("d0"), v("G3"), FF0, Op.mult, Op.max)
+        act(v("G2"), v("G3"), Act.Identity, bias=BG2, scale=KAP)
+        mm([(o32, v("ID", 0), v("slc")), (o32, v("ID", 1), v("k24")), (o32, v("ID", 1), v("fld", 0))], last=False)
+        scan(v("vv"), v("F", sl(0, 512)), v("Gb"), 0.0, Op.max, Op.min)
+        mm([(o32, wide("WL", u, 0), v("vv", slice(u, 512, 16))) for u in range(16)], first=False)
+        scan(v("nf", sl(1, 512)), v("Gb"), v("G2"), NF0, Op.add, Op.min)
         cp(v("off"), o32)
-        tt(ind(v("W"), v("off")), v("ff", sl(0, 512)), v("G2"), Op.add)
-        ts(v("s0"), v("qi"), -512.0, Op.mult, -512.0, Op.add)
-        tt(v("s1"), o32, v("s0"), Op.add)
+        tt(ind(v("W"), v("off")), v("G3"), v("nf", sl(0, 512)), Op.add)
         for n, s in enumerate(ORD):
-            o = secs[s]
-            out = v("pA", sl(96 * s, 96)) if s < 3 else v("pR1", sl(256, 96))
-            for h in range(2):
-                scan(v("Ds", n & 1, sl(768 * h, 768)), v("drow", sl(0, 768)), v("W", sl(o * WS + 512 + 768 * h, 768)),
-                     v("Ds", n & 1, sl(767, 1)) if h else 0.0, Op.mult, Op.add)
-            mm([(out, v("ID", 0), v("slc")), (out, v("ID", 0), v("n32"))] + [(out, wide("WA", u, o), v("Ds", n & 1, slice(u, C, 16))) for u in range(16)])
-        cp(v("ai", sl(0, 3)), v("pA", sl(0, 288)))
-        ts(v("aa", sl(0, 288)), v("ai", sl(0, 3)), 16383, Op.bitwise_and)
-        tt(v("pk"), ind(v("aa", sl(0, 288)), v("repl")), v("sc7"), Op.mult)
-        ts(v("pk2"), v("pk"), 49152, Op.bitwise_and)
-        tt(v("pk3"), v("aa", sl(0, 288)), v("pk2"), Op.add)
-        cp(v("asnd", rd, ALL, sl(0, 84)), v("pk3", ALL, sl(0, 84)))
-        tw = send3("ra%d" % rd, [v("asnd", rd, s, sl(0, 84)) for s in range(3)], [v("arcv", rd, 2 - s, sl(0, 84)) for s in range(3)])
-        arrive("ra%d" % rd, 3 * quarter, v("arcv", rd), tw)
-        cp(v("ai", 3), v("pR1", sl(256, 96)))
-        ts(v("aa", sl(288, 96)), v("ai", 3), 16383, Op.bitwise_and)
-        cp(v("hl", 3), v("aa", sl(288, 96)))
+            o, out = secs[s], v("p" + EB[n], sl(0, 96))
+            mm([(out, wide("WA", u, o), v("W", sl(o * WS + 512 + u, C - u, 16))) for u in range(16)])
+            act(v("dl", s, sl(1, 96)), out, Act.Identity, bias=16385.0)
+            act(v("sg", n & 1, sl(1, 96)), out, Act.Sign, bias=0.5)
+            mm([(out, v("TR", 1 - i), v("dl", s, sl(i, 96))) for i in range(2)] + [(out, v("TS", 1 - i), v("sg", n & 1, sl(i, 96))) for i in range(2)])
+            scan(v("aa", s), out, v("top"), 0.0, Op.add, Op.min)
+            if s == 3:
+                cp(v("hl", 3), v("aa", 3))
+            else:
+                tt(v("pk"), ind(v("aa", s), v("repl")), v("sc7"), Op.mult)
+                ts(v("pk2"), v("pk", sl(0, 84)), 49152, Op.bitwise_and)
+                tt(v("pk3"), v("aa", s, sl(0, 84)), v("pk2"), Op.add)
+                cp(v("asnd", rd, s, sl(0, 84)), v("pk3"))
+                twa[2 - s] = send1(s, "ra%d%d" % (2 - s, rd), v("asnd", rd, s, sl(0, 84)), v("arcv", rd, 2 - s, sl(0, 84)))
 
     def ends():
-        mm([(v("pC", sl(0, 32)), wide("WLb", u), v("Gb", slice(u, 512, 16))) for u in range(16)])
-        ts(v("s0"), v("qi"), 2048.0, Op.mult, 1536.0, Op.add)
-        tt(v("s2"), v("pC", sl(0, 32)), v("s1"), Op.add)
-        tt(v("s3"), v("s2"), v("s0"), Op.min)
-        tt(v("s2"), v("s3"), v("s1"), Op.subtract)
-        ts(v("s0"), v("s3"), 32.0, Op.mult)
-        ts(v("s4"), v("s2"), 0.0, Op.max, -32.0, Op.add)
-        tt(v("s2"), v("s0"), v("s4"), Op.add)
-        ts(v("Xq"), v("s2"), 0.0, Op.max)
+        mm([(v("pS", sl(32, 32)), wide("WL", u, 0), v("G3", slice(u, 512, 16))) for u in range(16)])
+        ts(v("s0"), v("fld", 0), -float(WS), Op.mult, HALF * WS - 512, Op.add)
+        tt(v("s1"), o32, v("s0"), Op.add)
+        tt(v("s2"), v("pS", sl(32, 32)), v("s1"), Op.add)
+        ts(v("s3"), v("s2"), 7.0, Op.add, C - 1.0, Op.min)
+        ts(v("s4"), v("s1"), 0.0, Op.max, float(C), Op.min)
+        tt(v("fld", 2), v("s3"), v("s4"), Op.max)
+        tt(v("fld", 3), v("fld", 2), v("s4"), Op.subtract)
+        ts(v("fld", 1), v("fld", 2), 1.0 / 96, Op.mult, HALF - 47.5 / 96, Op.add)
+        mm([(v("pK", slice(256 + a, 384, 4)), wide4("W4", a, f), v("fld", f)) for f in range(4) for a in range(4)])
 
     def bounds():
-        tt(v("Et"), v("F", slice(4, 513, 4)), v("r1"), Op.add)
-        ts(v("Es"), v("Et"), 1536.0, Op.min)
-        for o in range(4):
-            mm([(v("pZ", sl(128 * o, 128)), v("WE", o), v("Es"))])
-        act(v("EB"), v("pZ"), Act.Copy)
-        mm([(v("pZ", sl(0, 32)), wide("WDf", u), v("EB", slice(u, 512, 16))) for u in range(16)])
-        act(v("ch"), v("EB"), Act.Identity, bias=BCH, scale=1.0 / 128)
+        mm([(v("pT", sl(128 * o, 128)), v("WE", o), x) for o in range(4) for x in (v("r1"), v("F", slice(4, 513, 4)))])
+        act(v("ch"), v("pT"), Act.Identity, bias=160.0 - 63.5 / 128, scale=1.0 / 128)
         act(v("lt"), v("ch"), Act.Sigmoid, bias=BLT, scale=1000.0)
         ts(v("eq"), v("ch"), PCH, Op.is_equal)
-        cp(v("bi"), v("pZ", sl(0, 32)))
+        e1, e2 = v("pS", sl(64, 32)), v("pS", sl(96, 32))
+        mm([(e1, v("ME", sl(3 - b, 128)), x) for b in range(4) for x in (v("r1", slice(b, 128, 4)), v("F", slice(4 + 4 * b, 513, 16)))])
+        cp(v("bi"), e1)
         ts(v("bj"), v("bi"), 127, Op.bitwise_and)
-        cp(v("bl"), v("bj"))
+        cp(v("bh"), v("bj"))
+        mm([(v("pS", sl(96 + 8 * o, 8)), wide4("W4", o, b), v("bh", slice(b, 32, 4))) for o in range(4) for b in range(4)])
+        cp(v("bl"), e2)
 
-    def unpack_addr(rd):
-        cp(v("ui"), v("arcv", rd, ALL, sl(0, 84)))
-        ts(v("uh"), v("arcv", rd, ALL, sl(0, 84)), 1.0 / 16384, Op.mult, 160.0 - 8191.5 / 16384, Op.add)
+    def unpack_addr(rd, s):
+        land = v("arcv", rd, s, sl(0, 84))
+        arrive("ra%d%d" % (s, rd), whole, land, twa[s])
+        ts(v("uh"), land, 1.0 / 16384, Op.mult, 160.0 - 8191.5 / 16384, Op.add)
+        cp(v("ui"), land)
         scan(v("us"), v("pat7"), v("uh"), 0.0, Op.mult, Op.add)
-        ts(v("hl", sl(0, 3), sl(84, 12)), v("us", slice(6, 252, 7)), -160.0 * 5461, Op.add)
         ts(v("ua"), v("ui"), 16383, Op.bitwise_and)
-        cp(v("hl", sl(0, 3), sl(0, 84)), v("ua"))
+        ts(v("hl", s, sl(84, 12)), v("us", slice(6, 84, 7)), -160.0 * 5461, Op.add)
+        cp(v("hl", s, sl(0, 84)), v("ua"))
 
     def look(s):
-        bank, g0 = "pR%d" % (s & 1), C * (s & 1)
+        bank, g0 = "pA" if s & 1 else "pB", C * (s & 1)
 
-        def part(a, n, q="S"):
+        def part(a, n, q):
             if q == "S":
                 act(v("G", sl(g0 + 16 * a, 16 * n)), ind(v("HW"), v("hl", s, sl(a, n))), Act.Copy)
             else:
                 cp(v("G", sl(g0 + 16 * a, 16 * n)), ind(v("HW"), v("hl", s, sl(a, n))))
         if s == 3:
-            part(0, 48); part(48, 48)
-            mm([(v(bank, sl(0, 96)), wide("WH", u, 0), v("G", sl(g0 + u, C - u, 16))) for u in range(16)])
+            part(0, 48, LQ[s][0]); part(48, 48, LQ[s][1])
+            mm([(v(bank, sl(0, 96)), v("ID", 1), v("ck0"))] + [(v(bank, sl(0, 96)), wide("WH", u, 0), v("G", sl(g0 + u, C - u, 16))) for u in range(16)])
         else:
-            part(72, 24, LQ[s]); part(0, 36); part(36, 36)
-            mm([(v(bank, sl(0, 72)), wide("WH", 0, 0), v("ZB", sl(0, 72)))]
+            part(0, 36, LQ[s][1]); part(72, 24, LQ[s][0]); part(36, 36, LQ[s][2])
+            mm([(v(bank, sl(0, 72)), v("ID", 1), v("ck"))]
                + [(v(bank, slice(k, 72, 3)), wide("WH", u, k + 1), v("G", sl(g0 + 1152 + u, 384 - u, 16))) for u in range(16) for k in range(3)], last=False)
             mm([(v(bank, sl(0, 72)), wide("WH", u, 0), v("G", sl(g0 + u, 1152 - u, 16))) for u in range(16)], first=False)
 
-    twin = {}
-
     def reply(rd, s):
-        cp(v("rsnd", rd, s), v("pR%d" % (s & 1), sl(0, 72)))
+        cp(v("rsnd", rd, s), v("pA" if s & 1 else "pB", sl(0, 72)))
         twin[2 - s] = send1(s, "rr%d%d" % (2 - s, rd), v("rsnd", rd, s), v("rrcv", rd, 2 - s))
 
     def lists(rd, s):
         o = secs[s]
-        if s == 3:
-            cp(v("Ww", sl(128 * o, 96)), v("pR1", sl(0, 96)))
-        else:
+        if s < 3:
             arrive("rr%d%d" % (s, rd), whole, v("rrcv", rd, s), twin[s])
-            cp(v("ri"), v("rrcv", rd, s))
             ts(v("rh"), v("rrcv", rd, s), 1.0 / 4096, Op.mult, 160.0 - 2047.5 / 4096, Op.add)
-            ts(v("Ww", sl(128 * o, 72)), v("ri"), 4095, Op.bitwise_and)
+            cp(v("ri"), v("rrcv", rd, s))
             scan(v("rs"), v("pat3"), v("rh"), 0.0, Op.mult, Op.add)
-            ts(v("Ww", sl(128 * o + 72, 24)), v("rs", slice(2, 72, 3)), -160.0 * 273, Op.add)
-        cp(v("l1", s), v("Ww", sl(128 * o, 96)))
-        tt(v("w2"), v("Ww", sl(128 * o, 96)), v("ai", s), Op.max)
-        ts(v("l2", s), v("w2"), 4096.0, Op.min)
+            ts(v("Ww", sl(0, 72)), v("ri"), 4095, Op.bitwise_and)
+            ts(v("Ww", sl(72, 24)), v("rs", slice(2, 72, 3)), -160.0 * 273, Op.add)
+        ts(v("l1", s), v("pA", sl(0, 96)) if s == 3 else v("Ww"), 1.0, Op.add)
+        tt(v("W2", sl(96 * o, 96)), v("pA", sl(0, 96)) if s == 3 else v("Ww"), v("dl", s, sl(1, 96)), Op.min)
+        ts(v("l2", s), v("W2", sl(96 * o, 96)), 1.0, Op.add)
 
     Aw = v("A", sl(0, 4104))
 
     def phrases(s, n):
-        o, x0, c0 = secs[s], (n & 1) * XS + 8, (n & 1) * CS + 32
-        for h in range(NP):
-            w = C // NP
-            x, d, z, ct = v("xs", sl(x0 + w * h, w)), v("d1", sl(w * h, w)), v("z", sl(w * h, w)), v("ct", sl(c0 + w * h, w))
-            act(x, ind(Aw, v("l1", s, sl(w * h // 16, w // 16))), Act.Identity, bias=BXS)
-            act(d, x, Act.Sigmoid, bias=BSG, scale=1000.0)
-            tt(ct, ind(Aw, v("l2", s, sl(w * h // 16, w // 16))), v("xs", sl(x0 - 1 + w * h, w)), Op.is_equal)
-            scan(z, ct, d, v("z", sl(w * h - 1, 1)) if h else 0.0, Op.mult, Op.add)
-            k = 12 // NP
-            mm([(v("pZ", sl(0, 128)), wide("WZ", i), v("z", sl(128 * i, 128))) for i in range(k * h, k * h + k)], h == 0, h == NP - 1)
-            mm([(v("pC", sl(0, 152)), wide("WZ", i), v("ct", sl(c0 - 24 + 128 * i, 152))) for i in range(k * h, k * h + k)], h == 0, h == NP - 1)
-        scan(v("Pz", sl(1, 128)), v("pZ", sl(0, 128)), v("neg8"), 0.0, Op.add, Op.add)
-        tt(v("T1", n & 1), ind(v("Pz"), v("bl", sl(8 * o, 8))), v("eq", sl(128 * o, 128)), Op.mult)
-        act(v("T2", n & 1), v("lt", sl(128 * o, 128)), Act.Identity, scale=v("Pz", sl(128, 1)))
+        o, b = secs[s], n & 1
+        x0, c0 = b * XS + 8, b * CS + 32
+        at = 0
+        for h, w in enumerate(PARTS[n]):
+            x, d, z, ct = v("xs", sl(x0 + at, w)), v("d1", b, sl(at, w)), v("z", b, sl(at, w)), v("ct", sl(c0 + at, w))
+            act(x, ind(Aw, v("l1", s, sl(at // 16, w // 16))), Act.Identity, bias=1.0)
+            act(d, x, Act.Sigmoid, bias=-1250.0, scale=1000.0)
+            tt(ct, ind(Aw, v("l2", s, sl(at // 16, w // 16))), v("xs", sl(x0 - 1 + at, w)), Op.is_equal)
+            scan(z, ct, d, v("z", b, sl(at - 1, 1)) if h else 0.0, Op.mult, Op.add)
+            mm([(v("pZ", sl(0, 128)), wide("WZ", i, 0), v("z", b, sl(128 * i, 128))) for i in range(at // 128, (at + w) // 128)], at == 0, at + w == C)
+            at += w
+        scan(v("Pz", b, sl(1, 128)), v("pZ", sl(0, 128)), v("neg8"), 0.0, Op.add, Op.add)
+        tt(v("T1", b), ind(v("Pz", b, sl(0, 128)), v("bl", sl(8 * o, 8))), v("eq", sl(128 * o, 128)), Op.mult)
+        act(v("T2", b), v("lt", sl(128 * o, 128)), Act.Identity, scale=v("Pz", b, sl(128, 1)))
         t = v("pT", sl(0, 128))
-        mm([(t, v("ON8"), v("T1", n & 1)), (t, v("ON8"), v("T2", n & 1))], n == 0, n == 3)
-        act(v("nh"), v("pC", sl(0, 152)), Act.Sigmoid, bias=BNH, scale=-1000.0)
-        scan(v("DS", sl(256 * o, 152)), v("on1"), v("nh"), 100.0, Op.add, Op.mult)
+        mm([(t, v("ON8"), v(k)) for k in ["Cc"][n:]] + [(t, v("ON8"), v("T2", b))], n == 0, False)
+        mm([(t, v("ON8"), v("T1", b))], False, n == 3)
+        mm([(v("pC", sl(120 * o, 120)), wide("WZ", i, 0), v("ct", sl(c0 - 24 + 96 * i, 120))) for i in range(16)])
 
-    def winners():
-        tt(v("S", sl(1, 128)), v("pT", sl(0, 128)), v("Cc"), Op.add)
-        tt(v("key"), v("S", sl(1, 128)), v("S", sl(0, 128)), Op.subtract)
-        tt(v("m1"), v("key", slice(0, 128, 2)), v("key", slice(1, 128, 2)), Op.max)
-        tt(v("m"), v("m1", slice(0, 64, 2)), v("m1", slice(1, 64, 2)), Op.max)
-        for a in range(4):
-            tt(v("oh", slice(a, 128, 4)), v("key", slice(a, 128, 4)), v("m"), Op.is_equal)
+    def winners(rd):
+        cp(v("S", sl(1, 128)), v("pT", sl(0, 128)))
+        tt(v("key"), v("pT", sl(0, 128)), v("S", sl(0, 128)), Op.subtract)
+        scan(v("mk"), v("pat4"), v("key"), 0.0, Op.mult, Op.max)
+        tt(v("oh"), ind(v("mk"), v("l43")), v("key"), Op.is_equal)
+        act(v("kd"), v("key"), Act.Identity, bias=ROUND, scale=0.25)
+        act(v("yto", sl(128 * rd, 128)), v("kd"), Act.Identity, bias=-ROUND)
 
-    NP = 2
+    def heads(rd):
+        act(v("ywo", sl(32 * rd, 32)), select(1, RC1), Act.Copy)
+
+    def step(f, *a):
+        tag[:] = [(f, a[-1:] if f in (look, lists, reply, unpack_addr, phrases) else ()), 0]
+        f(*a)
+
     for rd in range(RO):
-        expand(rd)
+        step(expand, rd)
         if rd > 0:
-            barrier(rd - 1)
-            outputs(rd - 1)
-        up[0] = UP
-        gate.extend(sends[-1:] if GATE else [])
-        select(1, [v("nx")])
-        chain(rd < RO - 1)
-        up[0] = 0.0
-        ends()
-        bounds()
-        look(3)
-        lists(rd, 3)
-        unpack_addr(rd)
+            step(heads, rd - 1)
+            step(barrier, rd - 1)
+        else:
+            step(select, 1, RC1)
+        step(chain, rd < RO - 1)
+        step(ends)
+        step(bounds)
+        step(look, 3)
+        step(lists, rd, 3)
         for s in (2, 1, 0):
-            look(s)
-            reply(rd, s)
+            step(unpack_addr, rd, s)
+            step(look, s)
+            step(reply, rd, s)
         if rd < RO - 1:
-            zero_w(rd + 1, v("rsnd", rd, 0))
+            step(zero_w, rd + 1, v("rsnd", rd, 0))
         for n, s in enumerate((3, 0, 1, 2)):
             if s < 3:
-                lists(rd, s)
-            phrases(s, n)
-        winners()
-    outputs(RO - 1)
+                step(lists, rd, s)
+            step(phrases, s, n)
+        step(winners, rd)
+    step(heads, RO - 1)
     dma("Y", "oy0", T.yt[:], v("yto", p=rows(0)))
     dma("S", "oy1", T.yw[:], v("ywo", p=rows(9)))
-    barrier(RO - 1)
+    step(barrier, RO - 1)
     dma("Y", "oy2", T.yb[:], v("ybo", p=rows(0)))
 
     succ = [[] for _ in nodes]
     for i, x in enumerate(nodes):
         for j in x["dep"]:
             succ[j].append(i)
-    level = [0.0] * len(nodes)
-    for i in range(len(nodes) - 1, -1, -1):
-        level[i] = nodes[i]["busy"] + nodes[i]["late"] + max([level[k] + WAKE for k in succ[i]] + [0.0])
-    level = [level[i] + nodes[i]["up"] for i in range(len(nodes))]
-    Q_, K_, B_, L_ = [[x[k] for x in nodes] for k in ("q", "kind", "busy", "late")]
-    gap = [[(k, 30.0 if Q_[k] == Q_[i] and K_[i] == "c" else WAKE) for k in succ[i]] for i in range(len(nodes))]
+    n_, deps = len(nodes), [len(x["dep"]) for x in nodes]
+    Q_, K_ = ["AVSPQY".index(x["q"]) for x in nodes], ["acdr".index(x["kind"]) for x in nodes]
+    models = []
+    for m in MODELS:
+        gap = [[(j, -1e9 if K_[j] == 2 and not hard else 0.0 if not hard else m["same"] if Q_[j] == Q_[i] and K_[j] == 1 else m["wake"])
+                for j, hard in nodes[i]["dep"].items()] for i in range(n_)]
+        models.append(([x["busy"][0] + x["busy"][1] * m[x["busy"][2]] for x in nodes], [x["late"][0] * m[x["late"][1]] + (m["rows"] if x["kind"] == "d" else 0.0) for x in nodes], gap, m["dma"]))
+    B_, L_, G_, D_ = models[0]
+    level = [0.0] * n_
+    for i in range(n_ - 1, -1, -1):
+        level[i] = B_[i] + L_[i] + (D_ if K_[i] == 2 else 0.0) + max([level[k] + 90.0 for k in succ[i]] + [0.0])
 
     def lay_out(rank):
-        left = [len(x["dep"]) for x in nodes]
-        start, free, turn, end = [0.0] * len(nodes), {q: 0.0 for q in "VSPQYAD"}, [], 0.0
-        ready = {q: [i for i in range(len(nodes)) if not left[i] and Q_[i] == q] for q in "VSPQYA"}
+        left, done, free, dfree, turn = list(deps), [0.0] * n_, [0.0] * 6, 0.0, []
+        start = [0.0] * n_
+        ready = [[i for i in range(n_) if not left[i] and Q_[i] == q] for q in range(6)]
+        when = [0.0 if x else 1e18 for x in ready]
         for _ in nodes:
-            t0, q = min((max(free[q], min(start[i] for i in ready[q])), q) for q in ready if ready[q])
-            pick = max((i for i in ready[q] if start[i] <= t0 + 1.0), key=lambda i: rank[i])
-            soon = [i for i in ready[q] if start[i] < t0 + AHEAD * B_[pick] and rank[i] > rank[pick] + MARGIN]
-            if soon:
-                pick = max(soon, key=lambda i: rank[i])
-            ready[q].remove(pick)
-            turn.append(pick)
-            done = max(t0, start[pick]) + B_[pick]
-            if q != "A":
-                free[q] = done
-            if K_[pick] == "d":
-                free["D"] = max(free["D"], done) + L_[pick] - DMAT
-                done = free["D"] + DMAT
-            else:
-                done += L_[pick]
-            end = max(end, done)
-            for k, w in gap[pick]:
-                start[k] = max(start[k], done + w)
+            t0 = min(when)
+            q, top, one = when.index(t0), -1e18, 0
+            for i in ready[q]:
+                if rank[i] > top and start[i] <= t0:
+                    top, one = rank[i], i
+            t1, top = t0 + AHEAD * B_[one], top + 300.0
+            for i in ready[q]:
+                if rank[i] > top and start[i] < t1:
+                    top, one = rank[i], i
+            ready[q].remove(one)
+            turn.append(one)
+            t = max(t0, start[one]) + B_[one]
+            free[q] = t if q else 0.0
+            if K_[one] == 2:
+                dfree = max(dfree, t) + L_[one]
+            done[one] = dfree + D_ if K_[one] == 2 else max(dfree, t) if K_[one] == 3 else t + L_[one]
+            when[q] = max(free[q], min([start[i] for i in ready[q]])) if ready[q] else 1e18
+            for k in succ[one]:
                 left[k] -= 1
                 if not left[k]:
+                    start[k] = max([t0] + [done[j] + w for j, w in G_[k]])
                     ready[Q_[k]].append(k)
-        return end, turn
+                    when[Q_[k]] = min(when[Q_[k]], max(free[Q_[k]], start[k]))
+        return turn
+
+    def times(turn, m):
+        busy, late, pred, dmat = m
+        done, start, why = [0.0] * n_, [0.0] * n_, [-1] * n_
+        free, last, dfree, dlast, end, tip = [0.0] * 6, [-1] * 6, 0.0, -1, 0.0, 0
+        for i in turn:
+            q = Q_[i]
+            t, w = free[q], last[q]
+            for j, g_ in pred[i]:
+                if done[j] + g_ > t:
+                    t, w = done[j] + g_, j
+            start[i] = t
+            t += busy[i]
+            if q:
+                free[q], last[q] = t, i
+            if K_[i] > 1:
+                if dfree > t:
+                    t, w = dfree, dlast
+                if K_[i] == 2:
+                    t += late[i]
+                    dfree, dlast = t, i
+                    t += dmat
+            else:
+                t += late[i]
+            done[i], why[i] = t, w
+            if t > end:
+                end, tip = t, i
+        return end, start, why, tip
+
+    def moved(turn, u, x, up):
+        a, b = turn.index(u), turn.index(x)
+        part, go = turn[a:b + 1], {x if up else u}
+        for i in (part[::-1] if up else part):
+            if i not in go and any(k in go for k in (succ[i] if up else nodes[i]["dep"])):
+                go.add(i)
+        if (u if up else x) in go:
+            return None
+        one, two = [i for i in part if i in go], [i for i in part if i not in go]
+        return turn[:a] + (one + two if up else two + one) + turn[b + 1:]
 
     if not FOUND:
         rs = np.random.RandomState(SEED)
-        best, rank = lay_out(level)[0], np.array(level)
-        pred = [[] for _ in nodes]
-        for i in range(len(nodes)):
-            for k, w in gap[i]:
-                pred[k].append((i, w + L_[i]))
-
-        def backwards(turn):
-            place = {i: n for n, i in enumerate(turn)}
-            left, start, free, out = [len(x) for x in succ], list(L_), {q: 0.0 for q in "VSPQYA"}, [0.0] * len(nodes)
-            ready = {q: [i for i in range(len(nodes)) if not left[i] and Q_[i] == q] for q in free}
-            for _ in nodes:
-                t0, q = min((max(free[q], min(start[i] for i in ready[q])), q) for q in ready if ready[q])
-                pick = max((i for i in ready[q] if start[i] <= t0 + BACK), key=lambda i: place[i])
-                ready[q].remove(pick)
-                out[pick] = max(t0, start[pick]) + B_[pick]
-                if q != "A":
-                    free[q] = out[pick]
-                for k, w in pred[pick]:
-                    start[k] = max(start[k], out[pick] + w)
-                    left[k] -= 1
-                    if not left[k]:
-                        ready[Q_[k]].append(k)
-            return out
+        like = {}
+        for i, x in enumerate(nodes):
+            like.setdefault(x["tag"], []).append(i)
+        rank, turn = np.array(level), lay_out(level)
+        best = sum(times(turn, m)[0] for m in models)
+        for n in range(SHIFTS):
+            a, new = rs.randint(n_), rank.copy()
+            some = range(a, min(n_, a + rs.randint(1, rs.choice([3, 12, 40]))))
+            new[[j for i in some for j in (like[nodes[i]["tag"]] if n & 1 else [i])]] += rs.choice([-1.0, 1.0]) * rs.choice([300.0, 1000.0, 3000.0, 8000.0])
+            tn = lay_out(new.tolist())
+            c = sum(times(tn, m)[0] for m in models)
+            if c <= best:
+                best, rank, turn = c, new, tn
+        now = [times(turn, m) for m in models]
+        cost = best = sum(x[0] for x in now)
+        keep = turn
         for n in range(TRIES):
-            if n % 100 == 0:
-                new = backwards(lay_out(rank.tolist())[1])
-                for _ in range(4):
-                    t, tn = lay_out(new)
-                    if t < best:
-                        best, rank = t, np.array(new)
-                    new = backwards(tn)
-            a = rs.randint(0, len(nodes))
-            new = rank.copy()
-            new[a:a + rs.randint(1, 40)] += rs.choice([-1.0, 1.0]) * rs.choice([300.0, 1000.0, 3000.0, 8000.0])
-            t = lay_out(new.tolist())[0]
-            if t <= best:
-                best, rank = t, new
-        FOUND.extend([rank.tolist(), best])
-    turn = lay_out(FOUND[0])[1]
+            if n % 50 == 0:
+                turn = sorted(turn, key=lambda i: now[0][1][i])
+                now = [times(turn, m) for m in models]
+                cost = sum(x[0] for x in now)
+            _, _, why, x = now[rs.randint(len(now))]
+            pairs = []
+            while why[x] >= 0:
+                if why[x] not in nodes[x]["dep"]:
+                    pairs.append((why[x], x))
+                x = why[x]
+            u, x = pairs[rs.randint(len(pairs))]
+            up = rs.randint(2)
+            mates = [i for i in turn if Q_[i] == Q_[x]]
+            if Q_[u] == Q_[x] and rs.randint(2):
+                if up:
+                    u = mates[max(0, mates.index(u) - rs.randint(1, 6))]
+                else:
+                    x = mates[min(len(mates) - 1, mates.index(x) + rs.randint(1, 6))]
+            new = moved(turn, u, x, up)
+            if new:
+                then = [times(new, m) for m in models]
+                c = sum(y[0] for y in then)
+                if c <= cost + HEAT * (1.0 - n / TRIES) * rs.exponential():
+                    turn, now, cost = new, then, c
+                    if c < best:
+                        best, keep = c, new
+        FOUND.extend([keep, best / len(models)])
+    place = {i: n for n, i in enumerate(FOUND[0])}
+    left, ready, turn = list(deps), {i for i in range(n_) if not deps[i]}, []
+    while ready:
+        i = min(ready, key=place.get)
+        ready.remove(i)
+        turn.append(i)
+        for k in succ[i]:
+            left[k] -= 1
+            if not left[k]:
+                ready.add(k)
     count = {s: 0 for s in SEMAPHORES}
     seen = {q: {} for q in eng}
-    mark = {}
+    mark, known = {}, {}
 
     def wait(q, sem, val):
         if seen[q].get(sem, 0) < val:
@@ -703,21 +753,27 @@ def rank_program(g, core, T, topo):
         if x["kind"] != "a":
             need = {}
             for j, hard in x["dep"].items():
-                if hard and nodes[j]["kind"] != "r":
-                    need[mark[j][0]] = max(need.get(mark[j][0], 0), mark[j][1])
-            for sem in need:
-                wait(q, sem, need[sem])
+                if hard and nodes[j]["kind"] != "r" and mark[j][1] > need.get(mark[j][0], (0, 0))[0]:
+                    need[mark[j][0]] = (mark[j][1], j)
+            for sem, (val, j) in sorted(need.items(), key=lambda e: -mark[e[1][1]][2]):
+                wait(q, sem, val)
+                for s2, v2 in known.get(j, {}).items():
+                    seen[q][s2] = max(seen[q].get(s2, 0), v2)
+            known[i] = dict(seen[q])
             inst = x["call"]()
             if x["kind"] != "r":
                 inst.then_inc(T.sem[x["sem"] or q], x["n"])
         sem = "sent" if x["kind"] == "r" else x["sem"] or q
         count[sem] += x["n"]
-        mark[i] = (sem, count[sem])
+        mark[i] = (sem, count[sem], len(mark))
+    seen["Q"] = {}
     for s in SEMAPHORES:
         if count[s]:
             wait("Q", s, count[s])
 
 
-FOUND, SEED, TRIES, GATE = [], 1, 1500, False
-BACK = 800.0
-AHEAD, MARGIN, UP, ORD, HS, LQ = 0.4, 300.0, 0.0, (0, 1, 2, 3), 11, "VVV"
+FOUND, SEED, TRIES = [], 1, 5000
+HEAT, CHUNK, EB, EARLY, SHIFTS, AHEAD = 50.0, 900, "BAMB", 3, 4000, 0.4
+ORD, LQ = (3, 0, 1, 2), ("VSS", "VSV", "VSS", "SS")
+PARTS = ((768, 768),) * 4
+FILL = {"TB": "S", "W": "VVVS", "HW": "SSSSSQQQQQVVVVVV"}

@@ -5,36 +5,37 @@ from concourse.mybir import AluOpType, ActivationFunctionType
 N, RO, C = 4, 3, 1536
 F32, BF, F16, I32, U16 = "float32", "bfloat16", "float16", "int32", "uint16"
 XS, CS, WS = 1544, 1568, 2560
-ROUND, HALF = 12582912.0, 1536.0
+GX = 4 * C
+HALF = 1536.0
 
 BUFS = {
-    "wraw": (I32, [4096]), "A": (F32, [4240]), "hraw": (I32, [1024]), "HW": (BF, [16384]), "ZB": (BF, [1536]), "T3": (BF, [4096]),
-    "TB": (F32, [1024]), "srn": (I32, [2, 256]), "srd": (F32, [8, 64]), "nxn": (I32, [64]), "nxf": (F32, [2, 64]), "curi": (I32, [32]),
+    "wraw": (I32, [4096]), "A": (F32, [4240]), "hraw": (I32, [1024]), "HW": (BF, [16384]), "ZB": (BF, [1536]),
+    "TB": (F32, [1024]), "srn": (I32, [2, 256]), "srd": (F32, [9, 64]), "nxn": (I32, [64]), "curi": (I32, [32]),
     "mg": (I32, [64]), "mo": (I32, [64]), "mq": (I32, [2, 64]), "mf": (F32, [3, 64]), "mlf": (F32, [66]), "mlh": (F32, [66]),
     "mx": (U16, [4, 88]), "mi": (I32, [4, 86]), "ml": (I32, [4, 66]), "mlo": (I32, [4, 64]), "mrole": (BF, [3, 4, 64]),
     "pi": (I32, [8]), "pc": (F32, [128]), "X": (F32, [144]), "i16": (F32, [2, 128]), "NI": (F32, [400]),
     "Mw": (F32, [144]), "M4": (F32, [144]), "ONE": (F32, [128]), "M16": (F32, [128]), "TR": (F32, [3, 128]), "ON8": (F32, [128]),
     "WA": (BF, [4, 144]), "WL": (BF, [1, 144]), "TS": (BF, [2, 128]), "sg": (BF, [2, 104]), "WH": (BF, [4, 144]), "WZ": (BF, [2, 144]), "Wn": (F32, [2, 144]), "W4f": (F32, [2, 144]),
-    "W4": (BF, [4, 144]), "WB": (BF, [2, 144]), "ME": (BF, [144]), "WK": (BF, [12, 128]), "WE": (BF, [4, 128]), "ONn": (BF, [128]), "ID": (BF, [2, 128]),
-    "slc": (F16, [32]), "k24": (F16, [32]), "r1": (F16, [128]), "ck": (F16, [72]), "ck0": (F16, [96]), "Cc": (F32, [128]),
-    "pat4": (BF, [128]), "pat7": (BF, [84]), "pat3": (BF, [72]), "pat5": (F32, [66]), "pat16": (BF, [128]), "pat9": (BF, [72]),
+    "W4": (BF, [4, 144]), "WB": (BF, [2, 144]), "ME": (BF, [144]), "WK": (BF, [12, 128]), "WE": (BF, [4, 128]), "ONn": (BF, [128]), "ID": (BF, [5, 128]), "cu": (F16, [96]),
+    "slc": (F16, [32]), "k24": (F16, [32]), "r1": (F16, [128]), "ck": (BF, [72]), "ck0": (BF, [96]), "Cc": (F32, [128]),
+    "pat4": (BF, [128]), "pat7": (BF, [84]), "pat5": (F32, [66]), "pat16": (BF, [128]), "pat9": (BF, [72]),
     "sc7": (F32, [96]), "repf": (F32, [6]), "repl": (U16, [6]), "l43": (U16, [8]), "cap": (BF, [512]), "top": (F32, [96]),
     "neg8": (BF, [128]), "on1": (BF, [480]), "qrt": (F32, [128]), "Dc": (F32, [8]),
     "hc": (U16, [8]), "sl": (U16, [32]), "RG": (F32, [512]), "RS": (F32, [128]), "oh": (F32, [128]),
     "pr": (F32, [2, 128]), "ps": (F32, [2, 128]), "rq": (U16, [32]), "fld": (F16, [4, 32]),
     "G3": (BF, [512]), "Gb": (BF, [512]), "G2": (BF, [512]), "F": (F16, [520]), "vv": (F16, [512]), "nf": (BF, [520]),
-    "off": (U16, [32]), "W": (BF, [4 * WS]), "dl": (F32, [4, 104]), "aa": (F32, [4, 96]),
-    "pk": (I32, [96]), "pk2": (I32, [84]), "pk3": (F32, [84]), "asnd": (U16, [3, 3, 88]), "arcv": (U16, [3, 3, 88]),
+    "off": (U16, [32]), "Fc": (F32, [1]), "W": (BF, [4 * WS]), "dl": (F32, [4, 104]), "aa": (F32, [4, 96]),
+    "pk": (I32, [96]), "pk2": (I32, [84]), "pk3": (F32, [84]), "asnd": (U16, [3, 3, 96]), "arcv": (U16, [3, 3, 96]),
     "ui": (I32, [84]), "ua": (I32, [84]), "uh": (BF, [84]), "us": (F32, [84]), "hl": (U16, [4, 96]),
-    "G": (BF, [2 * C]), "rsnd": (U16, [3, 3, 72]), "rrcv": (U16, [3, 3, 72]), "ri": (I32, [72]), "rh": (BF, [72]), "rs": (F32, [72]),
-    "Ww": (I32, [96]), "W2": (I32, [400]), "l1": (U16, [4, 96]), "l2": (U16, [4, 96]),
+    "G": (BF, [GX + 1152]), "rsnd": (U16, [3, 3, 72]), "rrcv": (U16, [3, 3, 72]), "rh": (BF, [72]), "rs": (F32, [72]),
+    "W2": (I32, [400]), "l1": (U16, [4, 96]), "l2": (U16, [4, 96]),
     "xs": (F32, [2 * XS]), "ct": (BF, [2 * CS]), "d1": (BF, [2, C]), "z": (BF, [2, C]), "Pz": (F32, [2, 136]), "T1": (F32, [2, 128]), "T2": (F32, [2, 128]),
     "nh": (BF, [480]), "DS": (BF, [480]), "ch": (BF, [512]), "lt": (BF, [512]), "eq": (BF, [512]),
     "bi": (I32, [32]), "bj": (I32, [32]), "bh": (BF, [32]), "bl": (U16, [32]), "S": (F32, [136]), "key": (F32, [128]), "mk": (F32, [128]),
     "s0": (F32, [32]), "s1": (F32, [32]), "s2": (F32, [32]), "s3": (F32, [32]), "s4": (F32, [32]),
     "p2": (F16, [128]), "se": (F16, [128]), "cl": (U16, [3, 8]), "m1": (BF, [128]), "m2": (BF, [128]), "bg": (BF, [128]), "ys": (F32, [128]),
     "m3": (F32, [128]), "bw": (F32, [128]), "b0": (F32, [128]), "b1": (F32, [136]), "E3": (BF, [8, 16, 9]), "cn": (F32, [72]), "co": (F32, [8]),
-    "yto": (F32, [384]), "ybo": (F32, [384]), "ywo": (F32, [96]), "kd": (F32, [128]),
+    "yto": (F32, [384]), "ybo": (F32, [384]), "ywo": (F32, [96]),
 }
 BANKS = ["pA", "pB", "pK", "pM", "pZ", "pC", "pT", "pS"]
 PLACE, SCRATCH = {}, {}
@@ -46,10 +47,11 @@ for _k, (_d, _s) in BUFS.items():
     else:
         SCRATCH[_k] = ("sbuf", [128] + _s, _d)
 SCRATCH.update({k: ("psum", [128, 512], F32) for k in BANKS})
-SEMAPHORES = (["V", "S", "P", "Q", "sent", "rm", "lm", "ls", "lc", "lh", "tb", "t3a", "hw0", "hz", "oy0", "oy1", "oy2"]
-              + ["%s%d" % (k, i) for k in ("wz", "ra0", "ra1", "ra2", "rr0", "rr1", "rr2") for i in range(RO)] + ["lw%d" % i for i in range(8)])
+SEMAPHORES = (["V", "S", "P", "Q", "sent", "rm", "lm", "ls", "lc", "lh", "tb", "t3a", "hw0", "oy0", "oy1", "oy2"]
+              + ["%s%d" % (k, i) for k in ("wz", "wy", "ra0", "ra1", "ra2", "rr0", "rr1", "rr2") for i in range(RO)] + ["lw%d" % i for i in range(8)])
 ALL = slice(None)
-MODELS = [dict(c=1.04, g=1.62, s=3.95, p=0.52, byte=0.005, rows=250.0, same=30.0, wake=90.0, dma=2000.0, far=2800.0, call=300.0)]
+MODELS = [dict(c=1.04, g=1.62, s=3.95, p=0.52, byte=0.0045, rows=250.0, same=30.0, wake=90.0, dma=2000.0, far=2800.0, call=300.0),
+          dict(c=0.88, g=1.37, s=3.3, p=0.44, byte=0.003, rows=300.0, same=80.0, wake=200.0, dma=2200.0, far=3300.0, call=600.0)]
 
 
 def rank_program(g, core, T, topo):
@@ -58,7 +60,7 @@ def rank_program(g, core, T, topo):
         return
     Op, Act = AluOpType, ActivationFunctionType
     eng = {"V": g.vector, "S": g.scalar, "P": g.tensor, "Q": g, "Y": g.sync}
-    nodes, hist, bysem, tag = [], {}, {}, ["", 0]
+    nodes, hist, bysem, tag, table = [], {}, {}, ["", 0], []
 
     def v(name, *idx, p=ALL):
         if name in PLACE:
@@ -131,12 +133,18 @@ def rank_program(g, core, T, topo):
 
     def act(o, i, f, bias=0.0, scale=1.0):
         run("S", o, [i, bias, scale], lambda: g.scalar.activation(ap(o), ap(i), f, bias=ap(bias), scale=ap(scale)), 1.0, False)
+        if f is Act.Sigmoid and not table:
+            table.append(nodes[-1])
+            nodes[-1]["busy"] = (1300.0,) + nodes[-1]["busy"][1:]
 
     def iota(o, pat, base, cm):
         node("Q", "c", [o], [], lambda: g.iota(ap(o), pat, base, cm, allow_small_or_imprecise_dtypes=True), (130.0, 2 * o[3], "c"))
 
-    def pick(o, i, step, op):
-        node("Q", "c", [o], [i], lambda: g.affine_select(ap(o), ap(i), [[step, 128]], op, 0.0, 0, -step), (170.0, 2 * o[3], "c"))
+    def pick(o, i, step, op, c=0.0):
+        node("Q", "c", [o], [i], lambda: g.affine_select(ap(o), ap(i), [[step, 128]], op, c, 0, -step), (170.0, 2 * o[3], "c"))
+
+    def put(o, i, r, c):
+        node("Q", "c", [o], [i], lambda: g.affine_select(ap(o), ap(i), [[-16, 8], [0, 16]], Op.not_equal, c, -r, 1), (170.0, 2 * o[3], "c"))
 
     def fill(q, o, c):
         if q == "V":
@@ -160,7 +168,9 @@ def rank_program(g, core, T, topo):
             return inst
         node("P", "c", [items[0][0]], [y for x in items for y in x[1:]], call, (0.0, sum(cost), "p"))
 
-    def dma(q, sem, o, i, nbytes=0, gate=None, after=()):
+    def dma(q, sem, o, i, gate=None, after=()):
+        x = o if isinstance(o, tuple) else i
+        nbytes = x[3] * bin(x[1][0][3]).count("1") * (2 if x[4] else 4)
         node(q, "d", [o], [i, gate], lambda: eng[q].dma_start(ap(o), ap(i)), (100.0, 0, "c"), (nbytes, "byte"), sem, 16, after)
 
     peer = [T.cores[(me + 1 + s) % N] for s in range(3)]
@@ -205,17 +215,16 @@ def rank_program(g, core, T, topo):
 
     dma("Y", "lm", v("mg"), T.gst[:])
     dma("S", "lm", v("mo"), T.gln[:])
-    dma("Y", "ls", v("srn", 0), T.sens[:], 1 << 17)
-    dma("S", "ls", v("srn", 1), T.rel[:], 1 << 17)
+    dma("Y", "ls", v("srn", 0), T.sens[:])
+    dma("S", "ls", v("srn", 1), T.rel[:])
     dma("Y", "ls", v("nxn"), T.nxt[:])
     ms(v("curi"), 0)
     dma("S", "lc", v("curi", p=rows(0)), T.cur[:])
     ms(v("ZB"), 0.0)
     iota(v("pi", sl(0, 1)), [[0, 1]], 0, 1)
     iota(v("X"), [[1, 144]], 0, 0)
-    iota(v("nxf", 1), [[1, 64]], 0, 64)
     iota(v("i16", 0), [[0, 8], [1, 16]], 0, 0)
-    iota(v("i16", 1), [[1, 8], [0, 16]], 0, 0)
+    iota(v("i16", 1), [[16, 8], [0, 16]], 0, 0)
 
     ms(v("mlf"), 0.0)
     ms(v("pat5"), 32.0); ms(v("pat5", sl(0, 66, 3)), 0.0)
@@ -232,29 +241,27 @@ def rank_program(g, core, T, topo):
     tw = send_all("rm", v("mx", 3, sl(0, 86)), [v("mx", 2 - s, sl(0, 86)) for s in range(3)])
     arrive("rm", 3 * whole, v("mx", sl(0, 3)), tw)
 
-    for k, (sh, an) in enumerate(((0, 15), (0, 3), (2, 3), (0, 112), (4, 7), (0, 127))):
+    for k, (sh, an) in enumerate(((0, 15), (0, 3), (2, 3), (0, 112))):
         ts(v("pi", sl(k + 1, 1)), v("pi", sl(0, 1)), sh, Op.logical_shift_right, an, Op.bitwise_and)
-    P16, P4, PA, G16, PG, PP = cols(v("pi", sl(1, 6)), 0.0, Op.add)
+    P16, P4, PA, G16 = cols(v("pi", sl(1, 4)), 0.0, Op.add)
     QA = cols(v("X", sl(0, 4)), PA, Op.is_equal)
     Q4 = newcol(4)
     ts(Q4, v("X", sl(0, 4)), P4, Op.is_equal)
     ts(v("M16"), v("i16", 0), P16, Op.is_equal)
-    ts(v("ONE"), v("i16", 1), PG, Op.is_equal)
+    ts(v("ONE"), v("i16", 1), G16, Op.is_equal)
     Q16 = [v("M16", sl(i, 1)) for i in range(16)]
     ts(v("Mw"), v("X"), colts(G16, 15.0, Op.add), Op.is_equal)
     ts(v("M4"), v("X"), colts(G16, P4, Op.add, 12.0, Op.add), Op.is_equal)
 
     def weights(o, master, scale): act(o, v(master), Act.Identity, scale=scale)
 
-    fill(FILL["TB"], v("TB"), 0.0)
+    iota(v("TB"), [[1, 1024]], 0, 0)
     for t in range(2):
         for a in range(4):
             cp(v("srd", 4 * t + a), v("srn", t, slice(a, 256, 4)))
-    cp(v("nxf", 0), v("nxn"))
-    ts(v("nxf", 1), v("nxf", 1), colts(G16, 64.0, Op.mult), Op.subtract)
-    for r in range(10):
-        dma("YS"[r & 1], "tb", v("TB", p=rows(r)), v("srd", r) if r < 8 else v("nxf", r - 8))
-    dma("Y", "lh", v("hraw"), T.heap[:], 1 << 19, None, bysem["tb"][::2])
+    cp(v("srd", 8), v("nxn"))
+    for r in range(9):
+        dma("Y", "tb", v("TB", p=rows(r)), v("srd", r))
     for i in range(2):
         weights(v("W4f", i), "M4", QA[i])
         weights(v("Wn", i), "Mw", Q16[8 + i])
@@ -272,6 +279,8 @@ def rank_program(g, core, T, topo):
             cp(v("sl"), v("pK", sl(384, 32)))
             act(v("RG"), ind(v("TB"), v("sl")), Act.Copy)
             mm([(RC0, wide4("W4f", 1, b), v("RG", slice(b, 512, 4))) for b in range(4)])
+
+    def follow(more):
         mm([(RC1, wide("Wn", 9, 1), v("RS"))] + [(RC1, wide("Wn", b, 0), v("RG", slice(b, 512, 4))) for b in range(4 * more)])
 
     chain(True)
@@ -279,7 +288,7 @@ def rank_program(g, core, T, topo):
     LEN = colts(PA, 2.0, Op.is_ge)
     EMP = colts(LEN, -129.0, Op.mult, 128.0, Op.add)
     for h in range(4):
-        act(v("T3", sl(1024 * h, 1024)), v("ZB", sl(16, 1024)), Act.Identity, bias=EMP)
+        act(v("HW", sl(1024 * h, 1024)), v("ZB", sl(16, 1024)), Act.Identity, bias=EMP)
     for ss in (sl(3, 1), sl(0, 3)):
         cp(v("mi", ss), v("mx", ss, sl(0, 86)))
         for r in (0, 1, 2):
@@ -295,7 +304,8 @@ def rank_program(g, core, T, topo):
                 ts(v("mlo", ss), v("mi", ss, sl(0, 64)), 255, Op.bitwise_and)
                 ts(v("mrole", r, ss), v("mlo", ss), 128.0, Op.add)
             for s in range(4)[ss]:
-                dma("Y", "t3a", v("T3", sl(1024 * secs[s], 1024), p=rows(4 * r + secs[s])), v("mrole", r, s))
+                dma("Y", "t3a", v("HW", sl(1024 * secs[s], 1024), p=rows(4 * r + secs[s])), v("mrole", r, s))
+    dma("Y", "lh", v("hraw"), T.heap[:], None, bysem["tb"])
     BGB, KAP = colts(EMP, -4096.0, Op.mult), colts(LEN, -1.0, Op.add)
     BG2 = colts(LEN, QA[3], Op.add)
     NF0 = colts(LEN, 129.0, Op.mult, colts(BG2, -129.0, Op.add), Op.add)
@@ -307,85 +317,96 @@ def rank_program(g, core, T, topo):
     pick(v("TR", 2), v("ONE"), 1, Op.is_equal)
     act(v("ID", 0), v("TR", 2), Act.Copy)
     act(v("ID", 1), v("TR", 2), Act.Copy, scale=float(WS))
+    for i, c in enumerate((-4096.0, 256.0, 16.0)):
+        pick(v("ID", i + 2), v("ZB", sl(16, 128)), 1, Op.not_equal, c)
+    ms(v("cu", sl(0, 72)), 160.0 * 4096 / WS); ms(v("cu", sl(72, 24)), -160.0 * 273 / WS)
     iota(v("NI"), [[16, 400]], 0, 1)
     act(v("NI"), v("NI"), Act.Identity, bias=colts(G16, -1.0, Op.mult))
     cp(v("slc"), v("NI", sl(0, 32)))
     ms(v("k24"), -HALF)
-    weights(v("WL", 0), "Mw", LEN)
-    wa = colts(colts(PA, -127.0, Op.mult, 128.0, Op.add), -1.0, Op.max, colts(QA[3], -32767.0, Op.mult), Op.add)
-    for o, c in enumerate(cols(Q4, wa, Op.mult)):
+    weights(v("WL", 0), "Mw", QA[2])
+    wa = colts(colts(PA, -127.0, Op.mult, 128.0, Op.add), -1.0, Op.max, QA[3], Op.add)
+    for o, c in enumerate(cols(Q4, wa, Op.mult, colts(Q16[12], -32768.0, Op.mult), Op.add)):
         weights(v("WA", o), "Mw", c)
     ms(v("dl", ALL, sl(0, 1)), 0.0)
     ms(v("top"), 16383.0)
-    ms(v("sc7"), 0.0)
-    for k in range(7):
-        ms(v("sc7", slice(k, 84, 7)), float(4 ** (k + 1)))
+    ms(v("pat7"), 4.0); ms(v("pat7", sl(0, 84, 7)), 0.0)
+    ms(v("us"), 4.0); ms(v("sc7", sl(84, 12)), 0.0)
+    scan(v("sc7", sl(0, 84)), v("pat7"), v("us"), 0.0, Op.mult, Op.max)
     ts(v("repf"), v("NI", sl(0, 6)), 1.0 / 7, Op.mult, 84.0 - 3.0 / 7, Op.add)
     ts(v("repl"), v("repf"), 95.0, Op.min)
     ms(v("sg", ALL, sl(0, 1)), 0.0)
     for i in range(2):
         act(v("TS", i), v("TR", i), Act.Copy, scale=-16384.0)
-    cp(v("ZB", sl(0, 1)), QA[3])
+    cp(v("ZB", sl(0, 1)), Q16[12])
 
     def zero_w(rd, gate=None):
         for o in range(4):
             pp = slice(o, 128, 4)
-            dma("Y", "wz%d" % rd, v("W", sl(o * WS + 512, C), p=pp), v("ZB", p=pp), 3 << 15, gate)
+            dma("Y", "wz%d" % rd, v("W", sl(o * WS + 512, C), p=pp), v("ZB", p=pp), gate)
+            if o:
+                dma("Y", "wy%d" % rd, v("W", sl(o * WS + 512, C), p=rows(12)), v("ZB", p=rows(12)), gate)
     for o, q in enumerate(FILL["W"]):
         for h in range(2):
             fill(q, v("W", sl(o * WS + 512 + 768 * h, 768)), 0.0)
-    ts(v("W", slice(512, 4 * WS, WS)), v("X", sl(0, 4)), 0.0, Op.mult, QA[3], Op.add)
-    for k, q in enumerate(FILL["HW"]):
-        if q == "D":
-            dma("Y", "hz", v("HW", sl(1024 * k, 1024)), v("ZB", sl(16, 1024)), 1 << 18, v("hraw"))
-        else:
-            for h in range(2 if q == "Q" else 1):
-                fill(q, v("HW", sl(1024 * k + 512 * h, 512 if q == "Q" else 1024)), 0.0)
+    ts(v("W", slice(512, 4 * WS, WS)), v("X", sl(0, 4)), 0.0, Op.mult, Q16[12], Op.add)
+    for k, q in enumerate(FILL["HW"], 4):
+        for h in range(2 if q == "Q" else 1):
+            fill(q, v("HW", sl(1024 * k + 512 * h, 512 if q == "Q" else 1024)), 0.0)
     ts(v("G", sl(0, 1024)), v("hraw"), 1.0 / 256, Op.mult, 160.0 - 127.5 / 256, Op.add)
     ts(v("hraw"), v("hraw"), 255, Op.bitwise_and)
     cp(v("G", sl(1024, 1024)), v("hraw"))
+    weights(v("WH", 0), "Mw", colts(Q16[13], 256.0, Op.mult, Q16[14], Op.add))
+    fill("Q", v("ck0"), -16.0)
     act(v("G", sl(2048, 1024)), v("G", sl(1024, 1024)), Act.Identity, bias=160.0 - 7.5 / 16, scale=1.0 / 16)
-    for r in range(3):
-        dma("Y", "hw0", v("HW", p=rows(r)), v("G", sl(1024 * r, 1024)), 1 << 18)
-    h0, h1, h2 = cols(v("M16", sl(0, 3)), 4096.0, Op.mult)
-    for i, c in enumerate((colts(Q16[0], 256.0, Op.mult, Q16[1], Op.add), h0, h2, colts(Q16[2], -65536.0, Op.mult, h1, Op.add))):
-        weights(v("WH", i), "Mw", c)
-    ms(v("ck"), -272.0); ms(v("ck", slice(2, 72, 3)), 4080.0); ms(v("ck0"), -16.0)
+    h0, h1, h2 = cols(v("M16", sl(13, 3)), 4096.0, Op.mult)
+    for i, c in enumerate((h0, h2, colts(Q16[15], -65536.0, Op.mult, h1, Op.add))):
+        weights(v("WH", i + 1), "Mw", c)
+    fill("Q", v("ck"), -272.0); fill("Q", v("ck", slice(2, 72, 3)), 4080.0)
     act(v("WZ", 0), v("Mw"), Act.Copy)
     act(v("WZ", 1), v("Mw"), Act.Copy, scale=-1.0 / 16)
-    ms(v("pat7"), 4.0); ms(v("pat7", sl(0, 84, 7)), 0.0)
-    ms(v("pat3"), 16.0); ms(v("pat3", sl(0, 72, 3)), 0.0)
     act(v("ON8"), v("ONE"), Act.Copy, scale=8.0)
     act(v("ONn"), v("ONE"), Act.Copy, scale=-1.0)
     for a in range(4):
         weights(v("W4", a), "M4", QA[a])
-        weights(v("WE", a), "ONE", Q16[8 + a])
+        put(v("WE", a), v("ZB", sl(16, 128)), 8 + a, 1.0)
     ts(v("ME"), v("X"), colts(colts(P4, 4.0, Op.mult, G16, Op.add), 3.0, Op.add), Op.is_equal, QA[2], Op.mult)
     ts(v("r1"), v("X", sl(0, 128)), 4.0, Op.mult, -508.0, Op.add)
     weights(v("WB", 0), "M4", colts(QA[1], -96.0, Op.mult, colts(QA[0], 120.0, Op.mult, QA[2], Op.add), Op.add))
     weights(v("WB", 1), "M4", colts(QA[0], 96.0, Op.mult, colts(QA[2], 1.0 / 16, Op.mult), Op.add))
-    for k, c in enumerate(cols(v("M16", sl(0, 4)), float(C), Op.mult)):
-        weights(v("WK", k), "ONE", colts(c, Q16[8 + k], Op.add))
-        weights(v("WK", 4 + k), "ONE", Q16[4 + k])
-        weights(v("WK", 8 + k), "ONE", Q16[12 + k])
+    fill("Q", v("WK", sl(0, 4)), 0.0)
+    for k in range(4):
+        put(v("WK", k), v("WK", k), k, float(C))
+        put(v("WK", k), v("WK", k), 8 + k, 1.0)
+        put(v("WK", 4 + k), v("ZB", sl(16, 128)), 4 + k, 1.0)
+        put(v("WK", 8 + k), v("ZB", sl(16, 128)), 12 + k, 1.0)
     for k in range(2):
-        ms(v("xs", sl(k * XS, 8)), 0.0)
-        ms(v("ct", sl(k * CS, 32)), 0.0)
+        fill("Q", v("xs", sl(k * XS, 8)), 0.0)
+        fill("Q", v("ct", sl(k * CS, 32)), 0.0)
     PCH, PPC = colts(P16, 160.0, Op.add), colts(P16, HALF, Op.add)
     BLT = colts(P16, -1000.0, Op.mult, -160500.0, Op.add)
     act(v("neg8"), v("ZB", sl(16, 128)), Act.Identity, bias=colts(P16, 12.0, Op.is_lt, -8.0, Op.mult))
-    fill("S", v("on1"), 1.0); fill("S", v("qrt"), 0.25)
-    ms(v("Cc"), 1.5 / 128); ms(v("Cc", slice(1, 128, 4)), 2.0 / 128); ms(v("Cc", slice(3, 128, 4)), 0.0)
-    ms(v("pat16"), 1.0); ms(v("pat16", sl(0, 128, 16)), 0.0)
-    ms(v("pat9"), 1.0); ms(v("pat9", sl(0, 72, 9)), 0.0); ms(v("pat9", slice(8, 72, 9)), 8192.0)
+    act(v("on1"), v("ZB", sl(16, 480)), Act.Sigmoid, bias=200.0)
+    pick(v("qrt"), v("X", sl(0, 128)), 0, Op.not_equal, 0.25)
+    for a, c in enumerate((3, 5, 6, 6)):
+        iota(v("Cc", slice(a, 128, 4)), [[6, 32]], c, 0)
+    fill("Q", v("pat16"), 1.0); fill("Q", v("pat16", sl(0, 128, 16)), 0.0)
+    fill("Q", v("pat9"), 1.0); fill("Q", v("pat9", sl(0, 72, 9)), 0.0); fill("Q", v("pat9", slice(8, 72, 9)), 8192.0)
     act(v("Dc"), v("NI", sl(0, 8)), Act.Identity, bias=4104.0)
     ts(v("l43"), v("NI", sl(0, 8)), P4, Op.subtract, 3.0, Op.add)
-    ms(v("Pz", ALL, sl(0, 1)), 0.0); ms(v("S", sl(0, 1)), 0.0); ms(v("b1", sl(0, 1)), 0.0)
-    ms(v("E3"), 0.0); ms(v("W2", sl(384, 16)), -1)
-    ms(v("A", sl(0, 1)), -9.0); fill("S", v("A", sl(4097, 143)), -9.0)
-    for h in range(8):
-        dma("Y", "lw%d" % h, v("wraw", sl(512 * h, 512)), T.wpos[:, sl(512 * h, 512)], 1 << 18, None, bysem["t3a" if h < EARLY else "hw0"])
-        ts(v("A", sl(1 + 512 * h, 512)), v("wraw", sl(512 * h, 512)), 0.25, Op.max)
+    for x in (v("Pz", ALL, sl(0, 1)), v("S", sl(0, 1)), v("b1", sl(0, 1))) + tuple(v("E3", sl(2 * i, 2)) for i in range(4)):
+        fill("Q", x, 0.0)
+    fill("Q", v("W2", sl(384, 16)), -1.0)
+    fill("Q", v("A", sl(0, 1)), -9.0); fill("Q", v("A", sl(4097, 143)), -9.0)
+    def tables():
+        for r in range(3):
+            dma("Y", "hw0", v("HW", p=rows(13 + r)), v("G", sl(1024 * r, 1024)))
+        a = 0
+        for h, (n, when) in enumerate(LOADS):
+            dma("Y", "lw%d" % h, v("wraw", sl(512 * a, 512 * n)), T.wpos[:, sl(512 * a, 512 * n)], None, bysem[when])
+            for k in range(a, a + n):
+                ts(v("A", sl(1 + 512 * k, 512)), v("wraw", sl(512 * k, 512)), 0.25, Op.max)
+            a += n
 
     def select(i, src):
         tt(v("pr", i), src, v("oh"), Op.mult)
@@ -413,8 +434,10 @@ def rank_program(g, core, T, topo):
         tt(v("m3"), ind(v("NI"), v("cl", 1)), v("ys"), Op.is_equal)
         tt(v("bw"), ind(v("W2"), v("cl", 1)), v("m3"), Op.mult)
         mm([(xb, v("ON8"), v("bw"))])
-        act(xb, xb, Act.Relu, bias=1.0, scale=0.125)
-        if rd < RO - 1:
+        if rd == RO - 1:
+            ts(v("ybo", sl(128 * rd, 128)), xb, 0.125, Op.mult, -1.0, Op.max)
+        else:
+            act(xb, xb, Act.Relu, bias=1.0, scale=0.125)
             tt(v("b0"), xb, v("M16"), Op.mult)
             scan(v("b1", sl(1, 128)), v("pat16"), v("b0"), 0.0, Op.mult, Op.add)
             tt(v("E3", ALL, ALL, 7), xb, v("b1", sl(0, 128)), Op.is_equal)
@@ -426,25 +449,31 @@ def rank_program(g, core, T, topo):
             tt(v("co"), v("cn", slice(8, 72, 9)), v("Dc"), Op.min)
             cp(v("cl", 2), v("co"))
             cp(ind(v("A"), v("cl", 2)), v("qrt"))
-        act(v("ybo", sl(128 * rd, 128)), xb, Act.Identity, bias=-1.0)
+            act(v("ybo", sl(128 * rd, 128)), xb, Act.Identity, bias=-1.0)
 
-    o32 = v("pS", sl(0, 32))
     twa, twin = {}, {}
 
     def expand(rd):
         rq = select(0, RC0)
         cp(v("rq"), rq)
-        act(v("G3"), ind(v("T3"), v("rq")), Act.Copy)
         ts(v("fld", 0), rq, 1.0 / 1024, Op.mult, HALF - 511.5 / 1024, Op.add)
-        act(v("Gb"), v("G3"), Act.Identity, bias=BGB, scale=4096.0)
-        scan(v("F", sl(1, 512)), v("G3"), v("cap"), 512.0, Op.add, Op.min)
-        act(v("G2"), v("G3"), Act.Identity, bias=BG2, scale=KAP)
-        mm([(o32, v("ID", 0), v("slc")), (o32, v("ID", 1), v("k24")), (o32, v("ID", 1), v("fld", 0))], last=False)
-        scan(v("vv"), v("F", sl(0, 512)), v("Gb"), 0.0, Op.max, Op.min)
-        mm([(o32, wide("WL", u, 0), v("vv", slice(u, 512, 16))) for u in range(16)], first=False)
-        scan(v("nf", sl(1, 512)), v("Gb"), v("G2"), NF0, Op.add, Op.min)
-        cp(v("off"), o32)
-        tt(ind(v("W"), v("off")), v("G3"), v("nf", sl(0, 512)), Op.add)
+        a = 0
+        for n in CUT:
+            x, c = sl(a, n), sl(a // 16, n // 16)
+            oc = v("pM" if a else "pS", c)
+            act(v("G3", x), ind(v("HW", sl(0, 4096)), v("rq", c)), Act.Copy)
+            act(v("Gb", x), v("G3", x), Act.Identity, bias=BGB, scale=4096.0)
+            scan(v("F", sl(a + 1, n)), v("G3", x), v("cap", x), v("Fc") if a else 512.0, Op.add, Op.min)
+            if a + n < 512:
+                cp(v("Fc"), v("F", sl(a + n, 1)))
+            act(v("G2", x), v("G3", x), Act.Identity, bias=BG2, scale=KAP)
+            mm([(oc, v("ID", 0), v("slc", c)), (oc, v("ID", 1), v("k24", c)), (oc, v("ID", 1), v("fld", 0, c))], last=False)
+            scan(v("vv", x), v("F", x), v("Gb", x), 0.0, Op.max, Op.min)
+            mm([(oc, wide("WL", u, 0), v("vv", slice(a + u, a + n, 16))) for u in range(16)], first=False)
+            scan(v("nf", sl(a + 1, n)), v("Gb", x), v("G2", x), v("nf", sl(a, 1)) if a else NF0, Op.add, Op.min)
+            cp(v("off", c), oc)
+            tt(ind(v("W"), v("off", c)), v("G3", x), v("nf", x), Op.add)
+            a += n
         for n, s in enumerate(ORD):
             o, out = secs[s], v("p" + EB[n], sl(0, 96))
             mm([(out, wide("WA", u, o), v("W", sl(o * WS + 512 + u, C - u, 16))) for u in range(16)])
@@ -454,19 +483,24 @@ def rank_program(g, core, T, topo):
             scan(v("aa", s), out, v("top"), 0.0, Op.add, Op.min)
             if s == 3:
                 cp(v("hl", 3), v("aa", 3))
+                continue
+            w = 96 if (rd, s) == PLAIN else 84
+            if w == 96:
+                cp(v("asnd", rd, s), v("aa", s))
             else:
                 tt(v("pk"), ind(v("aa", s), v("repl")), v("sc7"), Op.mult)
                 ts(v("pk2"), v("pk", sl(0, 84)), 49152, Op.bitwise_and)
                 tt(v("pk3"), v("aa", s, sl(0, 84)), v("pk2"), Op.add)
                 cp(v("asnd", rd, s, sl(0, 84)), v("pk3"))
-                twa[2 - s] = send1(s, "ra%d%d" % (2 - s, rd), v("asnd", rd, s, sl(0, 84)), v("arcv", rd, 2 - s, sl(0, 84)))
+            twa[2 - s] = send1(s, "ra%d%d" % (2 - s, rd), v("asnd", rd, s, sl(0, w)), v("arcv", rd, 2 - s, sl(0, w)))
 
     def ends():
         mm([(v("pS", sl(32, 32)), wide("WL", u, 0), v("G3", slice(u, 512, 16))) for u in range(16)])
         ts(v("s0"), v("fld", 0), -float(WS), Op.mult, HALF * WS - 512, Op.add)
-        tt(v("s1"), o32, v("s0"), Op.add)
+        cp(v("s3"), v("off"))
+        tt(v("s1"), v("s3"), v("s0"), Op.add)
         tt(v("s2"), v("pS", sl(32, 32)), v("s1"), Op.add)
-        ts(v("s3"), v("s2"), 7.0, Op.add, C - 1.0, Op.min)
+        ts(v("s3"), v("s2"), 3.0, Op.add, C - 1.0, Op.min)
         ts(v("s4"), v("s1"), 0.0, Op.max, float(C), Op.min)
         tt(v("fld", 2), v("s3"), v("s4"), Op.max)
         tt(v("fld", 3), v("fld", 2), v("s4"), Op.subtract)
@@ -488,7 +522,9 @@ def rank_program(g, core, T, topo):
 
     def unpack_addr(rd, s):
         land = v("arcv", rd, s, sl(0, 84))
-        arrive("ra%d%d" % (s, rd), whole, land, twa[s])
+        arrive("ra%d%d" % (s, rd), whole, v("arcv", rd, s), twa[s])
+        if (rd, 2 - s) == PLAIN:
+            return
         ts(v("uh"), land, 1.0 / 16384, Op.mult, 160.0 - 8191.5 / 16384, Op.add)
         cp(v("ui"), land)
         scan(v("us"), v("pat7"), v("uh"), 0.0, Op.mult, Op.add)
@@ -496,25 +532,31 @@ def rank_program(g, core, T, topo):
         ts(v("hl", s, sl(84, 12)), v("us", slice(6, 84, 7)), -160.0 * 5461, Op.add)
         cp(v("hl", s, sl(0, 84)), v("ua"))
 
-    def look(s):
-        bank, g0 = "pA" if s & 1 else "pB", C * (s & 1)
+    def look(rd, s):
+        g0 = C * s
 
-        def part(a, n, q):
+        def part(at, a, n, q):
+            x = ind(v("HW"), v("arcv", rd, s, sl(a, n)) if (rd, 2 - s) == PLAIN else v("hl", s, sl(a, n)))
             if q == "S":
-                act(v("G", sl(g0 + 16 * a, 16 * n)), ind(v("HW"), v("hl", s, sl(a, n))), Act.Copy)
+                act(v("G", sl(at, 16 * n)), x, Act.Copy)
             else:
-                cp(v("G", sl(g0 + 16 * a, 16 * n)), ind(v("HW"), v("hl", s, sl(a, n))))
+                cp(v("G", sl(at, 16 * n)), x)
         if s == 3:
-            part(0, 48, LQ[s][0]); part(48, 48, LQ[s][1])
-            mm([(v(bank, sl(0, 96)), v("ID", 1), v("ck0"))] + [(v(bank, sl(0, 96)), wide("WH", u, 0), v("G", sl(g0 + u, C - u, 16))) for u in range(16)])
+            part(g0, 0, 48, LQ[s][0]); part(g0 + 768, 48, 48, LQ[s][1])
+            mm([(v("pA", sl(0, 96)), v("ID", 1), v("ck0"))] + [(v("pA", sl(0, 96)), wide("WH", u, 0), v("G", sl(g0 + u, C - u, 16))) for u in range(16)])
         else:
-            part(0, 36, LQ[s][1]); part(72, 24, LQ[s][0]); part(36, 36, LQ[s][2])
-            mm([(v(bank, sl(0, 72)), v("ID", 1), v("ck"))]
-               + [(v(bank, slice(k, 72, 3)), wide("WH", u, k + 1), v("G", sl(g0 + 1152 + u, 384 - u, 16))) for u in range(16) for k in range(3)], last=False)
-            mm([(v(bank, sl(0, 72)), wide("WH", u, 0), v("G", sl(g0 + u, 1152 - u, 16))) for u in range(16)], first=False)
+            part(GX + 384 * s, 72, 24, "V")
+            a = 0
+            for q, n in LQ[s]:
+                part(g0 + 16 * a, a, n, q)
+                a += n
+            bank = "pM" if s & 1 else "pB"
+            mm([(v(bank, sl(0, 72)), v("ID", 1), v("ck"))], last=False)
+            mm([(v(bank, slice(k, 72, 3)), wide("WH", u, k + 1), v("G", sl(GX + 384 * s + u, 384 - u, 16))) for u in range(16) for k in range(3)], False, False)
+            mm([(v(bank, sl(0, 72)), wide("WH", u, 0), v("G", sl(g0 + u, 1152 - u, 16))) for u in range(16)], False, True)
 
     def reply(rd, s):
-        cp(v("rsnd", rd, s), v("pA" if s & 1 else "pB", sl(0, 72)))
+        cp(v("rsnd", rd, s), v("pM" if s & 1 else "pB", sl(0, 72)))
         twin[2 - s] = send1(s, "rr%d%d" % (2 - s, rd), v("rsnd", rd, s), v("rrcv", rd, 2 - s))
 
     def lists(rd, s):
@@ -522,12 +564,11 @@ def rank_program(g, core, T, topo):
         if s < 3:
             arrive("rr%d%d" % (s, rd), whole, v("rrcv", rd, s), twin[s])
             ts(v("rh"), v("rrcv", rd, s), 1.0 / 4096, Op.mult, 160.0 - 2047.5 / 4096, Op.add)
-            cp(v("ri"), v("rrcv", rd, s))
-            scan(v("rs"), v("pat3"), v("rh"), 0.0, Op.mult, Op.add)
-            ts(v("Ww", sl(0, 72)), v("ri"), 4095, Op.bitwise_and)
-            ts(v("Ww", sl(72, 24)), v("rs", slice(2, 72, 3)), -160.0 * 273, Op.add)
-        ts(v("l1", s), v("pA", sl(0, 96)) if s == 3 else v("Ww"), 1.0, Op.add)
-        tt(v("W2", sl(96 * o, 96)), v("pA", sl(0, 96)) if s == 3 else v("Ww"), v("dl", s, sl(1, 96)), Op.min)
+            cp(v("rs"), v("rrcv", rd, s))
+            mm([(v("pA", sl(0, 96)), v("ID", 1), v("cu")), (v("pA", sl(0, 72)), v("ID", 2), v("rh"))]
+               + [(v("pA", sl(72, 24)), v("ID", (3, 4, 0)[k]), v("rh", slice(k, 72, 3))) for k in range(3)] + [(v("pA", sl(0, 72)), v("TR", 2), v("rs"))])
+        ts(v("l1", s), v("pA", sl(0, 96)), 1.0, Op.add)
+        tt(v("W2", sl(96 * o, 96)), v("pA", sl(0, 96)), v("dl", s, sl(1, 96)), Op.min)
         ts(v("l2", s), v("W2", sl(96 * o, 96)), 1.0, Op.add)
 
     Aw = v("A", sl(0, 4104))
@@ -548,7 +589,7 @@ def rank_program(g, core, T, topo):
         tt(v("T1", b), ind(v("Pz", b, sl(0, 128)), v("bl", sl(8 * o, 8))), v("eq", sl(128 * o, 128)), Op.mult)
         act(v("T2", b), v("lt", sl(128 * o, 128)), Act.Identity, scale=v("Pz", b, sl(128, 1)))
         t = v("pT", sl(0, 128))
-        mm([(t, v("ON8"), v(k)) for k in ["Cc"][n:]] + [(t, v("ON8"), v("T2", b))], n == 0, False)
+        mm([(t, v("TR", 2), v(k)) for k in ["Cc"][n:]] + [(t, v("ON8"), v("T2", b))], n == 0, False)
         mm([(t, v("ON8"), v("T1", b))], False, n == 3)
         mm([(v("pC", sl(120 * o, 120)), wide("WZ", i, 0), v("ct", sl(c0 - 24 + 96 * i, 120))) for i in range(16)])
 
@@ -557,8 +598,8 @@ def rank_program(g, core, T, topo):
         tt(v("key"), v("pT", sl(0, 128)), v("S", sl(0, 128)), Op.subtract)
         scan(v("mk"), v("pat4"), v("key"), 0.0, Op.mult, Op.max)
         tt(v("oh"), ind(v("mk"), v("l43")), v("key"), Op.is_equal)
-        act(v("kd"), v("key"), Act.Identity, bias=ROUND, scale=0.25)
-        act(v("yto", sl(128 * rd, 128)), v("kd"), Act.Identity, bias=-ROUND)
+        for a in range(4):
+            act(v("yto", slice(128 * rd + a, 128 * rd + 128, 4)), v("key", slice(a, 128, 4)), Act.Identity, bias=(a - 3) / 4.0, scale=0.25)
 
     def heads(rd):
         act(v("ywo", sl(32 * rd, 32)), select(1, RC1), Act.Copy)
@@ -573,15 +614,18 @@ def rank_program(g, core, T, topo):
             step(heads, rd - 1)
             step(barrier, rd - 1)
         else:
+            step(tables)
+            follow(True)
             step(select, 1, RC1)
         step(chain, rd < RO - 1)
+        step(follow, rd < RO - 1)
         step(ends)
         step(bounds)
-        step(look, 3)
+        step(look, rd, 3)
         step(lists, rd, 3)
         for s in (2, 1, 0):
             step(unpack_addr, rd, s)
-            step(look, s)
+            step(look, rd, s)
             step(reply, rd, s)
         if rd < RO - 1:
             step(zero_w, rd + 1, v("rsnd", rd, 0))
@@ -605,7 +649,7 @@ def rank_program(g, core, T, topo):
     models = []
     for m in MODELS:
         gap = [[(j, -1e9 if K_[j] == 2 and not hard else 0.0 if not hard else m["same"] if Q_[j] == Q_[i] and K_[j] == 1 else m["wake"])
-                for j, hard in nodes[i]["dep"].items()] for i in range(n_)]
+                for j, hard in nodes[i]["dep"].items() if not any(x and nodes[k]["dep"].get(j) for k, x in nodes[i]["dep"].items())] for i in range(n_)]
         models.append(([x["busy"][0] + x["busy"][1] * m[x["busy"][2]] for x in nodes], [x["late"][0] * m[x["late"][1]] + (m["rows"] if x["kind"] == "d" else 0.0) for x in nodes], gap, m["dma"]))
     B_, L_, G_, D_ = models[0]
     level = [0.0] * n_
@@ -643,11 +687,36 @@ def rank_program(g, core, T, topo):
                     when[Q_[k]] = min(when[Q_[k]], max(free[Q_[k]], start[k]))
         return turn
 
-    def times(turn, m):
+    def backwards(turn, m):
         busy, late, pred, dmat = m
-        done, start, why = [0.0] * n_, [0.0] * n_, [-1] * n_
+        place = {i: n for n, i in enumerate(turn)}
+        left, free, out = [len(x) for x in succ], [0.0] * 6, [0.0] * n_
+        start = [late[i] + (dmat if K_[i] == 2 else 0.0) for i in range(n_)]
+        ready = [[i for i in range(n_) if not left[i] and Q_[i] == q] for q in range(6)]
+        for _ in nodes:
+            t0, q = min((max(free[q], min(start[i] for i in ready[q])), q) for q in range(6) if ready[q])
+            one = max((i for i in ready[q] if start[i] <= t0 + BACK), key=place.get)
+            ready[q].remove(one)
+            out[one] = max(t0, start[one]) + busy[one]
+            free[q] = out[one] if q else 0.0
+            for k, w in pred[one]:
+                start[k] = max(start[k], out[one] + (0.0 if w < 0 else w + late[k] + (dmat if K_[k] == 2 else 0.0)))
+            for k in nodes[one]["dep"]:
+                left[k] -= 1
+                if not left[k]:
+                    ready[Q_[k]].append(k)
+        return out
+
+    def times(turn, m, a=0, old=None):
+        busy, late, pred, dmat = m
+        start, why, done = (list(old[1]), list(old[2]), list(old[4])) if old else ([0.0] * n_, [-1] * n_, [0.0] * n_)
         free, last, dfree, dlast, end, tip = [0.0] * 6, [-1] * 6, 0.0, -1, 0.0, 0
-        for i in turn:
+        for i in turn[:a][::-1]:
+            if last[Q_[i]] < 0 and Q_[i]:
+                free[Q_[i]], last[Q_[i]] = start[i] + busy[i], i
+            if dlast < 0 and K_[i] == 2:
+                dfree, dlast = done[i] - dmat, i
+        for i in turn[a:]:
             q = Q_[i]
             t, w = free[q], last[q]
             for j, g_ in pred[i]:
@@ -660,8 +729,8 @@ def rank_program(g, core, T, topo):
             if K_[i] > 1:
                 if dfree > t:
                     t, w = dfree, dlast
+                t += late[i]
                 if K_[i] == 2:
-                    t += late[i]
                     dfree, dlast = t, i
                     t += dmat
             else:
@@ -669,11 +738,11 @@ def rank_program(g, core, T, topo):
             done[i], why[i] = t, w
             if t > end:
                 end, tip = t, i
-        return end, start, why, tip
+        return end + SOON * sum(done) / n_, start, why, tip, done, end
 
-    def moved(turn, u, x, up):
+    def moved(turn, u, x, up, go):
         a, b = turn.index(u), turn.index(x)
-        part, go = turn[a:b + 1], {x if up else u}
+        part = turn[a:b + 1]
         for i in (part[::-1] if up else part):
             if i not in go and any(k in go for k in (succ[i] if up else nodes[i]["dep"])):
                 go.add(i)
@@ -682,21 +751,26 @@ def rank_program(g, core, T, topo):
         one, two = [i for i in part if i in go], [i for i in part if i not in go]
         return turn[:a] + (one + two if up else two + one) + turn[b + 1:]
 
-    if not FOUND:
-        rs = np.random.RandomState(SEED)
+    def improve(seed, turn, SHIFTS, TRIES):
+        rs = np.random.RandomState(seed)
         like = {}
         for i, x in enumerate(nodes):
             like.setdefault(x["tag"], []).append(i)
-        rank, turn = np.array(level), lay_out(level)
-        best = sum(times(turn, m)[0] for m in models)
+        rank = np.array(level)
+        cost = best = sum(times(turn, m)[0] for m in models)
         for n in range(SHIFTS):
             a, new = rs.randint(n_), rank.copy()
             some = range(a, min(n_, a + rs.randint(1, rs.choice([3, 12, 40]))))
+            some = [i for i in some if n & 2 or nodes[i]["tag"][0] == nodes[a]["tag"][0]]
             new[[j for i in some for j in (like[nodes[i]["tag"]] if n & 1 else [i])]] += rs.choice([-1.0, 1.0]) * rs.choice([300.0, 1000.0, 3000.0, 8000.0])
+            if n % TURNS == 0:
+                new = np.array(backwards(lay_out(new.tolist()), models[n // TURNS % len(models)]))
             tn = lay_out(new.tolist())
             c = sum(times(tn, m)[0] for m in models)
-            if c <= best:
-                best, rank, turn = c, new, tn
+            if c <= cost + WARM * (1.0 - n / SHIFTS) * rs.exponential():
+                cost, rank = c, new
+                if c <= best:
+                    best, turn = c, tn
         now = [times(turn, m) for m in models]
         cost = best = sum(x[0] for x in now)
         keep = turn
@@ -705,7 +779,7 @@ def rank_program(g, core, T, topo):
                 turn = sorted(turn, key=lambda i: now[0][1][i])
                 now = [times(turn, m) for m in models]
                 cost = sum(x[0] for x in now)
-            _, _, why, x = now[rs.randint(len(now))]
+            why, x = now[rs.randint(len(now))][2:4]
             pairs = []
             while why[x] >= 0:
                 if why[x] not in nodes[x]["dep"]:
@@ -713,21 +787,32 @@ def rank_program(g, core, T, topo):
                 x = why[x]
             u, x = pairs[rs.randint(len(pairs))]
             up = rs.randint(2)
+            if n % 3 == 0:
+                x = rs.randint(n_)
             mates = [i for i in turn if Q_[i] == Q_[x]]
-            if Q_[u] == Q_[x] and rs.randint(2):
-                if up:
-                    u = mates[max(0, mates.index(u) - rs.randint(1, 6))]
-                else:
-                    x = mates[min(len(mates) - 1, mates.index(x) + rs.randint(1, 6))]
-            new = moved(turn, u, x, up)
+            if n % 3 == 0:
+                u = mates[max(0, mates.index(x) - 1)]
+            go = {x if up else u}
+            if Q_[u] == Q_[x] and rs.randint(3):
+                a, b = mates.index(u), mates.index(x)
+                far, run_ = rs.geometric(JUMP), (rs.geometric(0.3) - 1) * rs.randint(2)
+                a, b = max(0, a - (far if up else run_)), min(len(mates) - 1, b + (run_ if up else far))
+                go = set(mates[mates.index(x):b + 1] if up else mates[a:mates.index(u) + 1])
+                u, x = mates[a], mates[b]
+            new = moved(turn, u, x, up, go)
             if new:
-                then = [times(new, m) for m in models]
+                then = [times(new, m, turn.index(u), y) for m, y in zip(models, now)]
                 c = sum(y[0] for y in then)
                 if c <= cost + HEAT * (1.0 - n / TRIES) * rs.exponential():
                     turn, now, cost = new, then, c
                     if c < best:
                         best, keep = c, new
-        FOUND.extend([keep, best / len(models)])
+        return best, keep
+
+    if not FOUND:
+        keep = min(improve(SEED + i, lay_out(level), SHIFTS, TRIES // 3) for i in range(STARTS))[1]
+        keep = improve(SEED, keep, 0, TRIES)[1]
+        FOUND.extend([keep, sum(times(keep, m)[5] for m in models) / len(models)])
     place = {i: n for n, i in enumerate(FOUND[0])}
     left, ready, turn = list(deps), {i for i in range(n_) if not deps[i]}, []
     while ready:
@@ -772,8 +857,11 @@ def rank_program(g, core, T, topo):
             wait("Q", s, count[s])
 
 
-FOUND, SEED, TRIES = [], 1, 5000
-HEAT, CHUNK, EB, EARLY, SHIFTS, AHEAD = 50.0, 900, "BAMB", 3, 4000, 0.4
-ORD, LQ = (3, 0, 1, 2), ("VSS", "VSV", "VSS", "SS")
-PARTS = ((768, 768),) * 4
-FILL = {"TB": "S", "W": "VVVS", "HW": "SSSSSQQQQQVVVVVV"}
+FOUND, SEED, STARTS, SHIFTS, TRIES = [], 1, 4, 1000, 27000
+WARM, HEAT, SOON, TURNS, BACK, AHEAD, JUMP, CHUNK = 300.0, 60.0, 0.1, 10, 800.0, 0.4, 0.2, 600
+ORD, EB = (3, 0, 1, 2), "BAMB"
+PLAIN = (0, 0)
+LOADS = ((1, "ls"), (3, "t3a"), (2, "hw0"), (2, "hw0"))
+LQ = ((("S", 36), ("S", 20), ("V", 16)), (("S", 36), ("V", 36)), (("S", 36), ("S", 36)), "SS")
+PARTS, CUT = ((768, 768),) * 3 + ((768, 512, 256),), (256, 256)
+FILL = {"W": "VVVS", "HW": "SSSSQQQQVVVV"}

import numpy as np
from concourse.bass import DstId, RemoteDMATransfer
from concourse.mybir import AluOpType, ActivationFunctionType

N, RO, C = 4, 3, 1536
F32, BF, F16, I32, U16 = "float32", "bfloat16", "float16", "int32", "uint16"
XS, CS, WS = 1544, 1568, 2560
GX = 4 * C
HALF = 1536.0

BUFS = {
    "wraw": (I32, [4096]), "A": (F32, [4240]), "hraw": (I32, [1024]), "HW": (BF, [16384]), "ZB": (BF, [1536]),
    "TB": (F32, [1024]), "srn": (I32, [2, 256]), "srd": (F32, [9, 64]), "nxn": (I32, [64]), "curi": (I32, [32]),
    "mg": (I32, [64]), "mo": (I32, [64]), "mq": (I32, [2, 64]), "mf": (F32, [3, 64]), "mlf": (F32, [66]), "mlh": (F32, [66]),
    "mx": (U16, [4, 88]), "mi": (I32, [4, 86]), "ml": (I32, [4, 66]), "mlo": (I32, [4, 64]), "mrole": (BF, [3, 4, 64]),
    "pi": (I32, [8]), "pc": (F32, [128]), "X": (F32, [144]), "i16": (F32, [2, 128]), "NI": (F32, [400]),
    "Mw": (F32, [144]), "M4": (F32, [144]), "ONE": (F32, [128]), "M16": (F32, [128]), "TR": (F32, [3, 128]), "ON8": (F32, [128]),
    "WA": (BF, [4, 144]), "WL": (BF, [1, 144]), "TS": (BF, [2, 128]), "sg": (BF, [2, 104]), "WH": (BF, [4, 144]), "WZ": (BF, [2, 144]), "Wn": (F32, [2, 144]), "W4f": (F32, [2, 144]),
    "W4": (BF, [4, 144]), "WB": (BF, [2, 144]), "ME": (BF, [144]), "WK": (BF, [12, 128]), "WE": (BF, [4, 128]), "ONn": (BF, [128]), "ID": (BF, [5, 128]), "cu": (F16, [96]),
    "slc": (F16, [32]), "k24": (F16, [32]), "r1": (F16, [128]), "ck": (BF, [72]), "ck0": (BF, [96]), "Cc": (F32, [128]),
    "pat4": (BF, [128]), "pat7": (BF, [84]), "pat5": (F32, [66]), "pat16": (BF, [128]), "pat9": (BF, [72]),
    "sc7": (F32, [96]), "repf": (F32, [6]), "repl": (U16, [6]), "l43": (U16, [8]), "cap": (BF, [512]), "top": (F32, [96]),
    "neg8": (BF, [128]), "on1": (BF, [480]), "qrt": (F32, [128]), "Dc": (F32, [8]),
    "hc": (U16, [8]), "sl": (U16, [32]), "RG": (F32, [512]), "RS": (F32, [128]), "oh": (F32, [128]),
    "pr": (F32, [2, 128]), "ps": (F32, [2, 128]), "rq": (U16, [32]), "fld": (F16, [4, 32]),
    "G3": (BF, [512]), "Gb": (BF, [512]), "G2": (BF, [512]), "F": (F16, [520]), "vv": (F16, [512]), "nf": (BF, [520]),
    "off": (U16, [32]), "Fc": (F32, [1]), "W": (BF, [4 * WS]), "dl": (F32, [4, 104]), "aa": (F32, [4, 96]),
    "pk": (I32, [96]), "pk2": (I32, [84]), "pk3": (F32, [84]), "asnd": (U16, [3, 3, 96]), "arcv": (U16, [3, 3, 96]),
    "ui": (I32, [84]), "ua": (I32, [84]), "uh": (BF, [84]), "us": (F32, [84]), "hl": (U16, [4, 96]),
    "G": (BF, [GX + 1152]), "rsnd": (U16, [3, 3, 72]), "rrcv": (U16, [3, 3, 72]), "rh": (BF, [72]), "rs": (F32, [72]),
    "W2": (I32, [400]), "l1": (U16, [4, 96]), "l2": (U16, [4, 96]),
    "xs": (F32, [2 * XS]), "ct": (BF, [2 * CS]), "d1": (BF, [2, C]), "z": (BF, [2, C]), "Pz": (F32, [2, 136]), "T1": (F32, [2, 128]), "T2": (F32, [2, 128]),
    "nh": (BF, [480]), "DS": (BF, [480]), "ch": (BF, [512]), "lt": (BF, [512]), "eq": (BF, [512]),
    "bi": (I32, [32]), "bj": (I32, [32]), "bh": (BF, [32]), "bl": (U16, [32]), "S": (F32, [136]), "key": (F32, [128]), "mk": (F32, [128]),
    "s0": (F32, [32]), "s1": (F32, [32]), "s2": (F32, [32]), "s3": (F32, [32]), "s4": (F32, [32]),
    "p2": (F16, [128]), "se": (F16, [128]), "cl": (U16, [3, 8]), "m1": (BF, [128]), "m2": (BF, [128]), "bg": (BF, [128]), "ys": (F32, [128]),
    "m3": (F32, [128]), "bw": (F32, [128]), "b0": (F32, [128]), "b1": (F32, [136]), "E3": (BF, [8, 16, 9]), "cn": (F32, [72]), "co": (F32, [8]),
    "yto": (F32, [384]), "ybo": (F32, [384]), "ywo": (F32, [96]),
}
BANKS = ["pA", "pB", "pK", "pM", "pZ", "pC", "pT", "pS"]
PLACE, SCRATCH = {}, {}
for _k, (_d, _s) in BUFS.items():
    if len(_s) == 1 and _s[0] <= 520:
        _at = SCRATCH.get("pool_" + _d, (0, [128, 0]))[1][1]
        PLACE[_k] = ("pool_" + _d, _at)
        SCRATCH["pool_" + _d] = ("sbuf", [128, _at + (_s[0] + 15) // 16 * 16], _d)
    else:
        SCRATCH[_k] = ("sbuf", [128] + _s, _d)
SCRATCH.update({k: ("psum", [128, 512], F32) for k in BANKS})
SEMAPHORES = (["V", "S", "P", "Q", "sent", "rm", "lm", "ls", "lc", "lh", "tb", "t3a", "hw0", "oy0", "oy1", "oy2"]
              + ["%s%d" % (k, i) for k in ("wz", "wy", "ra0", "ra1", "ra2", "rr0", "rr1", "rr2") for i in range(RO)] + ["lw%d" % i for i in range(8)])
ALL = slice(None)
MODELS = [dict(c=1.04, g=1.62, s=3.95, p=0.52, byte=0.0045, rows=250.0, same=30.0, wake=90.0, dma=2000.0, far=2800.0, call=300.0),
          dict(c=0.88, g=1.37, s=3.3, p=0.44, byte=0.003, rows=300.0, same=80.0, wake=200.0, dma=2200.0, far=3300.0, call=600.0)]


def rank_program(g, core, T, topo):
    me = T.rank_of(core)
    if me is None:
        return
    Op, Act = AluOpType, ActivationFunctionType
    eng = {"V": g.vector, "S": g.scalar, "P": g.tensor, "Q": g, "Y": g.sync}
    nodes, hist, bysem, tag, table = [], {}, {}, ["", 0], []

    def v(name, *idx, p=ALL):
        if name in PLACE:
            a, b, st = (idx[0] if idx else ALL).indices(BUFS[name][1][0])
            name, at = PLACE[name]
            idx = (slice(at + a, at + b, st) if st > 1 else slice(at + a, at + b),)
        shape = SCRATCH[name][1]
        cols = np.arange(int(np.prod(shape[1:]))).reshape(shape[1:])[idx if idx else ALL]
        lo, hi = int(np.min(cols)), int(np.max(cols)) + 1
        pm = sum(1 << int(x) for x in np.arange(128)[p])
        if name in BANKS:
            lo, hi, pm = 0, 512, (1 << 128) - 1
        return (T[name][(p,) + (tuple(idx) if idx else (ALL,))], [(name, lo, hi, pm)], [], int(np.size(cols)), SCRATCH[name][2] in (BF, F16, U16), name in BANKS)

    def ind(win, off):
        return (win[0].indirect(off[0]), win[1], off[1], 16 * off[3], win[4], False)

    def ap(x):
        return x[0] if isinstance(x, tuple) else x

    def node(q, kind, outs, ins, call, busy, late=(0, "c"), sem=None, n=1, after=()):
        outs = [x for x in outs if isinstance(x, tuple)]
        ins = [x for x in ins if isinstance(x, tuple)]
        rd = [r for x in ins for r in x[1]] + [r for x in outs + ins for r in x[2]]
        wr = [r for x in outs for r in x[1]]
        i = len(nodes)
        dep = {j: False for j in after}
        for k, rs in (("w", wr), ("r", rd)):
            for (nm, lo, hi, pm) in rs:
                for (l2, h2, p2, k2, j) in hist.get(nm, []):
                    if l2 < hi and lo < h2 and (pm & p2) and (k == "w" or k2 == "w" or (nm in BANKS and nodes[j]["q"] != q)):
                        soft = kind == "c" and nodes[j]["kind"] == "c" and nodes[j]["q"] == q == "P"
                        dep[j] = dep.get(j, False) or not soft
        for j in list(dep):
            if nodes[j]["kind"] == "d" and dep[j]:
                for j2 in bysem[nodes[j]["sem"]]:
                    dep[j2] = True
        for (nm, lo, hi, pm) in wr:
            hist[nm] = [e for e in hist.get(nm, []) if not (lo <= e[0] and e[1] <= hi and (e[2] & ~pm) == 0)] + [(lo, hi, pm, "w", i)]
        for (nm, lo, hi, pm) in rd:
            hist.setdefault(nm, []).append((lo, hi, pm, "r", i))
        nodes.append({"q": q, "kind": kind, "call": call, "busy": busy, "late": late, "sem": sem, "n": n, "dep": dep, "tag": tuple(tag)})
        tag[1] += 1
        if kind == "d":
            bysem.setdefault(sem, []).append(i)
        return i

    def run(q, o, ins, call, k=1.0, fast=True):
        xs = [x for x in [o] + ins if isinstance(x, tuple) and x[3] > 1] or [o]
        if o[2]:
            t = (50.0, o[3], "s")
        elif any(x[2] for x in xs):
            t = (50.0 if q == "V" else 65.0, o[3], "g")
        else:
            t = (0.0, max(64, max(x[3] for x in xs) * (0.5 if fast and all(x[4] for x in xs) else k)), "c")
        node(q, "c", [o], ins, call, t)

    def cp(o, i): run("V", o, [i], lambda: g.vector.tensor_copy(ap(o), ap(i)))
    def ms(o, c): run("V", o, [], lambda: g.vector.memset(ap(o), c))
    def tt(o, a, b, op): run("V", o, [a, b], lambda: g.vector.tensor_tensor(ap(o), ap(a), ap(b), op), 1.0 if a[5] or b[5] else 2.0, False)

    def ts(o, a, s1, op0, s2=None, op1=None):
        if op1 is None:
            run("V", o, [a, s1], lambda: g.vector.tensor_scalar(ap(o), ap(a), ap(s1), None, op0))
        else:
            run("V", o, [a, s1, s2], lambda: g.vector.tensor_scalar(ap(o), ap(a), ap(s1), ap(s2), op0, op1))

    def scan(o, a, b, init, op0, op1):
        run("V", o, [a, b, init], lambda: g.vector.tensor_tensor_scan(ap(o), ap(a), ap(b), ap(init), op0, op1))

    def act(o, i, f, bias=0.0, scale=1.0):
        run("S", o, [i, bias, scale], lambda: g.scalar.activation(ap(o), ap(i), f, bias=ap(bias), scale=ap(scale)), 1.0, False)
        if f is Act.Sigmoid and not table:
            table.append(nodes[-1])
            nodes[-1]["busy"] = (1300.0,) + nodes[-1]["busy"][1:]

    def iota(o, pat, base, cm):
        node("Q", "c", [o], [], lambda: g.iota(ap(o), pat, base, cm, allow_small_or_imprecise_dtypes=True), (130.0, 2 * o[3], "c"))

    def pick(o, i, step, op, c=0.0):
        node("Q", "c", [o], [i], lambda: g.affine_select(ap(o), ap(i), [[step, 128]], op, c, 0, -step), (170.0, 2 * o[3], "c"))

    def put(o, i, r, c):
        node("Q", "c", [o], [i], lambda: g.affine_select(ap(o), ap(i), [[-16, 8], [0, 16]], Op.not_equal, c, -r, 1), (170.0, 2 * o[3], "c"))

    def fill(q, o, c):
        if q == "V":
            ms(o, c)
        elif q == "S":
            act(o, v("ZB", sl(16, o[3])), Act.Identity, bias=c)
        else:
            iota(o, [[0, o[3]]], int(c), 0)

    def mm(items, first=True, last=True):
        cost = [max(64, x[2][3]) * (1 if x[2][4] else 4) for x in items]
        if sum(cost) > CHUNK and len(items) > 1:
            h = len(items) // 2
            mm(items[:h], first, False)
            mm(items[h:], False, last)
            return

        def call():
            for n, (o, l, r) in enumerate(items):
                inst = g.tensor.matmul(ap(o), ap(l), ap(r), first and n == 0, last and n == len(items) - 1)
            return inst
        node("P", "c", [items[0][0]], [y for x in items for y in x[1:]], call, (0.0, sum(cost), "p"))

    def dma(q, sem, o, i, gate=None, after=()):
        x = o if isinstance(o, tuple) else i
        nbytes = x[3] * bin(x[1][0][3]).count("1") * (2 if x[4] else 4)
        node(q, "d", [o], [i, gate], lambda: eng[q].dma_start(ap(o), ap(i)), (100.0, 0, "c"), (nbytes, "byte"), sem, 16, after)

    peer = [T.cores[(me + 1 + s) % N] for s in range(3)]
    whole = len(topo.engines(core, peer[0]))
    sends = []

    def send_all(sem, src, dsts):
        def call():
            ids = [DstId(rid=topo.addr(c)[0], pnc=topo.addr(c)[1]) for c in peer]
            g.remote_dma_fused([RemoteDMATransfer(dst_ids=ids, dma_engine_mask=topo.mask(core, peer[0]), remote_sem=T.sem[sem],
                                                  srcs=[ap(src)], dsts=[ap(d) for d in dsts])], local_sem=T.sem["sent"])
        sends.append(node("Q", "r", [], [src], call, (2000.0, 1, "call"), n=whole))
        return sends[-1]

    def send1(s, sem, src, dst):
        def call():
            rid, pid, _ = topo.addr(peer[s])
            g.remote_dma(ap(dst), ap(src), T.sem[sem], T.sem["sent"], pid, rid, topo.mask(core, peer[s]))
        sends.append(node("Q", "r", [], [src], call, (0.0, 1, "call"), n=whole, after=sends[-1:]))
        return sends[-1]

    def arrive(sem, n, land, twin):
        node("A", "a", [land], [], None, (0.0, 0, "c"), (1, "far"), sem, n, [twin])

    ncol = [0]

    def newcol(n=1):
        ncol[0] += n
        return v("pc", slice(ncol[0] - n, ncol[0]))

    def cols(a, s1, op0, s2=None, op1=None):
        at = ncol[0]
        ts(newcol(a[3]), a, s1, op0, s2, op1)
        return [v("pc", sl(at + i, 1)) for i in range(a[3])]

    def colts(*a): return cols(*a)[0]
    def sl(a, n, st=1): return slice(a, a + n, st)
    def wide(name, u, *i): return v(name, *i, slice(15 - u, 143 - u))
    def wide4(name, i, b): return v(name, i, slice(12 - 4 * b, 140 - 4 * b))
    def rows(r): return slice(r, 128, 16)
    secs = [(me + 1 + s) % N for s in range(3)] + [me]

    dma("Y", "lm", v("mg"), T.gst[:])
    dma("S", "lm", v("mo"), T.gln[:])
    dma("Y", "ls", v("srn", 0), T.sens[:])
    dma("S", "ls", v("srn", 1), T.rel[:])
    dma("Y", "ls", v("nxn"), T.nxt[:])
    ms(v("curi"), 0)
    dma("S", "lc", v("curi", p=rows(0)), T.cur[:])
    ms(v("ZB"), 0.0)
    iota(v("pi", sl(0, 1)), [[0, 1]], 0, 1)
    iota(v("X"), [[1, 144]], 0, 0)
    iota(v("i16", 0), [[0, 8], [1, 16]], 0, 0)
    iota(v("i16", 1), [[16, 8], [0, 16]], 0, 0)

    ms(v("mlf"), 0.0)
    ms(v("pat5"), 32.0); ms(v("pat5", sl(0, 66, 3)), 0.0)
    cp(v("mlf", sl(0, 64)), v("mo"))
    scan(v("mlh"), v("pat5"), v("mlf"), 0.0, Op.mult, Op.add)
    cp(v("mx", 3, sl(64, 22)), v("mlh", slice(2, 66, 3)))
    tt(v("mq", 0), v("mg"), v("mo"), Op.add)
    ts(v("mq", 1), v("mq", 0), 1.0 / 128, Op.mult, -64.5 / 128, Op.add)
    ts(v("mf", 0), v("mq", 1), 128.0, Op.mult, 256.0, Op.add)
    ts(v("mf", 2), v("mo"), 65535.0, Op.mult)
    tt(v("mf", 1), v("mf", 0), v("mq", 0), Op.add)
    tt(v("mf", 0), v("mf", 1), v("mf", 2), Op.min)
    cp(v("mx", 3, sl(0, 64)), v("mf", 0))
    tw = send_all("rm", v("mx", 3, sl(0, 86)), [v("mx", 2 - s, sl(0, 86)) for s in range(3)])
    arrive("rm", 3 * whole, v("mx", sl(0, 3)), tw)

    for k, (sh, an) in enumerate(((0, 15), (0, 3), (2, 3), (0, 112))):
        ts(v("pi", sl(k + 1, 1)), v("pi", sl(0, 1)), sh, Op.logical_shift_right, an, Op.bitwise_and)
    P16, P4, PA, G16 = cols(v("pi", sl(1, 4)), 0.0, Op.add)
    QA = cols(v("X", sl(0, 4)), PA, Op.is_equal)
    Q4 = newcol(4)
    ts(Q4, v("X", sl(0, 4)), P4, Op.is_equal)
    ts(v("M16"), v("i16", 0), P16, Op.is_equal)
    ts(v("ONE"), v("i16", 1), G16, Op.is_equal)
    Q16 = [v("M16", sl(i, 1)) for i in range(16)]
    ts(v("Mw"), v("X"), colts(G16, 15.0, Op.add), Op.is_equal)
    ts(v("M4"), v("X"), colts(G16, P4, Op.add, 12.0, Op.add), Op.is_equal)

    def weights(o, master, scale): act(o, v(master), Act.Identity, scale=scale)

    iota(v("TB"), [[1, 1024]], 0, 0)
    for t in range(2):
        for a in range(4):
            cp(v("srd", 4 * t + a), v("srn", t, slice(a, 256, 4)))
    cp(v("srd", 8), v("nxn"))
    for r in range(9):
        dma("Y", "tb", v("TB", p=rows(r)), v("srd", r))
    for i in range(2):
        weights(v("W4f", i), "M4", QA[i])
        weights(v("Wn", i), "Mw", Q16[8 + i])
    cp(v("ps", 1, slice(3, 128, 4)), v("curi"))
    ms(v("oh"), 0.0); ms(v("oh", sl(0, 128, 4)), 1.0)
    ms(v("pat4"), 1.0); ms(v("pat4", sl(0, 128, 4)), 0.0)
    RC0, RC1, XF = [v("pK", sl(128 * i, 128)) for i in range(3)]

    def chain(more):
        mm([(v("pK", sl(384, 8)), wide4("W4f", 0, b), v("ps", 1, slice(3 + 4 * b, 128, 16))) for b in range(4)])
        cp(v("hc"), v("pK", sl(384, 8)))
        act(v("RS"), ind(v("TB"), v("hc")), Act.Copy)
        if more:
            mm([(v("pK", sl(384, 32)), wide4("W4f", 0, b), v("RS", slice(b, 128, 4))) for b in range(4)])
            cp(v("sl"), v("pK", sl(384, 32)))
            act(v("RG"), ind(v("TB"), v("sl")), Act.Copy)
            mm([(RC0, wide4("W4f", 1, b), v("RG", slice(b, 512, 4))) for b in range(4)])

    def follow(more):
        mm([(RC1, wide("Wn", 9, 1), v("RS"))] + [(RC1, wide("Wn", b, 0), v("RG", slice(b, 512, 4))) for b in range(4 * more)])

    chain(True)

    LEN = colts(PA, 2.0, Op.is_ge)
    EMP = colts(LEN, -129.0, Op.mult, 128.0, Op.add)
    for h in range(4):
        act(v("HW", sl(1024 * h, 1024)), v("ZB", sl(16, 1024)), Act.Identity, bias=EMP)
    for ss in (sl(3, 1), sl(0, 3)):
        cp(v("mi", ss), v("mx", ss, sl(0, 86)))
        for r in (0, 1, 2):
            if r == 2 and ss.start:
                ts(v("mrole", r, 3), v("mo"), -1.0, Op.add)
            elif r == 2:
                for k in range(3):
                    ts(v("ml", ss, slice(k, 66, 3)), v("mi", ss, sl(64, 22)), 10 - 5 * k, Op.logical_shift_right, 31, Op.bitwise_and)
                ts(v("mrole", r, ss), v("ml", ss, sl(0, 64)), -1.0, Op.add)
            elif r == 0:
                ts(v("mrole", r, ss), v("mx", ss, sl(0, 64)), 1.0 / 256, Op.mult, 127.76, Op.add)
            else:
                ts(v("mlo", ss), v("mi", ss, sl(0, 64)), 255, Op.bitwise_and)
                ts(v("mrole", r, ss), v("mlo", ss), 128.0, Op.add)
            for s in range(4)[ss]:
                dma("Y", "t3a", v("HW", sl(1024 * secs[s], 1024), p=rows(4 * r + secs[s])), v("mrole", r, s))
    dma("Y", "lh", v("hraw"), T.heap[:], None, bysem["tb"])
    BGB, KAP = colts(EMP, -4096.0, Op.mult), colts(LEN, -1.0, Op.add)
    BG2 = colts(LEN, QA[3], Op.add)
    NF0 = colts(LEN, 129.0, Op.mult, colts(BG2, -129.0, Op.add), Op.add)
    cp(v("nf", sl(0, 1)), NF0)
    ms(v("F", sl(0, 1)), 512.0)
    fill("V", v("cap"), 2048.0)
    pick(v("TR", 0), v("ONE"), 1, Op.is_ge)
    pick(v("TR", 1), v("ONE"), -1, Op.is_gt)
    pick(v("TR", 2), v("ONE"), 1, Op.is_equal)
    act(v("ID", 0), v("TR", 2), Act.Copy)
    act(v("ID", 1), v("TR", 2), Act.Copy, scale=float(WS))
    for i, c in enumerate((-4096.0, 256.0, 16.0)):
        pick(v("ID", i + 2), v("ZB", sl(16, 128)), 1, Op.not_equal, c)
    ms(v("cu", sl(0, 72)), 160.0 * 4096 / WS); ms(v("cu", sl(72, 24)), -160.0 * 273 / WS)
    iota(v("NI"), [[16, 400]], 0, 1)
    act(v("NI"), v("NI"), Act.Identity, bias=colts(G16, -1.0, Op.mult))
    cp(v("slc"), v("NI", sl(0, 32)))
    ms(v("k24"), -HALF)
    weights(v("WL", 0), "Mw", QA[2])
    wa = colts(colts(PA, -127.0, Op.mult, 128.0, Op.add), -1.0, Op.max, QA[3], Op.add)
    for o, c in enumerate(cols(Q4, wa, Op.mult, colts(Q16[12], -32768.0, Op.mult), Op.add)):
        weights(v("WA", o), "Mw", c)
    ms(v("dl", ALL, sl(0, 1)), 0.0)
    ms(v("top"), 16383.0)
    ms(v("pat7"), 4.0); ms(v("pat7", sl(0, 84, 7)), 0.0)
    ms(v("us"), 4.0); ms(v("sc7", sl(84, 12)), 0.0)
    scan(v("sc7", sl(0, 84)), v("pat7"), v("us"), 0.0, Op.mult, Op.max)
    ts(v("repf"), v("NI", sl(0, 6)), 1.0 / 7, Op.mult, 84.0 - 3.0 / 7, Op.add)
    ts(v("repl"), v("repf"), 95.0, Op.min)
    ms(v("sg", ALL, sl(0, 1)), 0.0)
    for i in range(2):
        act(v("TS", i), v("TR", i), Act.Copy, scale=-16384.0)
    cp(v("ZB", sl(0, 1)), Q16[12])

    def zero_w(rd, gate=None):
        for o in range(4):
            pp = slice(o, 128, 4)
            dma("Y", "wz%d" % rd, v("W", sl(o * WS + 512, C), p=pp), v("ZB", p=pp), gate)
            if o:
                dma("Y", "wy%d" % rd, v("W", sl(o * WS + 512, C), p=rows(12)), v("ZB", p=rows(12)), gate)
    for o, q in enumerate(FILL["W"]):
        for h in range(2):
            fill(q, v("W", sl(o * WS + 512 + 768 * h, 768)), 0.0)
    ts(v("W", slice(512, 4 * WS, WS)), v("X", sl(0, 4)), 0.0, Op.mult, Q16[12], Op.add)
    for k, q in enumerate(FILL["HW"], 4):
        for h in range(2 if q == "Q" else 1):
            fill(q, v("HW", sl(1024 * k + 512 * h, 512 if q == "Q" else 1024)), 0.0)
    ts(v("G", sl(0, 1024)), v("hraw"), 1.0 / 256, Op.mult, 160.0 - 127.5 / 256, Op.add)
    ts(v("hraw"), v("hraw"), 255, Op.bitwise_and)
    cp(v("G", sl(1024, 1024)), v("hraw"))
    weights(v("WH", 0), "Mw", colts(Q16[13], 256.0, Op.mult, Q16[14], Op.add))
    fill("Q", v("ck0"), -16.0)
    act(v("G", sl(2048, 1024)), v("G", sl(1024, 1024)), Act.Identity, bias=160.0 - 7.5 / 16, scale=1.0 / 16)
    h0, h1, h2 = cols(v("M16", sl(13, 3)), 4096.0, Op.mult)
    for i, c in enumerate((h0, h2, colts(Q16[15], -65536.0, Op.mult, h1, Op.add))):
        weights(v("WH", i + 1), "Mw", c)
    fill("Q", v("ck"), -272.0); fill("Q", v("ck", slice(2, 72, 3)), 4080.0)
    act(v("WZ", 0), v("Mw"), Act.Copy)
    act(v("WZ", 1), v("Mw"), Act.Copy, scale=-1.0 / 16)
    act(v("ON8"), v("ONE"), Act.Copy, scale=8.0)
    act(v("ONn"), v("ONE"), Act.Copy, scale=-1.0)
    for a in range(4):
        weights(v("W4", a), "M4", QA[a])
        put(v("WE", a), v("ZB", sl(16, 128)), 8 + a, 1.0)
    ts(v("ME"), v("X"), colts(colts(P4, 4.0, Op.mult, G16, Op.add), 3.0, Op.add), Op.is_equal, QA[2], Op.mult)
    ts(v("r1"), v("X", sl(0, 128)), 4.0, Op.mult, -508.0, Op.add)
    weights(v("WB", 0), "M4", colts(QA[1], -96.0, Op.mult, colts(QA[0], 120.0, Op.mult, QA[2], Op.add), Op.add))
    weights(v("WB", 1), "M4", colts(QA[0], 96.0, Op.mult, colts(QA[2], 1.0 / 16, Op.mult), Op.add))
    fill("Q", v("WK", sl(0, 4)), 0.0)
    for k in range(4):
        put(v("WK", k), v("WK", k), k, float(C))
        put(v("WK", k), v("WK", k), 8 + k, 1.0)
        put(v("WK", 4 + k), v("ZB", sl(16, 128)), 4 + k, 1.0)
        put(v("WK", 8 + k), v("ZB", sl(16, 128)), 12 + k, 1.0)
    for k in range(2):
        fill("Q", v("xs", sl(k * XS, 8)), 0.0)
        fill("Q", v("ct", sl(k * CS, 32)), 0.0)
    PCH, PPC = colts(P16, 160.0, Op.add), colts(P16, HALF, Op.add)
    BLT = colts(P16, -1000.0, Op.mult, -160500.0, Op.add)
    act(v("neg8"), v("ZB", sl(16, 128)), Act.Identity, bias=colts(P16, 12.0, Op.is_lt, -8.0, Op.mult))
    act(v("on1"), v("ZB", sl(16, 480)), Act.Sigmoid, bias=200.0)
    pick(v("qrt"), v("X", sl(0, 128)), 0, Op.not_equal, 0.25)
    for a, c in enumerate((3, 5, 6, 6)):
        iota(v("Cc", slice(a, 128, 4)), [[6, 32]], c, 0)
    fill("Q", v("pat16"), 1.0); fill("Q", v("pat16", sl(0, 128, 16)), 0.0)
    fill("Q", v("pat9"), 1.0); fill("Q", v("pat9", sl(0, 72, 9)), 0.0); fill("Q", v("pat9", slice(8, 72, 9)), 8192.0)
    act(v("Dc"), v("NI", sl(0, 8)), Act.Identity, bias=4104.0)
    ts(v("l43"), v("NI", sl(0, 8)), P4, Op.subtract, 3.0, Op.add)
    for x in (v("Pz", ALL, sl(0, 1)), v("S", sl(0, 1)), v("b1", sl(0, 1))) + tuple(v("E3", sl(2 * i, 2)) for i in range(4)):
        fill("Q", x, 0.0)
    fill("Q", v("W2", sl(384, 16)), -1.0)
    fill("Q", v("A", sl(0, 1)), -9.0); fill("Q", v("A", sl(4097, 143)), -9.0)
    def tables():
        for r in range(3):
            dma("Y", "hw0", v("HW", p=rows(13 + r)), v("G", sl(1024 * r, 1024)))
        a = 0
        for h, (n, when) in enumerate(LOADS):
            dma("Y", "lw%d" % h, v("wraw", sl(512 * a, 512 * n)), T.wpos[:, sl(512 * a, 512 * n)], None, bysem[when])
            for k in range(a, a + n):
                ts(v("A", sl(1 + 512 * k, 512)), v("wraw", sl(512 * k, 512)), 0.25, Op.max)
            a += n

    def select(i, src):
        tt(v("pr", i), src, v("oh"), Op.mult)
        scan(v("ps", i), v("pat4"), v("pr", i), 0.0, Op.mult, Op.add)
        return v("ps", i, slice(3, 128, 4))

    def barrier(rd):
        act(v("nh"), v("pC", sl(0, 480)), Act.Sigmoid, bias=8500.0, scale=-1000.0)
        scan(v("DS"), v("on1"), v("nh"), 100.0, Op.add, Op.mult)
        tt(v("p2"), XF, v("oh"), Op.mult)
        scan(v("se"), v("pat4"), v("p2"), 0.0, Op.mult, Op.add)
        lanes, by4 = v("se", slice(3, 128, 4)), [v("se", slice(3 + 4 * b, 128, 16)) for b in range(4)]
        mm([(v("pZ", sl(0, 8)), wide4("WB", 0, b), by4[b]) for b in range(4)]
           + [(v("pZ", slice(128 * i + k, 128 * i + 128, 4)), v("WK", 4 * i + k), lanes) for i in (1, 2) for k in range(4)])
        y, y16, xb = v("pZ", sl(384, 128)), v("pC", sl(480, 8)), v("pZ", sl(128, 128))
        mm([(y16, wide4("WB", 1, b), by4[b]) for b in range(4)], last=False)
        ts(v("cl", 0), v("pZ", sl(0, 8)), 24.0 - 24.0 * HALF, Op.add)
        ts(v("m1"), v("pZ", sl(128, 128)), PPC, Op.is_equal)
        tt(v("m2"), v("pZ", sl(256, 128)), v("m1"), Op.mult)
        tt(v("bg"), ind(v("DS"), v("cl", 0)), v("m2"), Op.min)
        mm([(y16, wide("WZ", u, 1), v("bg", slice(u, 128, 16))) for u in range(16)], first=False)
        mm([(y, v("ONn"), v("bg"))] + [(v("pZ", slice(384 + k, 512, 4)), v("WK", k), lanes) for k in range(4)])
        ts(v("cl", 1), y16, -96.0 * HALF - 7.5 / 16, Op.add)
        act(v("ys"), y, Act.Identity, bias=-HALF * C)
        tt(v("m3"), ind(v("NI"), v("cl", 1)), v("ys"), Op.is_equal)
        tt(v("bw"), ind(v("W2"), v("cl", 1)), v("m3"), Op.mult)
        mm([(xb, v("ON8"), v("bw"))])
        if rd == RO - 1:
            ts(v("ybo", sl(128 * rd, 128)), xb, 0.125, Op.mult, -1.0, Op.max)
        else:
            act(xb, xb, Act.Relu, bias=1.0, scale=0.125)
            tt(v("b0"), xb, v("M16"), Op.mult)
            scan(v("b1", sl(1, 128)), v("pat16"), v("b0"), 0.0, Op.mult, Op.add)
            tt(v("E3", ALL, ALL, 7), xb, v("b1", sl(0, 128)), Op.is_equal)
            for c in range(7):
                ts(v("E3", slice(c + 1, 8), ALL, c), v("pZ", slice(144 + 16 * c, 256)), v("b1", sl(16 * c + 16, 1)), Op.is_equal)
            mm([(v("pC", sl(0, 72)), wide("WZ", u, 0), v("E3", ALL, u, ALL)) for u in range(16)]
               + [(v("pC", slice(8, 72, 9)), v("TR", 2), v("b1", slice(16, 129, 16)))])
            scan(v("cn"), v("pat9"), v("pC", sl(0, 72)), 0.0, Op.mult, Op.add)
            tt(v("co"), v("cn", slice(8, 72, 9)), v("Dc"), Op.min)
            cp(v("cl", 2), v("co"))
            cp(ind(v("A"), v("cl", 2)), v("qrt"))
            act(v("ybo", sl(128 * rd, 128)), xb, Act.Identity, bias=-1.0)

    twa, twin = {}, {}

    def expand(rd):
        rq = select(0, RC0)
        cp(v("rq"), rq)
        ts(v("fld", 0), rq, 1.0 / 1024, Op.mult, HALF - 511.5 / 1024, Op.add)
        a = 0
        for n in CUT:
            x, c = sl(a, n), sl(a // 16, n // 16)
            oc = v("pM" if a else "pS", c)
            act(v("G3", x), ind(v("HW", sl(0, 4096)), v("rq", c)), Act.Copy)
            act(v("Gb", x), v("G3", x), Act.Identity, bias=BGB, scale=4096.0)
            scan(v("F", sl(a + 1, n)), v("G3", x), v("cap", x), v("Fc") if a else 512.0, Op.add, Op.min)
            if a + n < 512:
                cp(v("Fc"), v("F", sl(a + n, 1)))
            act(v("G2", x), v("G3", x), Act.Identity, bias=BG2, scale=KAP)
            mm([(oc, v("ID", 0), v("slc", c)), (oc, v("ID", 1), v("k24", c)), (oc, v("ID", 1), v("fld", 0, c))], last=False)
            scan(v("vv", x), v("F", x), v("Gb", x), 0.0, Op.max, Op.min)
            mm([(oc, wide("WL", u, 0), v("vv", slice(a + u, a + n, 16))) for u in range(16)], first=False)
            scan(v("nf", sl(a + 1, n)), v("Gb", x), v("G2", x), v("nf", sl(a, 1)) if a else NF0, Op.add, Op.min)
            cp(v("off", c), oc)
            tt(ind(v("W"), v("off", c)), v("G3", x), v("nf", x), Op.add)
            a += n
        for n, s in enumerate(ORD):
            o, out = secs[s], v("p" + EB[n], sl(0, 96))
            mm([(out, wide("WA", u, o), v("W", sl(o * WS + 512 + u, C - u, 16))) for u in range(16)])
            act(v("dl", s, sl(1, 96)), out, Act.Identity, bias=16385.0)
            act(v("sg", n & 1, sl(1, 96)), out, Act.Sign, bias=0.5)
            mm([(out, v("TR", 1 - i), v("dl", s, sl(i, 96))) for i in range(2)] + [(out, v("TS", 1 - i), v("sg", n & 1, sl(i, 96))) for i in range(2)])
            scan(v("aa", s), out, v("top"), 0.0, Op.add, Op.min)
            if s == 3:
                cp(v("hl", 3), v("aa", 3))
                continue
            w = 96 if (rd, s) == PLAIN else 84
            if w == 96:
                cp(v("asnd", rd, s), v("aa", s))
            else:
                tt(v("pk"), ind(v("aa", s), v("repl")), v("sc7"), Op.mult)
                ts(v("pk2"), v("pk", sl(0, 84)), 49152, Op.bitwise_and)
                tt(v("pk3"), v("aa", s, sl(0, 84)), v("pk2"), Op.add)
                cp(v("asnd", rd, s, sl(0, 84)), v("pk3"))
            twa[2 - s] = send1(s, "ra%d%d" % (2 - s, rd), v("asnd", rd, s, sl(0, w)), v("arcv", rd, 2 - s, sl(0, w)))

    def ends():
        mm([(v("pS", sl(32, 32)), wide("WL", u, 0), v("G3", slice(u, 512, 16))) for u in range(16)])
        ts(v("s0"), v("fld", 0), -float(WS), Op.mult, HALF * WS - 512, Op.add)
        cp(v("s3"), v("off"))
        tt(v("s1"), v("s3"), v("s0"), Op.add)
        tt(v("s2"), v("pS", sl(32, 32)), v("s1"), Op.add)
        ts(v("s3"), v("s2"), 3.0, Op.add, C - 1.0, Op.min)
        ts(v("s4"), v("s1"), 0.0, Op.max, float(C), Op.min)
        tt(v("fld", 2), v("s3"), v("s4"), Op.max)
        tt(v("fld", 3), v("fld", 2), v("s4"), Op.subtract)
        ts(v("fld", 1), v("fld", 2), 1.0 / 96, Op.mult, HALF - 47.5 / 96, Op.add)
        mm([(v("pK", slice(256 + a, 384, 4)), wide4("W4", a, f), v("fld", f)) for f in range(4) for a in range(4)])

    def bounds():
        mm([(v("pT", sl(128 * o, 128)), v("WE", o), x) for o in range(4) for x in (v("r1"), v("F", slice(4, 513, 4)))])
        act(v("ch"), v("pT"), Act.Identity, bias=160.0 - 63.5 / 128, scale=1.0 / 128)
        act(v("lt"), v("ch"), Act.Sigmoid, bias=BLT, scale=1000.0)
        ts(v("eq"), v("ch"), PCH, Op.is_equal)
        e1, e2 = v("pS", sl(64, 32)), v("pS", sl(96, 32))
        mm([(e1, v("ME", sl(3 - b, 128)), x) for b in range(4) for x in (v("r1", slice(b, 128, 4)), v("F", slice(4 + 4 * b, 513, 16)))])
        cp(v("bi"), e1)
        ts(v("bj"), v("bi"), 127, Op.bitwise_and)
        cp(v("bh"), v("bj"))
        mm([(v("pS", sl(96 + 8 * o, 8)), wide4("W4", o, b), v("bh", slice(b, 32, 4))) for o in range(4) for b in range(4)])
        cp(v("bl"), e2)

    def unpack_addr(rd, s):
        land = v("arcv", rd, s, sl(0, 84))
        arrive("ra%d%d" % (s, rd), whole, v("arcv", rd, s), twa[s])
        if (rd, 2 - s) == PLAIN:
            return
        ts(v("uh"), land, 1.0 / 16384, Op.mult, 160.0 - 8191.5 / 16384, Op.add)
        cp(v("ui"), land)
        scan(v("us"), v("pat7"), v("uh"), 0.0, Op.mult, Op.add)
        ts(v("ua"), v("ui"), 16383, Op.bitwise_and)
        ts(v("hl", s, sl(84, 12)), v("us", slice(6, 84, 7)), -160.0 * 5461, Op.add)
        cp(v("hl", s, sl(0, 84)), v("ua"))

    def look(rd, s):
        g0 = C * s

        def part(at, a, n, q):
            x = ind(v("HW"), v("arcv", rd, s, sl(a, n)) if (rd, 2 - s) == PLAIN else v("hl", s, sl(a, n)))
            if q == "S":
                act(v("G", sl(at, 16 * n)), x, Act.Copy)
            else:
                cp(v("G", sl(at, 16 * n)), x)
        if s == 3:
            part(g0, 0, 48, LQ[s][0]); part(g0 + 768, 48, 48, LQ[s][1])
            mm([(v("pA", sl(0, 96)), v("ID", 1), v("ck0"))] + [(v("pA", sl(0, 96)), wide("WH", u, 0), v("G", sl(g0 + u, C - u, 16))) for u in range(16)])
        else:
            part(GX + 384 * s, 72, 24, "V")
            a = 0
            for q, n in LQ[s]:
                part(g0 + 16 * a, a, n, q)
                a += n
            bank = "pM" if s & 1 else "pB"
            mm([(v(bank, sl(0, 72)), v("ID", 1), v("ck"))], last=False)
            mm([(v(bank, slice(k, 72, 3)), wide("WH", u, k + 1), v("G", sl(GX + 384 * s + u, 384 - u, 16))) for u in range(16) for k in range(3)], False, False)
            mm([(v(bank, sl(0, 72)), wide("WH", u, 0), v("G", sl(g0 + u, 1152 - u, 16))) for u in range(16)], False, True)

    def reply(rd, s):
        cp(v("rsnd", rd, s), v("pM" if s & 1 else "pB", sl(0, 72)))
        twin[2 - s] = send1(s, "rr%d%d" % (2 - s, rd), v("rsnd", rd, s), v("rrcv", rd, 2 - s))

    def lists(rd, s):
        o = secs[s]
        if s < 3:
            arrive("rr%d%d" % (s, rd), whole, v("rrcv", rd, s), twin[s])
            ts(v("rh"), v("rrcv", rd, s), 1.0 / 4096, Op.mult, 160.0 - 2047.5 / 4096, Op.add)
            cp(v("rs"), v("rrcv", rd, s))
            mm([(v("pA", sl(0, 96)), v("ID", 1), v("cu")), (v("pA", sl(0, 72)), v("ID", 2), v("rh"))]
               + [(v("pA", sl(72, 24)), v("ID", (3, 4, 0)[k]), v("rh", slice(k, 72, 3))) for k in range(3)] + [(v("pA", sl(0, 72)), v("TR", 2), v("rs"))])
        ts(v("l1", s), v("pA", sl(0, 96)), 1.0, Op.add)
        tt(v("W2", sl(96 * o, 96)), v("pA", sl(0, 96)), v("dl", s, sl(1, 96)), Op.min)
        ts(v("l2", s), v("W2", sl(96 * o, 96)), 1.0, Op.add)

    Aw = v("A", sl(0, 4104))

    def phrases(s, n):
        o, b = secs[s], n & 1
        x0, c0 = b * XS + 8, b * CS + 32
        at = 0
        for h, w in enumerate(PARTS[n]):
            x, d, z, ct = v("xs", sl(x0 + at, w)), v("d1", b, sl(at, w)), v("z", b, sl(at, w)), v("ct", sl(c0 + at, w))
            act(x, ind(Aw, v("l1", s, sl(at // 16, w // 16))), Act.Identity, bias=1.0)
            act(d, x, Act.Sigmoid, bias=-1250.0, scale=1000.0)
            tt(ct, ind(Aw, v("l2", s, sl(at // 16, w // 16))), v("xs", sl(x0 - 1 + at, w)), Op.is_equal)
            scan(z, ct, d, v("z", b, sl(at - 1, 1)) if h else 0.0, Op.mult, Op.add)
            mm([(v("pZ", sl(0, 128)), wide("WZ", i, 0), v("z", b, sl(128 * i, 128))) for i in range(at // 128, (at + w) // 128)], at == 0, at + w == C)
            at += w
        scan(v("Pz", b, sl(1, 128)), v("pZ", sl(0, 128)), v("neg8"), 0.0, Op.add, Op.add)
        tt(v("T1", b), ind(v("Pz", b, sl(0, 128)), v("bl", sl(8 * o, 8))), v("eq", sl(128 * o, 128)), Op.mult)
        act(v("T2", b), v("lt", sl(128 * o, 128)), Act.Identity, scale=v("Pz", b, sl(128, 1)))
        t = v("pT", sl(0, 128))
        mm([(t, v("TR", 2), v(k)) for k in ["Cc"][n:]] + [(t, v("ON8"), v("T2", b))], n == 0, False)
        mm([(t, v("ON8"), v("T1", b))], False, n == 3)
        mm([(v("pC", sl(120 * o, 120)), wide("WZ", i, 0), v("ct", sl(c0 - 24 + 96 * i, 120))) for i in range(16)])

    def winners(rd):
        cp(v("S", sl(1, 128)), v("pT", sl(0, 128)))
        tt(v("key"), v("pT", sl(0, 128)), v("S", sl(0, 128)), Op.subtract)
        scan(v("mk"), v("pat4"), v("key"), 0.0, Op.mult, Op.max)
        tt(v("oh"), ind(v("mk"), v("l43")), v("key"), Op.is_equal)
        for a in range(4):
            act(v("yto", slice(128 * rd + a, 128 * rd + 128, 4)), v("key", slice(a, 128, 4)), Act.Identity, bias=(a - 3) / 4.0, scale=0.25)

    def heads(rd):
        act(v("ywo", sl(32 * rd, 32)), select(1, RC1), Act.Copy)

    def step(f, *a):
        tag[:] = [(f, a[-1:] if f in (look, lists, reply, unpack_addr, phrases) else ()), 0]
        f(*a)

    for rd in range(RO):
        step(expand, rd)
        if rd > 0:
            step(heads, rd - 1)
            step(barrier, rd - 1)
        else:
            step(tables)
            follow(True)
            step(select, 1, RC1)
        step(chain, rd < RO - 1)
        step(follow, rd < RO - 1)
        step(ends)
        step(bounds)
        step(look, rd, 3)
        step(lists, rd, 3)
        for s in (2, 1, 0):
            step(unpack_addr, rd, s)
            step(look, rd, s)
            step(reply, rd, s)
        if rd < RO - 1:
            step(zero_w, rd + 1, v("rsnd", rd, 0))
        for n, s in enumerate((3, 0, 1, 2)):
            if s < 3:
                step(lists, rd, s)
            step(phrases, s, n)
        step(winners, rd)
    step(heads, RO - 1)
    dma("Y", "oy0", T.yt[:], v("yto", p=rows(0)))
    dma("S", "oy1", T.yw[:], v("ywo", p=rows(9)))
    step(barrier, RO - 1)
    dma("Y", "oy2", T.yb[:], v("ybo", p=rows(0)))

    succ = [[] for _ in nodes]
    for i, x in enumerate(nodes):
        for j in x["dep"]:
            succ[j].append(i)
    n_, deps = len(nodes), [len(x["dep"]) for x in nodes]
    Q_, K_ = ["AVSPQY".index(x["q"]) for x in nodes], ["acdr".index(x["kind"]) for x in nodes]
    models = []
    for m in MODELS:
        gap = [[(j, -1e9 if K_[j] == 2 and not hard else 0.0 if not hard else m["same"] if Q_[j] == Q_[i] and K_[j] == 1 else m["wake"])
                for j, hard in nodes[i]["dep"].items() if not any(x and nodes[k]["dep"].get(j) for k, x in nodes[i]["dep"].items())] for i in range(n_)]
        models.append(([x["busy"][0] + x["busy"][1] * m[x["busy"][2]] for x in nodes], [x["late"][0] * m[x["late"][1]] + (m["rows"] if x["kind"] == "d" else 0.0) for x in nodes], gap, m["dma"]))
    B_, L_, G_, D_ = models[0]
    level = [0.0] * n_
    for i in range(n_ - 1, -1, -1):
        level[i] = B_[i] + L_[i] + (D_ if K_[i] == 2 else 0.0) + max([level[k] + 90.0 for k in succ[i]] + [0.0])

    def lay_out(rank):
        left, done, free, dfree, turn = list(deps), [0.0] * n_, [0.0] * 6, 0.0, []
        start = [0.0] * n_
        ready = [[i for i in range(n_) if not left[i] and Q_[i] == q] for q in range(6)]
        when = [0.0 if x else 1e18 for x in ready]
        for _ in nodes:
            t0 = min(when)
            q, top, one = when.index(t0), -1e18, 0
            for i in ready[q]:
                if rank[i] > top and start[i] <= t0:
                    top, one = rank[i], i
            t1, top = t0 + AHEAD * B_[one], top + 300.0
            for i in ready[q]:
                if rank[i] > top and start[i] < t1:
                    top, one = rank[i], i
            ready[q].remove(one)
            turn.append(one)
            t = max(t0, start[one]) + B_[one]
            free[q] = t if q else 0.0
            if K_[one] == 2:
                dfree = max(dfree, t) + L_[one]
            done[one] = dfree + D_ if K_[one] == 2 else max(dfree, t) if K_[one] == 3 else t + L_[one]
            when[q] = max(free[q], min([start[i] for i in ready[q]])) if ready[q] else 1e18
            for k in succ[one]:
                left[k] -= 1
                if not left[k]:
                    start[k] = max([t0] + [done[j] + w for j, w in G_[k]])
                    ready[Q_[k]].append(k)
                    when[Q_[k]] = min(when[Q_[k]], max(free[Q_[k]], start[k]))
        return turn

    def backwards(turn, m):
        busy, late, pred, dmat = m
        place = {i: n for n, i in enumerate(turn)}
        left, free, out = [len(x) for x in succ], [0.0] * 6, [0.0] * n_
        start = [late[i] + (dmat if K_[i] == 2 else 0.0) for i in range(n_)]
        ready = [[i for i in range(n_) if not left[i] and Q_[i] == q] for q in range(6)]
        for _ in nodes:
            t0, q = min((max(free[q], min(start[i] for i in ready[q])), q) for q in range(6) if ready[q])
            one = max((i for i in ready[q] if start[i] <= t0 + BACK), key=place.get)
            ready[q].remove(one)
            out[one] = max(t0, start[one]) + busy[one]
            free[q] = out[one] if q else 0.0
            for k, w in pred[one]:
                start[k] = max(start[k], out[one] + (0.0 if w < 0 else w + late[k] + (dmat if K_[k] == 2 else 0.0)))
            for k in nodes[one]["dep"]:
                left[k] -= 1
                if not left[k]:
                    ready[Q_[k]].append(k)
        return out

    def times(turn, m, a=0, old=None):
        busy, late, pred, dmat = m
        start, why, done = (list(old[1]), list(old[2]), list(old[4])) if old else ([0.0] * n_, [-1] * n_, [0.0] * n_)
        free, last, dfree, dlast, end, tip = [0.0] * 6, [-1] * 6, 0.0, -1, 0.0, 0
        for i in turn[:a][::-1]:
            if last[Q_[i]] < 0 and Q_[i]:
                free[Q_[i]], last[Q_[i]] = start[i] + busy[i], i
            if dlast < 0 and K_[i] == 2:
                dfree, dlast = done[i] - dmat, i
        for i in turn[a:]:
            q = Q_[i]
            t, w = free[q], last[q]
            for j, g_ in pred[i]:
                if done[j] + g_ > t:
                    t, w = done[j] + g_, j
            start[i] = t
            t += busy[i]
            if q:
                free[q], last[q] = t, i
            if K_[i] > 1:
                if dfree > t:
                    t, w = dfree, dlast
                t += late[i]
                if K_[i] == 2:
                    dfree, dlast = t, i
                    t += dmat
            else:
                t += late[i]
            done[i], why[i] = t, w
            if t > end:
                end, tip = t, i
        return end + SOON * sum(done) / n_, start, why, tip, done, end

    def moved(turn, u, x, up, go):
        a, b = turn.index(u), turn.index(x)
        part = turn[a:b + 1]
        for i in (part[::-1] if up else part):
            if i not in go and any(k in go for k in (succ[i] if up else nodes[i]["dep"])):
                go.add(i)
        if (u if up else x) in go:
            return None
        one, two = [i for i in part if i in go], [i for i in part if i not in go]
        return turn[:a] + (one + two if up else two + one) + turn[b + 1:]

    def improve(seed, turn, SHIFTS, TRIES):
        rs = np.random.RandomState(seed)
        like = {}
        for i, x in enumerate(nodes):
            like.setdefault(x["tag"], []).append(i)
        rank = np.array(level)
        cost = best = sum(times(turn, m)[0] for m in models)
        for n in range(SHIFTS):
            a, new = rs.randint(n_), rank.copy()
            some = range(a, min(n_, a + rs.randint(1, rs.choice([3, 12, 40]))))
            some = [i for i in some if n & 2 or nodes[i]["tag"][0] == nodes[a]["tag"][0]]
            new[[j for i in some for j in (like[nodes[i]["tag"]] if n & 1 else [i])]] += rs.choice([-1.0, 1.0]) * rs.choice([300.0, 1000.0, 3000.0, 8000.0])
            if n % TURNS == 0:
                new = np.array(backwards(lay_out(new.tolist()), models[n // TURNS % len(models)]))
            tn = lay_out(new.tolist())
            c = sum(times(tn, m)[0] for m in models)
            if c <= cost + WARM * (1.0 - n / SHIFTS) * rs.exponential():
                cost, rank = c, new
                if c <= best:
                    best, turn = c, tn
        now = [times(turn, m) for m in models]
        cost = best = sum(x[0] for x in now)
        keep = turn
        for n in range(TRIES):
            if n % 50 == 0:
                turn = sorted(turn, key=lambda i: now[0][1][i])
                now = [times(turn, m) for m in models]
                cost = sum(x[0] for x in now)
            why, x = now[rs.randint(len(now))][2:4]
            pairs = []
            while why[x] >= 0:
                if why[x] not in nodes[x]["dep"]:
                    pairs.append((why[x], x))
                x = why[x]
            u, x = pairs[rs.randint(len(pairs))]
            up = rs.randint(2)
            if n % 3 == 0:
                x = rs.randint(n_)
            mates = [i for i in turn if Q_[i] == Q_[x]]
            if n % 3 == 0:
                u = mates[max(0, mates.index(x) - 1)]
            go = {x if up else u}
            if Q_[u] == Q_[x] and rs.randint(3):
                a, b = mates.index(u), mates.index(x)
                far, run_ = rs.geometric(JUMP), (rs.geometric(0.3) - 1) * rs.randint(2)
                a, b = max(0, a - (far if up else run_)), min(len(mates) - 1, b + (run_ if up else far))
                go = set(mates[mates.index(x):b + 1] if up else mates[a:mates.index(u) + 1])
                u, x = mates[a], mates[b]
            new = moved(turn, u, x, up, go)
            if new:
                then = [times(new, m, turn.index(u), y) for m, y in zip(models, now)]
                c = sum(y[0] for y in then)
                if c <= cost + HEAT * (1.0 - n / TRIES) * rs.exponential():
                    turn, now, cost = new, then, c
                    if c < best:
                        best, keep = c, new
        return best, keep

    if not FOUND:
        keep = min(improve(SEED + i, lay_out(level), SHIFTS, TRIES // 3) for i in range(STARTS))[1]
        keep = improve(SEED, keep, 0, TRIES)[1]
        FOUND.extend([keep, sum(times(keep, m)[5] for m in models) / len(models)])
    place = {i: n for n, i in enumerate(FOUND[0])}
    left, ready, turn = list(deps), {i for i in range(n_) if not deps[i]}, []
    while ready:
        i = min(ready, key=place.get)
        ready.remove(i)
        turn.append(i)
        for k in succ[i]:
            left[k] -= 1
            if not left[k]:
                ready.add(k)
    count = {s: 0 for s in SEMAPHORES}
    seen = {q: {} for q in eng}
    mark, known = {}, {}

    def wait(q, sem, val):
        if seen[q].get(sem, 0) < val:
            eng[q].wait_ge(T.sem[sem], val)
            seen[q][sem] = val

    for i in turn:
        x = nodes[i]
        q = x["q"]
        if x["kind"] != "a":
            need = {}
            for j, hard in x["dep"].items():
                if hard and nodes[j]["kind"] != "r" and mark[j][1] > need.get(mark[j][0], (0, 0))[0]:
                    need[mark[j][0]] = (mark[j][1], j)
            for sem, (val, j) in sorted(need.items(), key=lambda e: -mark[e[1][1]][2]):
                wait(q, sem, val)
                for s2, v2 in known.get(j, {}).items():
                    seen[q][s2] = max(seen[q].get(s2, 0), v2)
            known[i] = dict(seen[q])
            inst = x["call"]()
            if x["kind"] != "r":
                inst.then_inc(T.sem[x["sem"] or q], x["n"])
        sem = "sent" if x["kind"] == "r" else x["sem"] or q
        count[sem] += x["n"]
        mark[i] = (sem, count[sem], len(mark))
    seen["Q"] = {}
    for s in SEMAPHORES:
        if count[s]:
            wait("Q", s, count[s])


FOUND, SEED, STARTS, SHIFTS, TRIES = [], 1, 4, 1000, 27000
WARM, HEAT, SOON, TURNS, BACK, AHEAD, JUMP, CHUNK = 300.0, 60.0, 0.1, 10, 800.0, 0.4, 0.2, 600
ORD, EB = (3, 0, 1, 2), "BAMB"
PLAIN = (0, 0)
LOADS = ((1, "ls"), (3, "t3a"), (2, "hw0"), (2, "hw0"))
LQ = ((("S", 36), ("S", 20), ("V", 16)), (("S", 36), ("V", 36)), (("S", 36), ("S", 36)), "SS")
PARTS, CUT = ((768, 768),) * 3 + ((768, 512, 256),), (256, 256)
FILL = {"W": "VVVS", "HW": "SSSSQQQQVVVV"}
